import numpy as np, ml_dtypes
CORES = [16,18,20,22]
N = 4
import mx_ref
BF = ml_dtypes.bfloat16
def gentries(a):
    return np.ascontiguousarray(a.reshape(8, 16, -1).transpose(0, 2, 1)).reshape(8, -1)
def gtable(e):
    e = np.asarray(e); return np.ascontiguousarray(e.reshape(8, -1, 16).transpose(0, 2, 1)).reshape(128, -1).astype(np.int32)
def gcols(t, e):
    v = np.concatenate([t.reshape(8, 16, -1, 4), np.zeros((8, 16, 1, 4), BF)], axis=2)
    return np.ascontiguousarray(np.stack([v[g][:, e[g]] for g in range(8)])).reshape(128, -1)
def gpick(z, e):
    return np.concatenate([z[16 * g:16 * g + 16][:, e[g]] for g in range(8)])
def tile(rs):
    return np.stack(rs, axis=2).reshape(128, -1).astype(BF)
def pick(q, e):
    c = np.concatenate([q[0].reshape(128, -1, 4), np.zeros((128, 1, 4), np.uint8)], axis=1); s = np.concatenate([q[1], np.ones((16, 1), np.uint8)], axis=1)
    return (np.ascontiguousarray(c[:, e].reshape(128, -1)), np.ascontiguousarray(s[:, e]))
def join(*qs):
    return (np.concatenate([q[0] for q in qs], axis=1), np.concatenate([q[1] for q in qs], axis=1))
def put(q, e, v):
    c, s = q[0].reshape(128, -1, 4).copy(), q[1].copy(); c[:, e] = v[0].reshape(128, -1, 4); s[:, e] = v[1]
    return (c.reshape(128, -1), s)
def pk(c, s):
    return (np.ascontiguousarray(c), mx_ref.live(s))
def emit(q):
    return q[0], q[1]
def packed(v, rng):
    q = [mx_ref.quantize(np.ascontiguousarray(v[r])) for r in range(N)]
    return np.stack([a for a, b in q]), np.stack([mx_ref.plane(b, rng) for a, b in q])
def values_of_codes():
    e, c = np.zeros((128, 128, 4), np.float32), np.zeros((128, 2, 4), np.uint8)
    e[np.arange(128), np.arange(128), 0] = 1
    c[:127, :, 0] = np.arange(256).reshape(2, 128).T[:127]
    return mx_ref.matmul(mx_ref.quantize(e.reshape(128, 512).astype(BF)), (c.reshape(128, 8), np.full((16, 2), 127, np.uint8))).T.reshape(-1).astype(np.float64)
CODE_VALUE, SCALE_VALUE = values_of_codes(), 2.0 ** (np.arange(256) - 127.0)
def decode(q):
    return (CODE_VALUE[q[0]].reshape(16, 8, -1, 4) * SCALE_VALUE[q[1]][:, None, :, None] + 0.0).reshape(128, -1).astype(np.float32)
def f(rng, *shape):
    return mx_ref.flush((rng.standard_normal(shape, dtype=np.float32) * np.exp2(rng.integers(-2, 3, shape[:-1] + (1,)))).astype(BF))
def wide(rng, *shape, cols=0):
    v = rng.standard_normal(shape, dtype=np.float32) * np.exp2(rng.integers(-12, 13, shape)).astype(np.float32)
    if cols: v *= np.repeat(np.exp2(rng.integers(-cols, cols + 1, shape[:-2] + (1, shape[-1] // 4))) * (rng.random(shape[:-2] + (1, shape[-1] // 4)) > 0.0625), 4, axis=-1).astype(np.float32)
    return mx_ref.flush(v.astype(BF))
C = 448
STEP = [1, 2, 3]
def numbers_of(rng):
    return {"x": np.array(f(rng, N, 128, 4 * C)), "u": np.array(f(rng, N, 128, 512)), "v": np.array(f(rng, N, 128, 512))}
def stored(k):
    return {"od": np.stack([gtable(k[r]) for r in range(N)])}
def orders(rng):
    return stored(rng.permuted(np.tile(np.arange(C), (N, 8, 1)), axis=2))
def rings(rng):
    h = rng.permutation(8)
    pairs = [1] + [2] * (C // 2 - 1) + [1]
    sizes = [[C], [C], [1, C - 1], [257, C - 257], pairs, pairs, [C // 2, C // 2], [1] * C]
    i = np.arange(N)
    odd = (i ^ (i >> 1) ^ (i >> 2)) % 2
    k = np.zeros((N, 8, C), np.int64)
    for g in range(8):
        w = np.arange(C) if h[g] % 2 == 0 else rng.permutation(C)
        c, after = rng.permutation(C), np.zeros(C, np.int64)
        a = 0
        for m in sizes[h[g]]:
            after[w[a:a + m]] = np.roll(w[a:a + m], -1)
            a += m
        k[:, g] = np.where(odd[:, None] == 1, c[after], c)
    return stored(k)
def layers(rng):
    return np.array(f(rng, N, 128, 2048)).reshape(N, 8, 16, 4, 8, 16, 4)
def weights(rng, w):
    c, s = packed(np.ascontiguousarray(w).reshape(N, 128, 2048), rng)
    return {"wc": c, "ws": s}
def setup_inputs(rng):
    return {**numbers_of(rng), **orders(rng), **weights(rng, layers(rng))}
def setup_inputs_ties(rng):
    d = numbers_of(rng)
    o = rng.permutation(N)
    k = rng.integers(-1, 2, (N, 8, C)).astype(np.float32)
    k[o[0]] = 0
    k[o[1]] = 1
    k[o[2]] = -1
    x = d["x"].reshape(N, 8, 16, C, 4)
    x[:, :, 0] = 0
    x[:, :, 0, :, 0] = k.astype(BF)
    u = d["u"].reshape(N, 128, 128, 4)
    u[:, :, ::16] = 0
    for h in range(0, 128, 16): u[:, h, h, 0] = 1
    w = layers(rng)
    w[:, :, :, :, :, 0] = 0
    return {"x": x.reshape(N, 128, 4 * C), "u": u.reshape(N, 128, 512), "v": d["v"], **rings(rng), **weights(rng, w)}
def setup_inputs_near(rng):
    d = numbers_of(rng)
    small = ((np.arange(N) & STEP[1]) > 0) ^ (rng.random() < 0.5)
    k = np.where(small, 2.0 ** -30, 1.0)
    x = d["x"].astype(np.float32).reshape(N, 8, 16, C, 4)
    x[:, :, :8] = 0
    s = rng.integers(-1, 2, (N, 8, C)) * k[:, None, None]
    x[:, :, 0, :, 0] = 1.125 * s
    x[:, :, 1, :, 0] = -1.25 * s
    x[:, :, 2, :, 0] = rng.choice([-1.0, 1.0], (N, 8, C)) * 2.0 ** -30
    x[:, :, 4, :, 0] = 2.0 ** -30
    for r in range(N):
        at = [0, C - 1, int(rng.integers(C)), int(rng.integers(C))]
        for g, j in zip(rng.permutation(8)[:4], at): x[r, g, 0, j, 0] = 2.0 ** 30 * rng.choice([-1.0, 1.0])
    k = k.astype(np.float32)
    u = d["u"].reshape(N, 128, 128, 4)
    u[:, :, ::16] = 0
    for h in range(0, 128, 16):
        u[:, h, h, 0] = (1.125 * k).astype(BF)
        u[:, h + 1, h, 0] = k.astype(BF)
        u[:, h + 3, h, 0] = k.astype(BF)
    w = layers(rng)
    w[:, :, :8] = 0
    w[:, :, :, :, :, :8] = 0
    for r in range(N):
        for g in range(8):
            if small[r]: w[r, g, 2, 0, g, 3, 0] = 2.0 ** -8
    return {"x": x.reshape(N, 128, 4 * C).astype(BF), "u": u.reshape(N, 128, 512), "v": d["v"], **orders(rng), **weights(rng, w)}
def setup_inputs_odd(rng):
    d = numbers_of(rng)
    x = (1.0 + (2 * rng.integers(0, 64, (N, 16, 8, C, 4)) + 1) * 2.0 ** -7) * np.exp2(-rng.integers(0, 7, (N, 16, 8, C, 4)).astype(np.float64)) * rng.choice([-1.0, 1.0], (N, 16, 8, C, 4))
    x[:, :, 0, :, 0] = np.where(rng.random((N, 16, C)) < 0.5, 1.96875, 1.875) * 2.0 ** 8 * rng.choice([-1.0, 1.0], (N, 16, 1))
    x[:, ::2, 1, :, 0] = rng.integers(7, 10, (N, 8, C)) * 2.0 ** -8
    x[:, ::2, 2, :, 0] = -8 * 2.0 ** -8
    u = d["u"].reshape(N, 16, 8, 128, 4)
    u[:, :, :, ::16] = 0
    for g in range(8): u[:, 2 * g, 1:3, 16 * g, 0] = 1
    w = layers(rng)
    for i in (0, 8):
        w[:, :, i] = 0
        w[:, :, :, :, :, i] = 0
    return {"x": x.astype(np.float32).reshape(N, 128, 4 * C).astype(BF), "u": u.reshape(N, 128, 512), "v": d["v"], **orders(rng), **weights(rng, w)}
def setup_inputs_ends(rng):
    d = numbers_of(rng)
    o, most = rng.permutation(N) % 4, rng.permutation(N) % 2
    h, e = rng.permutation(8), int(rng.integers(8))
    c = np.where(h < 2, 0.0, h % 2 * 2.0 - 1.0)[None, :, None]
    k = np.array([2.0, 4.0])[rng.permutation(8) % 2]
    x = np.zeros((N, 8, 16, C, 4))
    u = d["u"].astype(np.float32).reshape(N, 128, 128, 4)
    v = np.zeros((N, 128, 512), np.float32)
    w = np.zeros((N, 128, 4, 128, 4), np.float32)
    i = np.arange(128)
    for r in range(N):
        low = -0.7 * (0.9 + 0.1 * rng.random((8, 16, C, 4))) * 2.0 ** 30
        tiny = -(1.0 + 0.125 * rng.integers(0, 8, (8, 16, C, 4))) * 2.0 ** -30
        if o[r] == 0: x[r] = low
        if o[r] == 1: x[r] = np.where((rng.random(C) < 0.5)[:, None], 0.7 * (1.0 + 0.4 * rng.random((8, 16, C, 4))) * 2.0 ** 27, low)
        if o[r] == 2: x[r] = tiny
        if o[r] == 3: x[r] = d["x"][r].astype(np.float32).reshape(8, 16, C, 4)[:, :, :1]
        x[r, e, 8:] = tiny[e, 8:, :1] if o[r] == 3 else tiny[e, 8:]
        if o[r] < 2: u[r, :, ::16] = c * (0.9 + 0.1 * rng.random((128, 8, 4))) * 2.0 ** 30
        if o[r] == 2: u[r, :, ::16] = c * (1.0 + 0.125 * rng.integers(0, 8, (128, 8, 4))) * 2.0 ** -30
        if o[r] == 3: u[r, :, ::16] *= np.abs(c).astype(np.float32)
        a = (0.9 + 0.1 * rng.random((128, 512))) * 2.0 ** 30 if o[r] < 2 else (1.0 + 0.125 * rng.integers(0, 8, (128, 512))) * 2.0 ** -30
        v[r] = rng.choice([-1.0, 1.0], (128, 512)) * a
        t = k[i // 16]
        t[16 * e + 8:16 * e + 16] = 2.0 ** 8 if most[r] else 2.0 ** -8
        for b in range(4): w[r, i, b, i, b] = t
    return {"x": x.astype(np.float32).reshape(N, 128, 4 * C).astype(BF), "u": u.reshape(N, 128, 512).astype(BF), "v": v.astype(BF), **rings(rng), **weights(rng, w.astype(BF))}
def setup_inputs_spread(rng):
    d = setup_inputs(rng)
    d["x"] = wide(rng, N, 128, 4 * C, cols=6)
    return d
def check_inputs(d):
    b = []
    for k in ("x", "u", "v"):
        a = np.abs(d[k].astype(np.float32))
        if not (np.isfinite(a).all() and ((a == 0) | (a >= 2.0 ** -30) & (a <= 2.0 ** 30)).all()): b.append("a value of " + k)
    none, least, most = [emit(mx_ref.quantize(np.full((128, 16), k, np.float32).astype(BF)))[1][0, 0] for k in (0.0, 2.0 ** -8, 2.0 ** 8)]
    for r in range(N):
        if not (np.sort(gentries(d["od"][r]), axis=1) == np.arange(C)).all(): b.append("od: a group whose entries are not all columns once")
        if ((d["wc"][r] == 0x7F) | (d["wc"][r] == 0xFF)).any(): b.append("wc: a code that is no number")
        s = mx_ref.live(d["ws"][r])
        if ((s != none) & ((s < least) | (s > most))).any(): b.append("ws: a scale out of range")
        if (((d["wc"][r].reshape(16, 8, 512, 4) & 0x7F) != 0) & (s == none)[:, None, :, None]).any(): b.append("wc: a code other than zero under the scale of zeros")
    return b
def at(t, e):
    return np.take_along_axis(t, e, axis=1)
def reference(x, u, v, od, wc, ws):
    qu = [mx_ref.quantize(u[r]) for r in range(N)]
    lay = [pk(wc[r], ws[r]) for r in range(N)]
    now = [x[r] for r in range(N)]
    order = [gentries(od[r]).astype(np.int64) for r in range(N)]
    for step in STEP:
        old, order, far, z = order, [], [], []
        for r in range(N):
            q = mx_ref.quantize(now[r])
            s = mx_ref.matmul(qu[r], q)[::16]
            mine, other = old[r], old[r ^ step]
            jump = at(np.argsort(other, axis=1), mine)
            low = np.tile(np.arange(C), (8, 1))
            for i in range(9):
                low = np.minimum(low, at(low, jump))
                jump = at(jump, jump)
            order.append(np.where(at(s, at(mine, low)) > 0, other, mine))
            far.append(decode(q))
            t = far[r].astype(BF)
            pair = gcols(t, order[r]).astype(np.float32) + gcols(t, at(order[r], order[r])).astype(np.float32)
            z.append(mx_ref.quantize((pair * np.float32(0.5)).astype(BF)))
        for r in range(N):
            back = np.argsort(order[r], axis=1)
            now[r] = tile([gpick(mx_ref.matmul(pick(lay[r], np.arange(128 * b, 128 * b + 128)), z[r ^ step]) * np.float32(0.03125), back) + far[r][:, b::4] for b in range(4)])
    y, fo = np.zeros((N, 128, C), np.float32), np.zeros((N, 8, C), np.float32)
    oc, osc = np.zeros((N, 128, 4 * C), np.uint8), np.zeros((N, 16, C), np.uint8)
    for r in range(N):
        q = mx_ref.quantize(now[r])
        y[r] = mx_ref.matmul(mx_ref.quantize(v[r]), q)
        fo[r] = order[r]
        oc[r], osc[r] = emit(q)
    return {"y": y, "fo": fo, "oc": oc, "osc": osc}

@@ -1,0 +1,440 @@
+from concourse.mybir import dt, AluOpType, ActivationFunctionType
+
+C = 448
+K = C // 16
+STEP = [1, 2, 3]
+RADIX = [3, 3, 2, 3, 3, 3]
+F1 = ((0,), (1,), (2,))
+F2 = (((0, 1),), ((2,), (3,)))
+LATE = 0
+VF0 = False
+PRE = 4
+TV1, TV2 = (0, 1, 2, 3), (1, 2, 4)
+MID = C // 2
+UP = 512.0
+SCN = "float16"
+
+SCRATCH = {
+    "md": ("sbuf", [128, C], "int32"), "rti": ("sbuf", [128, C], "bfloat16"), "m4": ("sbuf", [128, 4], "float32"),
+    "thr": ("sbuf", [128, C], "float32"), "d0": ("sbuf", [128, C], "bfloat16"),
+    "da": ("sbuf", [128, C], "bfloat16"), "db": ("sbuf", [128, C], "bfloat16"),
+    "rst": ("sbuf", [128, C], "bfloat16"), "iots": ("sbuf", [128, C], "bfloat16"),
+    "iotd": ("sbuf", [128, C], "bfloat16"), "iotf": ("sbuf", [128, C], "float32"), "ones": ("sbuf", [128, 516], "bfloat16"),
+    "eye": ("sbuf", [128, 516], "bfloat16"), "bia": ("sbuf", [128, 4], "float32"),
+    "uoi": ("sbuf", [128, 8], "int32"), "uo": ("sbuf", [128, 8], "uint16"),
+    "odl": ("sbuf", [128, K], "int32"), "ut": ("sbuf", [128, 512], "bfloat16"),
+    "vt": ("sbuf", [128, 512], "bfloat16"), "xt0": ("sbuf", [128, 4 * C], "bfloat16"),
+    "qu": ("sbuf", [128, 128], "float8_e4m3fn_x4"), "su": ("sbuf", [128, 128], "uint8"),
+    "qur": ("sbuf", [128, 128], "float8_e4m3fn_x4"), "sur": ("sbuf", [128, 128], "uint8"),
+    "qv": ("sbuf", [128, 128], "float8_e4m3fn_x4"), "sv": ("sbuf", [128, 128], "uint8"),
+    "qe": ("sbuf", [128, 512], "float8_e4m3fn_x4"), "se": ("sbuf", [128, 512], "uint8"),
+    "wq": ("sbuf", [128, 512], "float8_e4m3fn_x4"), "wp": ("sbuf", [128, 512], "uint8"),
+    "odr": ("sbuf", [128, K], "int32"),
+    "sc": ("sbuf", [128, C], "float32"), "so": ("sbuf", [128, C], "float32"),
+    "dm": ("sbuf", [128, C], "bfloat16"), "ds": ("sbuf", [128, C], "bfloat16"),
+
+    "zt": ("sbuf", [128, 4 * C], "bfloat16"), "xt": ("sbuf", [128, 4 * C], "bfloat16"),
+    "ysb": ("sbuf", [128, C], "float32"), "osp": ("sbuf", [128, C], "float32"),
+    "tu": ("sbuf", [128, K * 40], "uint16"), "tf": ("sbuf", [128, K * 20], "float32"),
+    "pa": ("psum", [128, 2048], "float32"), "pb": ("psum", [128, 2048], "float32"),
+}
+for _b in range(4):
+    SCRATCH["f%d" % _b] = ("sbuf", [128, C], "bfloat16")
+    SCRATCH["fd%d" % _b] = ("sbuf", [128, C], "bfloat16")
+    SCRATCH["u%d" % _b] = ("sbuf", [128, C], "float32")
+    SCRATCH["gg%d" % _b] = ("sbuf", [128, C], "bfloat16")
+    SCRATCH["ld%d" % _b] = ("sbuf", [128, C], "bfloat16")
+    SCRATCH["r%d" % _b] = ("sbuf", [128, C], "float32")
+    SCRATCH["scn%d" % _b] = ("sbuf", [128, C], SCN)
+    SCRATCH["kb%d" % _b] = ("sbuf", [128, C], "bfloat16")
+    SCRATCH["lb%d" % _b] = ("sbuf", [128, C], "bfloat16")
+    SCRATCH["xq%d" % _b] = ("sbuf", [128, C], "float8_e4m3fn_x4")
+    SCRATCH["xs%d" % _b] = ("sbuf", [128, C], "uint8")
+SCRATCH["bk0"] = ("sbuf", [128, C], "bfloat16")
+for _n in (1, 2, 3):
+    SCRATCH["zq%d" % _n] = ("sbuf", [128, C], "float8_e4m3fn_x4")
+    SCRATCH["zs%d" % _n] = ("sbuf", [128, C], "uint8")
+    SCRATCH["zl%d" % _n] = ("sbuf", [128, C], "float8_e4m3fn_x4")
+    SCRATCH["zp%d" % _n] = ("sbuf", [128, C], "uint8")
+    SCRATCH["bk%d" % _n] = ("sbuf", [128, C], "bfloat16")
+for _n in (2, 3):
+    SCRATCH["ol%d" % _n] = ("sbuf", [128, K], "uint16")
+
+SEMAPHORES = ["cv", "cs", "ct", "cg", "sent", "a_od"] \
+    + ["a_z10", "a_z20", "a_z30", "a_z31"] + ["a_ol%d" % n for n in (2, 3)] \
+    + ["l_" + n for n in ("od", "x", "u", "v", "wc", "ws", "y0", "y1", "fo", "oc0", "oc1", "osc0", "osc1", "f0", "f1", "f2")]
+
+ADD, MUL, SUB, MIN, MAX = AluOpType.add, AluOpType.mult, AluOpType.subtract, AluOpType.min, AluOpType.max
+COPY = ActivationFunctionType.Copy
+
+
+def rank_program(g, core, T, topo):
+    rank = T.rank_of(core)
+    if rank is None:
+        return
+    queues = {"v": g.vector, "s": g.scalar, "t": g.tensor, "g": g, "y": g.sync}
+    count = {"v": 0, "s": 0, "t": 0, "g": 0}
+    wrote, read, snap = {}, {}, {}
+    seen = {q: {} for q in queues}
+    totals = {}
+
+    def learn(q, sem, val):
+        s = seen[q]
+        if s.get(sem, 0) < val:
+            s[sem] = val
+        for a, b in snap.get((sem, val), {}).items():
+            if s.get(a, 0) < b:
+                s[a] = b
+
+    def await_for(q, reads, writes):
+        need = {}
+        for k in reads:
+            for sem, val in wrote.get(k, []):
+                need[sem] = max(need.get(sem, 0), val)
+        for k in writes:
+            for sem, val in wrote.get(k, []):
+                need[sem] = max(need.get(sem, 0), val)
+            for sem, val in read.get(k, []):
+                need[sem] = max(need.get(sem, 0), val)
+        for sem in sorted(need):
+            if seen[q].get(sem, 0) < need[sem]:
+                queues[q].wait_ge(T.sem[sem], need[sem])
+                learn(q, sem, need[sem])
+
+    def note(q, tok, reads, writes):
+        snap[tok] = dict(seen[q])
+        for k in reads:
+            read.setdefault(k, []).append(tok)
+        for k in writes:
+            wrote[k] = [tok]
+            read[k] = []
+
+    def op(q, reads, writes, call):
+        await_for(q, reads, writes)
+        count[q] += 1
+        sem = "c" + q
+        call().then_inc(T.sem[sem], 1)
+        totals[sem] = count[q]
+        note(q, (sem, count[q]), reads, writes)
+
+    def load(q, sem, reads, writes, pairs):
+        await_for(q, reads, writes)
+        for out, in_ in pairs:
+            queues[q].dma_start(out, in_).then_inc(T.sem[sem], 16)
+            totals[sem] = totals.get(sem, 0) + 16
+        note(q, (sem, totals[sem]), reads, writes)
+
+    def peer(step):
+        return T.cores[rank ^ step]
+
+    def bits(engines):
+        return sum(1 << e for e in engines)
+
+    def send(step, out, in_, key, sem, few=None):
+        dst = peer(step)
+        e = topo.engines(core, dst)
+        if few is not None:
+            e = e[few::2]
+        await_for("g", [key], [])
+        rid, pid, _ = topo.addr(dst)
+        g.remote_dma(out, in_, T.sem[sem], T.sem["sent"], pid, rid, bits(e))
+        totals["sent"] = totals.get("sent", 0) + len(e)
+        return len(e)
+
+    def arrives(sem, engines, keys):
+        totals[sem] = totals.get(sem, 0) + engines
+        for k in keys:
+            wrote[k] = [(sem, totals[sem])]
+        if len(keys) > 0:
+            snap.setdefault((sem, totals[sem]), {})
+
+    V, S = g.vector, g.scalar
+    slots, fslots = [0], [0]
+
+    def slot():
+        slots[0] += 1
+        return slots[0] - 1
+
+    def fslot():
+        fslots[0] += 1
+        return fslots[0] - 1
+
+    def tu(i):
+        return T.tu[:, K * i:K * (i + 1)]
+
+    def tf(i):
+        return T.tf[:, K * i:K * (i + 1)]
+
+    def by(name, i):
+        return T[name][:, 0:C].indirect(tu(i))
+
+    def tok(i):
+        return "tu%d" % i
+
+    load("y", "l_od", [], ["odl"], [(T.odl[:], T.od[:])])
+    load("y", "l_u", [], ["ut"], [(T.ut[:], T.u[:])])
+    load("y", "l_x", [], ["xt0"], [(T.xt0[:], T.x[:])])
+    load("y", "l_wc", [], ["wq"], [(T.wq[:, 0:512].bitcast(dt.uint8), T.wc[:, 0:2048])])
+    load("y", "l_ws", [], ["wp"], [(T.wp[:, 0:512], T.ws[:, 0:512])])
+    load("y", "l_v", [], ["vt"], [(T.vt[:], T.v[:])])
+
+    op("g", [], ["md"], lambda: g.iota(T.md[:], [[1, C]], 128, -1))
+    op("g", [], ["iots"], lambda: g.iota(T.iots[:], [[1, C]], -MID, 0, allow_small_or_imprecise_dtypes=True))
+    op("v", [], ["ones"], lambda: V.memset(T.ones[:], 1.0))
+    op("v", [], ["m4a"], lambda: V.memset(T.m4[:, 0:1], -4.0))
+    op("v", [], ["m4b"], lambda: V.memset(T.m4[:, 1:2], 2 * UP))
+    arrives("a_od", send(STEP[0], T.odr[:], T.odl[:], "odl", "a_od", few=0), ["odr"])
+    op("g", ["ones"], ["eye"], lambda: g.affine_select(T.eye[:], T.ones[:], [[1, 516]], AluOpType.is_equal, 0.0, -3, -4))
+    op("g", [], ["uoi"], lambda: g.iota(T.uoi[:], [[16, 8]], 0, 0))
+    op("g", [], ["iotd"], lambda: g.iota(T.iotd[:], [[1, C]], -MID, 0, allow_small_or_imprecise_dtypes=True))
+    op("g", [], ["rti"], lambda: g.iota(T.rti[:], [[0, K], [1, 16]], 0, 0, allow_small_or_imprecise_dtypes=True))
+    op("g", [], ["iotf"], lambda: g.iota(T.iotf[:], [[1, C]], 0, 0, allow_small_or_imprecise_dtypes=True))
+
+    op("v", ["md"], ["md"], lambda: V.tensor_scalar(T.md[:], T.md[:], 15, None, AluOpType.bitwise_and))
+    op("v", ["md"], ["da"], lambda: V.tensor_scalar(T.da[:], T.md[:], 2.0, 3.0, MIN, MUL))
+    op("s", ["da", "m4a", "m4b"], ["db"], lambda: S.activation(T.db[:], T.da[:], ActivationFunctionType.Abs, bias=T.m4[:, 0:1]))
+    op("s", ["db"], ["d0"], lambda: S.activation(T.d0[:], T.db[:], ActivationFunctionType.Identity, bias=T.m4[:, 1:2], scale=-UP))
+    op("s", ["da"], ["thr"], lambda: S.activation(T.thr[:], T.da[:], COPY, scale=1e28))
+    o_u, o_f = slot(), fslot()
+    op("v", ["odl"], [tok(o_u)], lambda: V.tensor_copy(tu(o_u), T.odl[:]))
+    op("v", ["odl"], ["tf%d" % o_f], lambda: V.tensor_copy(tf(o_f), T.odl[:]))
+    op("v", ["iots", tok(o_u)], ["bk0"], lambda: V.tensor_copy(by("bk0", o_u), T.iots[:]))
+    op("v", ["md"], ["bia0"], lambda: V.tensor_scalar(T.bia[:, 0:1], T.md[:, 15:16], 0.0, UP, AluOpType.is_equal, MUL))
+    op("v", ["bia0"], ["bia"], lambda: V.tensor_scalar(T.bia[:, 1:2], T.bia[:, 0:1], MID - UP, None, ADD))
+
+    def conv(name, between=None):
+        i = slot()
+        h = "scn%d" % (i % 4)
+        op("v", [name, "d0"], [h], lambda: V.tensor_tensor_scan(T[h][:], T.d0[:], T[name][:], 0.0, ADD, MAX))
+        if between is not None:
+            between()
+        op("v", [h, "bia"], [tok(i)], lambda: V.tensor_scalar(tu(i), T[h][:, 15:C:16], T.bia[:, 1:2], None, ADD))
+        return i
+
+    out = {"fill_s": [], "fill_v": []}
+
+    def between(k):
+        if len(out[k]) > 0:
+            out[k].pop(0)()
+
+    def drain(k):
+        while len(out[k]) > 0:
+            out[k].pop(0)()
+
+    def chain(n, o_u, o_f, twin_v):
+        star = fslot()
+        delta = fslot()
+        bk = "bk%d" % (n - 1)
+        src = "odr" if n == 1 else "ol%d" % n
+        offs, okey = T[src][:, 0:K], src
+        if n == 1:
+            su = slot()
+            op("v", ["odr"], [tok(su)], lambda: V.tensor_copy(tu(su), T.odr[:]))
+            offs, okey = tu(su), tok(su)
+        kn, kname = 0, "kb0"
+        op("s", [bk, okey], [kname], lambda: S.activation(T[kname][:], T[bk][:, 0:C].indirect(offs), COPY))
+        if n == 1:
+            yield
+        a = conv(kname)
+        op("v", [src], ["tf%d" % star], lambda: V.tensor_copy(tf(star), T[src][:]))
+        op("v", ["tf%d" % star, "tf%d" % o_f], ["tf%d" % delta], lambda: V.tensor_tensor(tf(delta), tf(star), tf(o_f), SUB))
+        yield
+        low, ln, twin = "iots", 0, "iotd"
+        for j, r in enumerate(RADIX):
+            last = j == len(RADIX) - 1
+            acc = twin
+            cur = kname
+            if not last:
+                for e in range(r - 1):
+                    kn = (kn + 1) % 4
+                    new = "kb%d" % kn
+                    between("fill_s")
+                    op("s", [cur, tok(a)], [new], lambda: S.activation(T[new][:], by(cur, a), COPY))
+                    cur = new
+            drain("fill_s")
+            for e in range(r - 1):
+                if e > 0 or VF0:
+                    between("fill_v")
+                ln = (ln + 1) % 4
+                lnew = "lb%d" % ln
+                op("v", [acc, low, tok(a)], [lnew], lambda: V.tensor_tensor(T[lnew][:], by(acc, a), T[low][:], MIN))
+                acc = lnew
+            low = acc
+            kname = cur
+            if not last:
+                twin = "ld%d" % (j % 4)
+                between("fill_v")
+                if j in twin_v:
+                    a = conv(kname, lambda: op("v", [low], [twin], lambda: V.tensor_copy(T[twin][:], T[low][:])))
+                else:
+                    op("s", [low], [twin], lambda: S.activation(T[twin][:], T[low][:], COPY))
+                    a = conv(kname)
+            drain("fill_v")
+            yield
+        out["low"] = conv(low)
+        out["delta"] = delta
+        yield
+
+    def pieces(n):
+        return [(0, C)] if n < len(STEP) else [(0, C // 2), (C // 2, C)]
+
+    def unpack_products(n):
+        xq, xs = "xq%d" % n, "xs%d" % n
+        op("t", ["qur", "sur", xq], ["pb0"], lambda: g.tensor.matmul_mx(T.pb[:, 0:C], T.qur[:, 0:128], T.sur[:, 0:128], T[xq][:, 0:C], T[xs][:, 0:C], True, True))
+        for b in range(4):
+            op("t", ["qe%d" % b, xq], ["pa%d" % b], lambda: g.tensor.matmul_mx(T.pa[:, 512 * b:512 * b + C], T.qe[:, 128 * b:128 * b + 128], T.se[:, 128 * b:128 * b + 128], T[xq][:, 0:C], T[xs][:, 0:C], True, True))
+
+    def f_copy(b):
+        op("s", ["pa%d" % b], ["f%d" % b], lambda: S.activation(T["f%d" % b][:], T.pa[:, 512 * b:512 * b + C], COPY))
+        if b < 3:
+            load("y", "l_f%d" % b, ["f%d" % b], ["fd%d" % b], [(T["fd%d" % b][:], T["f%d" % b][:])])
+
+    def scores(o_u):
+        op("s", ["pb0"], ["sc"], lambda: S.activation(T.sc[:], T.pb[:, 0:C], COPY))
+        op("s", ["sc", tok(o_u)], ["so"], lambda: S.activation(T.so[:], by("sc", o_u), COPY))
+
+    def choose(o_f):
+        low, delta = out["low"], out["delta"]
+        t, nf, nu = fslot(), fslot(), slot()
+        op("v", ["so", "thr", tok(low)], ["dm"], lambda: V.tensor_tensor(T.dm[:], by("so", low), T.thr[:], AluOpType.is_gt))
+        op("v", ["dm", "rst"], ["ds"], lambda: V.tensor_tensor_scan(T.ds[:], T.rst[:], T.dm[:], 0.0, MUL, ADD))
+        op("v", ["ds", "tf%d" % delta], ["tf%d" % t], lambda: V.tensor_tensor(tf(t), T.ds[:, 15:C:16], tf(delta), MUL))
+        op("v", ["tf%d" % t, "tf%d" % o_f], ["tf%d" % nf], lambda: V.tensor_tensor(tf(nf), tf(t), tf(o_f), ADD))
+        op("v", ["tf%d" % nf], [tok(nu)], lambda: V.tensor_copy(tu(nu), tf(nf)))
+        return nu, nf
+
+    def means(n, o_u):
+        bk = "bk%d" % n
+
+        def inverse():
+            op("v", ["iots", tok(o_u)], [bk], lambda: V.tensor_copy(by(bk, o_u), T.iots[:]))
+
+        if n < len(STEP):
+            m = n + 1
+            arrives("a_ol%d" % m, send(STEP[n], T["ol%d" % m][:], tu(o_u), tok(o_u), "a_ol%d" % m, few=1), ["ol%d" % m])
+        shared = (3,)
+        for b in shared:
+            op("s", ["f%d" % b, tok(o_u)], ["gg%d" % b], lambda: S.activation(T["gg%d" % b][:], by("f%d" % b, o_u), COPY))
+        parts = pieces(n)
+        turn = [(b, 0) for b in range(4)]
+        for b in range(4):
+            if b in shared:
+                op("v", ["gg%d" % b, "pa%d" % b], ["u%d" % b], lambda: V.tensor_tensor(T["u%d" % b][:], T["gg%d" % b][:], T.pa[:, 512 * b:512 * b + C], ADD))
+            else:
+                op("v", ["f%d" % b, "fd%d" % b, tok(o_u)], ["u%d" % b], lambda: V.tensor_tensor(T["u%d" % b][:], by("f%d" % b, o_u), T["fd%d" % b][:], ADD))
+        if len(parts) == 2:
+            turn = [(0, 0), (0, 1), (1, 0), (2, 0), (1, 1), (2, 1)]
+        for b, h in turn:
+            p, e = parts[h]
+            op("s", ["u%d" % b, tok(o_u)], ["zt%d%d" % (b, h)], lambda: S.activation(T.zt[:, 4 * p + b:4 * e:4], T["u%d" % b][:, 0:C].indirect(T.tu[:, K * o_u + p // 16:K * o_u + e // 16]), COPY, scale=0.5))
+        if n < len(STEP):
+            inverse()
+        zq, zs, zl, zp = "zq%d" % n, "zs%d" % n, "zl%d" % n, "zp%d" % n
+        for h, (p, e) in enumerate(parts):
+            key, sem = "%s%d" % (zq, h), "a_z%d%d" % (n, h)
+            if len(parts) == 2:
+                op("v", ["u3", tok(o_u)], ["zt3%d" % h], lambda: V.tensor_scalar(T.zt[:, 4 * p + 3:4 * e:4], T.u3[:, 0:C].indirect(T.tu[:, K * o_u + p // 16:K * o_u + e // 16]), 0.5, None, MUL))
+            op("v", ["zt%d%d" % (b, h) for b in range(4)], [key], lambda: V.quantize_mx(T[zq][:, p:e], T[zs][:, p:e], T.zt[:, 4 * p:4 * e]))
+            k = send(STEP[n - 1], T[zl][:, p:e].bitcast(dt.uint8), T[zq][:, p:e].bitcast(dt.uint8), key, sem)
+            k += send(STEP[n - 1], T[zp][:, p:e], T[zs][:, p:e], key, sem)
+            arrives(sem, k, ["%s%d" % (zl, h)])
+        if n == len(STEP):
+            inverse()
+        return conv(bk)
+
+    def new_state_between(n, back):
+        zl, zp, xq, xs = "zl%d" % n, "zp%d" % n, "xq%d" % n, "xs%d" % n
+
+        def r_copy(b):
+            op("s", ["pb%d" % b], ["r%d0" % b], lambda: S.activation(T["r%d" % b][:], T.pb[:, 512 * b:512 * b + C], COPY, scale=0.03125))
+
+        def x_add(b):
+            op("v", ["r%d0" % b, "f%d" % b, tok(back)], ["xt_%d0" % b], lambda: V.tensor_tensor(T.xt[:, b:4 * C:4], by("r%d" % b, back), T["f%d" % b][:], ADD))
+            if b == 3:
+                op("v", ["xt_%d0" % k for k in range(4)], [xq], lambda: V.quantize_mx(T[xq][:, 0:C], T[xs][:, 0:C], T.xt[:, 0:4 * C]))
+
+        for b in range(4):
+            op("t", ["wq", "wp", "%s0" % zl], ["pb%d" % b], lambda: g.tensor.matmul_mx(T.pb[:, 512 * b:512 * b + C], T.wq[:, 128 * b:128 * b + 128], T.wp[:, 128 * b:128 * b + 128], T[zl][:, 0:C], T[zp][:, 0:C], True, True))
+            out["fill_s"].append(lambda b=b: r_copy(b))
+            out["fill_v"].append(lambda b=b: x_add(b))
+
+    def new_state(n, back):
+        zl, zp, xq, xs = "zl%d" % n, "zp%d" % n, "xq%d" % n, "xs%d" % n
+        parts = pieces(n)
+        for h, (p, e) in enumerate(parts):
+            bank = "pb" if h == 0 else "pa"
+            for b in range(4):
+                op("t", ["wq", "wp", "%s%d" % (zl, h)], ["%s%d" % (bank, b)], lambda: g.tensor.matmul_mx(T[bank][:, 512 * b:512 * b + e - p], T.wq[:, 128 * b:128 * b + 128], T.wp[:, 128 * b:128 * b + 128], T[zl][:, p:e], T[zp][:, p:e], True, True))
+                op("s", ["%s%d" % (bank, b)], ["r%d%d" % (b, h)], lambda: S.activation(T["r%d" % b][:, p:e], T[bank][:, 512 * b:512 * b + e - p], COPY, scale=0.03125))
+        for h, (p, e) in enumerate(parts):
+            for b in range(4):
+                op("v", ["r%d%d" % (b, k) for k in range(2)] + ["f%d" % b, tok(back)], ["xt_%d%d" % (b, h)], lambda: V.tensor_tensor(T.xt[:, 4 * p + b:4 * e:4], T["r%d" % b][:, 0:C].indirect(T.tu[:, K * back + p // 16:K * back + e // 16]), T["f%d" % b][:, p:e], ADD))
+            op("v", ["xt_%d%d" % (b, h) for b in range(4)], [xq if n < len(STEP) else "%s%d" % (xq, h)], lambda: V.quantize_mx(T[xq][:, p:e], T[xs][:, p:e], T.xt[:, 4 * p:4 * e]))
+            if n == len(STEP):
+                results(h, p, e)
+
+    def results(h, p, e):
+        key, bank = "xq3%d" % h, "pb%d" % h
+        op("t", ["qv", key], [bank], lambda: g.tensor.matmul_mx(T.pb[:, 512 * h:512 * h + e - p], T.qv[:, 0:128], T.sv[:, 0:128], T.xq3[:, p:e], T.xs3[:, p:e], True, True))
+        load("y", "l_oc%d" % h, [key], [], [(T.oc[:, 4 * p:4 * e], T.xq3[:, p:e].bitcast(dt.uint8))])
+        op("s", [bank], ["ysb%d" % h], lambda: S.activation(T.ysb[:, p:e], T.pb[:, 512 * h:512 * h + e - p], COPY))
+        load("y", "l_y%d" % h, ["ysb%d" % h], [], [(T.y[:, p:e], T.ysb[:, p:e])])
+        load("s", "l_osc%d" % h, [key], [], [(T.osc[4 * k:4 * k + 4, p:e], T.xs3[32 * k:32 * k + 4, p:e]) for k in range(4)])
+
+    ch = chain(1, o_u, o_f, TV1)
+    if not LATE:
+        next(ch)
+    op("v", ["uoi"], ["uo"], lambda: V.tensor_copy(T.uo[:], T.uoi[:]))
+    op("v", ["ut"], ["qu"], lambda: V.quantize_mx(T.qu[:, 0:128], T.su[:, 0:128], T.ut[:, 0:512]))
+    op("v", ["qu", "uo"], ["qur"], lambda: V.tensor_copy(T.qur[:, 0:128].bitcast(dt.uint32), T.qu[:, 0:128].bitcast(dt.uint32).indirect(T.uo[:, 0:8])))
+    for b in range(4):
+        op("v", ["eye"], ["qe%d" % b], lambda: V.quantize_mx(T.qe[:, 128 * b:128 * b + 128], T.se[:, 128 * b:128 * b + 128], T.eye[:, 3 - b:515 - b]))
+    if LATE:
+        if LATE > 1:
+            op("v", ["xt0"], ["xq0"], lambda: V.quantize_mx(T.xq0[:, 0:C], T.xs0[:, 0:C], T.xt0[:, 0:4 * C]))
+        next(ch)
+    next(ch)
+    next(ch)
+    op("s", ["rti"], ["rst"], lambda: S.activation(T.rst[:], T.rti[:], ActivationFunctionType.Sign))
+    op("s", ["qu", "uo"], ["sur"], lambda: S.activation(T.sur[:, 0:128], T.su[:, 0:128].indirect(T.uo[:, 0:8]), COPY))
+    if LATE < 2:
+        op("v", ["xt0"], ["xq0"], lambda: V.quantize_mx(T.xq0[:, 0:C], T.xs0[:, 0:C], T.xt0[:, 0:4 * C]))
+    unpack_products(0)
+    for fs in F1:
+        next(ch)
+        for b in fs:
+            f_copy(b)
+    next(ch)
+    scores(o_u)
+    f_copy(3)
+    next(ch)
+    next(ch)
+
+    for n in (1, 2, 3):
+        o_u, o_f = choose(o_f)
+        back = means(n, o_u)
+        if n < 3:
+            ch = chain(n + 1, o_u, o_f, TV2)
+            for _ in range(PRE):
+                next(ch)
+            new_state_between(n, back)
+            next(ch)
+            unpack_products(n)
+            for fs in F2[0]:
+                next(ch)
+                for b in fs:
+                    f_copy(b)
+            scores(o_u)
+            for fs in F2[1]:
+                for b in fs:
+                    f_copy(b)
+                next(ch)
+        else:
+            op("s", ["iotf", tok(o_u)], ["osp"], lambda: S.activation(T.osp[:], by("iotf", o_u), COPY))
+            load("y", "l_fo", ["osp"], ["fo"], [(T.fo[:, 0:C], T.osp[0:128:16, 0:C])])
+            op("v", ["vt"], ["qv"], lambda: V.quantize_mx(T.qv[:, 0:128], T.sv[:, 0:128], T.vt[:, 0:512]))
+            new_state(n, back)
+
+    for sem in sorted(totals):
+        if seen["g"].get(sem, 0) < totals[sem]:
+            g.wait_ge(T.sem[sem], totals[sem])

@@ -3,24 +3,49 @@ from concourse.mybir import dt, AluOpType, ActivationFunctionType
 C = 448
 K = C // 16
 STEP = [1, 2, 3]
-RADIX = [3, 3, 2, 3, 3, 3]
-F1 = ((0,), (1,), (2,))
-F2 = (((0, 1),), ((2,), (3,)))
-LATE = 0
-VF0 = False
-PRE = 4
-TV1, TV2 = (0, 1, 2, 3), (1, 2, 4)
 MID = C // 2
 UP = 512.0
-SCN = "float16"
+LAST = [(0, 224), (224, C)]
+ENDS = [(0, 320), (320, C)]
 
+RADIX = {n: [2, 3, 3, 3, 3, 3] for n in (1, 2, 3)}
+APART = {2: "h2 h3", 3: "h2 h3", 4: "h20 h30 h21 h31"}
+SHARED = {1: (), 2: (), 3: (3,)}
+SPLIT = {1: "dm", 2: "dm", 3: "dm", 4: ""}
+BEHIND = ""
+BOTH = ()
+
+
+def line(head, stage, last, tail, behind):
+    moved = " ".join(behind.values()).split()
+    names = [k.replace("#", str(j)) for j in range(1, last + 1) for k in stage.split()]
+    return " ".join([head] + [name + " " + behind.get(name, "") for name in names if name not in moved] + [tail])
+
+
+PLAN = {
+    "v": {1: line("ones md idx e1 bia0 iots uo e0 ou d0 inv d1 eye d2 qu e1q mid d3 e2q e0q d4 e3q d5 qx bia1 ka kb ia m ib of ic", "a# b# l# l#'", 5, "la lb dm> base ds t nf nu",
+                  {"b1": "qur", "b2": "w2", "a3": "w3", "b3": "delta", "l3": "less", "b4": "w4", "a5": "w5"}),
+          2: line("u2 es u1 et ef eu u3 u0 k ka kb w1 qz m", "a# b# l# l#'", 5, "la lb dm> ds t nf nu",
+                  {"l1'": "delta", "a2": "less", "b2": "base", "l2'": "r0", "b3": "x0", "l3": "x1", "a4": "x2", "b4": "x3 qx", "l4": "a5", "b5": "w5"}),
+          4: "u2 u1 u0 u3 z30 qz0 z01 qz1 es et ef qv eu r10 r20 r00 r11 x10 r31 x11 r21 x00 x30 x20 qx0 x21 x01 x31 qx1 y1"},
+    "s": {1: line("sur k p0 w1", "p# p#'", 4, "f2 sc so dm<", {"p1'": "f0", "p2'": "f3", "p3'": "f1"}),
+          2: line("dd z2 z1 bk z3 z0 p0", "p# p#'", 4, "f2 f1 sc f0 so dm< f3", {"p1'": "w2", "p2": "r3", "p2'": "r1", "p3": "r2", "p3'": "h2 h3"}),
+          4: "dd g3 z20 z10 z00 z21 z11 z31 osp r30 r01 h30 h20 h21 h31 y0 yo1"},
+    "g": {1: "mdi one uoi send_o send_b", 2: "send_o send_b send_z w3 w4", 4: "send_z0 send_z1"},
+    "t": {1: "mf0 mf3 mf1 mf2 ms", 2: "mr3 mr0 mr1 mr2 mf2 mf1 ms mf0 mf3", 4: "mr10 mr20 mr00 mr11 mr30 mr31 mr01 mr21 my0 my1"},
+    "y": {1: "od u x wc v ws fd0 fd3 fd1 fd2", 2: "fd2 fd1 fd0 fd3", 4: "fo oc0 yo0 oc1 o0 o1 o2 o3"},
+}
+LIKE = {1: 1, 2: 2, 3: 2, 4: 4}
+ON_VECTOR = {n: PLAN["v"][LIKE[n]] for n in LIKE}
+BY_DMA = {n: PLAN["y"][LIKE[n]] for n in LIKE}
+STORES = {name: q for q in "sy" for name in PLAN[q][4].split()}
+TWIN = {n: "-" + "".join(q for j in range(1, len(RADIX[n])) for q in "vsg" if "w%d" % j in PLAN[q][LIKE[n]].split()) for n in RADIX}
+
+LISTS = 36
 SCRATCH = {
-    "md": ("sbuf", [128, C], "int32"), "rti": ("sbuf", [128, C], "bfloat16"), "m4": ("sbuf", [128, 4], "float32"),
-    "thr": ("sbuf", [128, C], "float32"), "d0": ("sbuf", [128, C], "bfloat16"),
-    "da": ("sbuf", [128, C], "bfloat16"), "db": ("sbuf", [128, C], "bfloat16"),
-    "rst": ("sbuf", [128, C], "bfloat16"), "iots": ("sbuf", [128, C], "bfloat16"),
-    "iotd": ("sbuf", [128, C], "bfloat16"), "iotf": ("sbuf", [128, C], "float32"), "ones": ("sbuf", [128, 516], "bfloat16"),
-    "eye": ("sbuf", [128, 516], "bfloat16"), "bia": ("sbuf", [128, 4], "float32"),
+    "md": ("sbuf", [128, 16], "int32"), "ee": ("sbuf", [128, 32], "float32"), "d0": ("sbuf", [128, C], "bfloat16"),
+    "iots": ("sbuf", [128, C], "bfloat16"), "ones": ("sbuf", [128, 516], "bfloat16"),
+    "idx": ("sbuf", [128, 516], "float16"), "eye": ("sbuf", [128, 516], "bfloat16"), "bia": ("sbuf", [128, 4], "float32"),
     "uoi": ("sbuf", [128, 8], "int32"), "uo": ("sbuf", [128, 8], "uint16"),
     "odl": ("sbuf", [128, K], "int32"), "ut": ("sbuf", [128, 512], "bfloat16"),
     "vt": ("sbuf", [128, 512], "bfloat16"), "xt0": ("sbuf", [128, 4 * C], "bfloat16"),
@@ -29,13 +54,11 @@ SCRATCH = {
     "qv": ("sbuf", [128, 128], "float8_e4m3fn_x4"), "sv": ("sbuf", [128, 128], "uint8"),
     "qe": ("sbuf", [128, 512], "float8_e4m3fn_x4"), "se": ("sbuf", [128, 512], "uint8"),
     "wq": ("sbuf", [128, 512], "float8_e4m3fn_x4"), "wp": ("sbuf", [128, 512], "uint8"),
-    "odr": ("sbuf", [128, K], "int32"),
-    "sc": ("sbuf", [128, C], "float32"), "so": ("sbuf", [128, C], "float32"),
-    "dm": ("sbuf", [128, C], "bfloat16"), "ds": ("sbuf", [128, C], "bfloat16"),
-
+    "sc": ("sbuf", [128, C], "bfloat16"), "so": ("sbuf", [128, C], "bfloat16"),
     "zt": ("sbuf", [128, 4 * C], "bfloat16"), "xt": ("sbuf", [128, 4 * C], "bfloat16"),
     "ysb": ("sbuf", [128, C], "float32"), "osp": ("sbuf", [128, C], "float32"),
-    "tu": ("sbuf", [128, K * 40], "uint16"), "tf": ("sbuf", [128, K * 20], "float32"),
+    "ls": ("sbuf", [128, C * LISTS], "bfloat16"), "hs": ("sbuf", [128, C * 14], "float16"),
+    "tu": ("sbuf", [128, K * 48], "uint16"), "tf": ("sbuf", [128, K * 48], "float32"),
     "pa": ("psum", [128, 2048], "float32"), "pb": ("psum", [128, 2048], "float32"),
 }
 for _b in range(4):
@@ -43,26 +66,25 @@ for _b in range(4):
     SCRATCH["fd%d" % _b] = ("sbuf", [128, C], "bfloat16")
     SCRATCH["u%d" % _b] = ("sbuf", [128, C], "float32")
     SCRATCH["gg%d" % _b] = ("sbuf", [128, C], "bfloat16")
-    SCRATCH["ld%d" % _b] = ("sbuf", [128, C], "bfloat16")
     SCRATCH["r%d" % _b] = ("sbuf", [128, C], "float32")
-    SCRATCH["scn%d" % _b] = ("sbuf", [128, C], SCN)
-    SCRATCH["kb%d" % _b] = ("sbuf", [128, C], "bfloat16")
-    SCRATCH["lb%d" % _b] = ("sbuf", [128, C], "bfloat16")
+    SCRATCH["hh%d" % _b] = ("sbuf", [128, C], "float32")
     SCRATCH["xq%d" % _b] = ("sbuf", [128, C], "float8_e4m3fn_x4")
     SCRATCH["xs%d" % _b] = ("sbuf", [128, C], "uint8")
-SCRATCH["bk0"] = ("sbuf", [128, C], "bfloat16")
 for _n in (1, 2, 3):
+    SCRATCH["bk%d" % (_n - 1)] = ("sbuf", [128, C], "bfloat16")
+    SCRATCH["ol%d" % _n] = ("sbuf", [128, K], "uint16")
+    SCRATCH["bl%d" % _n] = ("sbuf", [128, 2 * K], "float32")
+    SCRATCH["ll%d" % _n] = ("sbuf", [128, K], "uint16")
+    SCRATCH["tw%d0" % _n] = ("sbuf", [128, C], "bfloat16")
+    SCRATCH["tw%d1" % _n] = ("sbuf", [128, C], "bfloat16")
     SCRATCH["zq%d" % _n] = ("sbuf", [128, C], "float8_e4m3fn_x4")
     SCRATCH["zs%d" % _n] = ("sbuf", [128, C], "uint8")
     SCRATCH["zl%d" % _n] = ("sbuf", [128, C], "float8_e4m3fn_x4")
     SCRATCH["zp%d" % _n] = ("sbuf", [128, C], "uint8")
-    SCRATCH["bk%d" % _n] = ("sbuf", [128, C], "bfloat16")
-for _n in (2, 3):
-    SCRATCH["ol%d" % _n] = ("sbuf", [128, K], "uint16")
 
-SEMAPHORES = ["cv", "cs", "ct", "cg", "sent", "a_od"] \
-    + ["a_z10", "a_z20", "a_z30", "a_z31"] + ["a_ol%d" % n for n in (2, 3)] \
-    + ["l_" + n for n in ("od", "x", "u", "v", "wc", "ws", "y0", "y1", "fo", "oc0", "oc1", "osc0", "osc1", "f0", "f1", "f2")]
+SEMAPHORES = ["cv", "cs", "ct", "cg", "sent"] \
+    + ["a_z10", "a_z20", "a_z30", "a_z31", "a_z32"] + ["a_%s%d" % (k, n) for k in "obl" for n in (1, 2, 3)] \
+    + ["l_" + n for n in ("od", "x", "u", "v", "wc", "ws", "y0", "y1", "fo", "oc0", "oc1", "osc0", "osc1", "osc2", "osc3", "f0", "f1", "f2", "f3")]
 
 ADD, MUL, SUB, MIN, MAX = AluOpType.add, AluOpType.mult, AluOpType.subtract, AluOpType.min, AluOpType.max
 COPY = ActivationFunctionType.Copy
@@ -72,369 +94,397 @@ def rank_program(g, core, T, topo):
     rank = T.rank_of(core)
     if rank is None:
         return
-    queues = {"v": g.vector, "s": g.scalar, "t": g.tensor, "g": g, "y": g.sync}
-    count = {"v": 0, "s": 0, "t": 0, "g": 0}
-    wrote, read, snap = {}, {}, {}
-    seen = {q: {} for q in queues}
-    totals = {}
-
-    def learn(q, sem, val):
-        s = seen[q]
-        if s.get(sem, 0) < val:
-            s[sem] = val
-        for a, b in snap.get((sem, val), {}).items():
-            if s.get(a, 0) < b:
-                s[a] = b
-
-    def await_for(q, reads, writes):
-        need = {}
-        for k in reads:
-            for sem, val in wrote.get(k, []):
-                need[sem] = max(need.get(sem, 0), val)
-        for k in writes:
-            for sem, val in wrote.get(k, []):
-                need[sem] = max(need.get(sem, 0), val)
-            for sem, val in read.get(k, []):
-                need[sem] = max(need.get(sem, 0), val)
-        for sem in sorted(need):
-            if seen[q].get(sem, 0) < need[sem]:
-                queues[q].wait_ge(T.sem[sem], need[sem])
-                learn(q, sem, need[sem])
-
-    def note(q, tok, reads, writes):
-        snap[tok] = dict(seen[q])
-        for k in reads:
-            read.setdefault(k, []).append(tok)
-        for k in writes:
-            wrote[k] = [tok]
-            read[k] = []
-
-    def op(q, reads, writes, call):
-        await_for(q, reads, writes)
-        count[q] += 1
-        sem = "c" + q
-        call().then_inc(T.sem[sem], 1)
-        totals[sem] = count[q]
-        note(q, (sem, count[q]), reads, writes)
-
-    def load(q, sem, reads, writes, pairs):
-        await_for(q, reads, writes)
-        for out, in_ in pairs:
-            queues[q].dma_start(out, in_).then_inc(T.sem[sem], 16)
-            totals[sem] = totals.get(sem, 0) + 16
-        note(q, (sem, totals[sem]), reads, writes)
-
-    def peer(step):
-        return T.cores[rank ^ step]
-
-    def bits(engines):
-        return sum(1 << e for e in engines)
-
-    def send(step, out, in_, key, sem, few=None):
-        dst = peer(step)
-        e = topo.engines(core, dst)
-        if few is not None:
-            e = e[few::2]
-        await_for("g", [key], [])
-        rid, pid, _ = topo.addr(dst)
-        g.remote_dma(out, in_, T.sem[sem], T.sem["sent"], pid, rid, bits(e))
-        totals["sent"] = totals.get("sent", 0) + len(e)
-        return len(e)
-
-    def arrives(sem, engines, keys):
-        totals[sem] = totals.get(sem, 0) + engines
-        for k in keys:
-            wrote[k] = [(sem, totals[sem])]
-        if len(keys) > 0:
-            snap.setdefault((sem, totals[sem]), {})
-
     V, S = g.vector, g.scalar
-    slots, fslots = [0], [0]
+    queues = {"v": V, "s": S, "t": g.tensor, "g": g, "y": g.sync}
 
-    def slot():
-        slots[0] += 1
-        return slots[0] - 1
+    calls, wrote, read = {}, {}, {}
+    phase = [1]
 
-    def fslot():
-        fslots[0] += 1
-        return fslots[0] - 1
+    def record(name, q, kind, reads, writes, what):
+        name = "%d:%s" % (phase[0], name)
+        after = set()
+        for k in reads:
+            after.update(wrote.get(k, []))
+        for k in writes:
+            after.update(wrote.get(k, []))
+            after.update(read.get(k, []))
+        for k in reads:
+            read.setdefault(k, []).append(name)
+        for k in writes:
+            wrote[k], read[k] = [name], []
+        calls[name] = {"q": q, "kind": kind, "after": after, "what": what}
 
-    def tu(i):
-        return T.tu[:, K * i:K * (i + 1)]
+    def op(name, q, reads, writes, call):
+        record(name, q, "op", reads, writes, call)
 
-    def tf(i):
-        return T.tf[:, K * i:K * (i + 1)]
+    def load(name, q, sem, reads, writes, pairs):
+        record(name, q, "load", reads, writes, (sem, pairs))
 
-    def by(name, i):
-        return T[name][:, 0:C].indirect(tu(i))
+    def send(name, step, pairs, key, sem, lands, few=None):
+        record(name, "g", "send", key, [lands], (step, pairs, sem, few))
 
-    def tok(i):
-        return "tu%d" % i
+    def issue(order):
+        count, totals, token, snap = {q: 0 for q in queues}, {}, {}, {}
+        seen = {q: {} for q in queues}
+        heads = {q: 0 for q in queues}
 
-    load("y", "l_od", [], ["odl"], [(T.odl[:], T.od[:])])
-    load("y", "l_u", [], ["ut"], [(T.ut[:], T.u[:])])
-    load("y", "l_x", [], ["xt0"], [(T.xt0[:], T.x[:])])
-    load("y", "l_wc", [], ["wq"], [(T.wq[:, 0:512].bitcast(dt.uint8), T.wc[:, 0:2048])])
-    load("y", "l_ws", [], ["wp"], [(T.wp[:, 0:512], T.ws[:, 0:512])])
-    load("y", "l_v", [], ["vt"], [(T.vt[:], T.v[:])])
+        def wait(q, sem, val):
+            if seen[q].get(sem, 0) < val:
+                queues[q].wait_ge(T.sem[sem], val)
+                seen[q][sem] = val
+                for a, b in snap.get((sem, val), {}).items():
+                    seen[q][a] = max(seen[q].get(a, 0), b)
 
-    op("g", [], ["md"], lambda: g.iota(T.md[:], [[1, C]], 128, -1))
-    op("g", [], ["iots"], lambda: g.iota(T.iots[:], [[1, C]], -MID, 0, allow_small_or_imprecise_dtypes=True))
-    op("v", [], ["ones"], lambda: V.memset(T.ones[:], 1.0))
-    op("v", [], ["m4a"], lambda: V.memset(T.m4[:, 0:1], -4.0))
-    op("v", [], ["m4b"], lambda: V.memset(T.m4[:, 1:2], 2 * UP))
-    arrives("a_od", send(STEP[0], T.odr[:], T.odl[:], "odl", "a_od", few=0), ["odr"])
-    op("g", ["ones"], ["eye"], lambda: g.affine_select(T.eye[:], T.ones[:], [[1, 516]], AluOpType.is_equal, 0.0, -3, -4))
-    op("g", [], ["uoi"], lambda: g.iota(T.uoi[:], [[16, 8]], 0, 0))
-    op("g", [], ["iotd"], lambda: g.iota(T.iotd[:], [[1, C]], -MID, 0, allow_small_or_imprecise_dtypes=True))
-    op("g", [], ["rti"], lambda: g.iota(T.rti[:], [[0, K], [1, 16]], 0, 0, allow_small_or_imprecise_dtypes=True))
-    op("g", [], ["iotf"], lambda: g.iota(T.iotf[:], [[1, C]], 0, 0, allow_small_or_imprecise_dtypes=True))
-
-    op("v", ["md"], ["md"], lambda: V.tensor_scalar(T.md[:], T.md[:], 15, None, AluOpType.bitwise_and))
-    op("v", ["md"], ["da"], lambda: V.tensor_scalar(T.da[:], T.md[:], 2.0, 3.0, MIN, MUL))
-    op("s", ["da", "m4a", "m4b"], ["db"], lambda: S.activation(T.db[:], T.da[:], ActivationFunctionType.Abs, bias=T.m4[:, 0:1]))
-    op("s", ["db"], ["d0"], lambda: S.activation(T.d0[:], T.db[:], ActivationFunctionType.Identity, bias=T.m4[:, 1:2], scale=-UP))
-    op("s", ["da"], ["thr"], lambda: S.activation(T.thr[:], T.da[:], COPY, scale=1e28))
-    o_u, o_f = slot(), fslot()
-    op("v", ["odl"], [tok(o_u)], lambda: V.tensor_copy(tu(o_u), T.odl[:]))
-    op("v", ["odl"], ["tf%d" % o_f], lambda: V.tensor_copy(tf(o_f), T.odl[:]))
-    op("v", ["iots", tok(o_u)], ["bk0"], lambda: V.tensor_copy(by("bk0", o_u), T.iots[:]))
-    op("v", ["md"], ["bia0"], lambda: V.tensor_scalar(T.bia[:, 0:1], T.md[:, 15:16], 0.0, UP, AluOpType.is_equal, MUL))
-    op("v", ["bia0"], ["bia"], lambda: V.tensor_scalar(T.bia[:, 1:2], T.bia[:, 0:1], MID - UP, None, ADD))
-
-    def conv(name, between=None):
-        i = slot()
-        h = "scn%d" % (i % 4)
-        op("v", [name, "d0"], [h], lambda: V.tensor_tensor_scan(T[h][:], T.d0[:], T[name][:], 0.0, ADD, MAX))
-        if between is not None:
-            between()
-        op("v", [h, "bia"], [tok(i)], lambda: V.tensor_scalar(tu(i), T[h][:, 15:C:16], T.bia[:, 1:2], None, ADD))
-        return i
-
-    out = {"fill_s": [], "fill_v": []}
-
-    def between(k):
-        if len(out[k]) > 0:
-            out[k].pop(0)()
-
-    def drain(k):
-        while len(out[k]) > 0:
-            out[k].pop(0)()
-
-    def chain(n, o_u, o_f, twin_v):
-        star = fslot()
-        delta = fslot()
-        bk = "bk%d" % (n - 1)
-        src = "odr" if n == 1 else "ol%d" % n
-        offs, okey = T[src][:, 0:K], src
-        if n == 1:
-            su = slot()
-            op("v", ["odr"], [tok(su)], lambda: V.tensor_copy(tu(su), T.odr[:]))
-            offs, okey = tu(su), tok(su)
-        kn, kname = 0, "kb0"
-        op("s", [bk, okey], [kname], lambda: S.activation(T[kname][:], T[bk][:, 0:C].indirect(offs), COPY))
-        if n == 1:
-            yield
-        a = conv(kname)
-        op("v", [src], ["tf%d" % star], lambda: V.tensor_copy(tf(star), T[src][:]))
-        op("v", ["tf%d" % star, "tf%d" % o_f], ["tf%d" % delta], lambda: V.tensor_tensor(tf(delta), tf(star), tf(o_f), SUB))
-        yield
-        low, ln, twin = "iots", 0, "iotd"
-        for j, r in enumerate(RADIX):
-            last = j == len(RADIX) - 1
-            acc = twin
-            cur = kname
-            if not last:
-                for e in range(r - 1):
-                    kn = (kn + 1) % 4
-                    new = "kb%d" % kn
-                    between("fill_s")
-                    op("s", [cur, tok(a)], [new], lambda: S.activation(T[new][:], by(cur, a), COPY))
-                    cur = new
-            drain("fill_s")
-            for e in range(r - 1):
-                if e > 0 or VF0:
-                    between("fill_v")
-                ln = (ln + 1) % 4
-                lnew = "lb%d" % ln
-                op("v", [acc, low, tok(a)], [lnew], lambda: V.tensor_tensor(T[lnew][:], by(acc, a), T[low][:], MIN))
-                acc = lnew
-            low = acc
-            kname = cur
-            if not last:
-                twin = "ld%d" % (j % 4)
-                between("fill_v")
-                if j in twin_v:
-                    a = conv(kname, lambda: op("v", [low], [twin], lambda: V.tensor_copy(T[twin][:], T[low][:])))
-                else:
-                    op("s", [low], [twin], lambda: S.activation(T[twin][:], T[low][:], COPY))
-                    a = conv(kname)
-            drain("fill_v")
-            yield
-        out["low"] = conv(low)
-        out["delta"] = delta
-        yield
-
-    def pieces(n):
-        return [(0, C)] if n < len(STEP) else [(0, C // 2), (C // 2, C)]
-
-    def unpack_products(n):
-        xq, xs = "xq%d" % n, "xs%d" % n
-        op("t", ["qur", "sur", xq], ["pb0"], lambda: g.tensor.matmul_mx(T.pb[:, 0:C], T.qur[:, 0:128], T.sur[:, 0:128], T[xq][:, 0:C], T[xs][:, 0:C], True, True))
-        for b in range(4):
-            op("t", ["qe%d" % b, xq], ["pa%d" % b], lambda: g.tensor.matmul_mx(T.pa[:, 512 * b:512 * b + C], T.qe[:, 128 * b:128 * b + 128], T.se[:, 128 * b:128 * b + 128], T[xq][:, 0:C], T[xs][:, 0:C], True, True))
-
-    def f_copy(b):
-        op("s", ["pa%d" % b], ["f%d" % b], lambda: S.activation(T["f%d" % b][:], T.pa[:, 512 * b:512 * b + C], COPY))
-        if b < 3:
-            load("y", "l_f%d" % b, ["f%d" % b], ["fd%d" % b], [(T["fd%d" % b][:], T["f%d" % b][:])])
-
-    def scores(o_u):
-        op("s", ["pb0"], ["sc"], lambda: S.activation(T.sc[:], T.pb[:, 0:C], COPY))
-        op("s", ["sc", tok(o_u)], ["so"], lambda: S.activation(T.so[:], by("sc", o_u), COPY))
-
-    def choose(o_f):
-        low, delta = out["low"], out["delta"]
-        t, nf, nu = fslot(), fslot(), slot()
-        op("v", ["so", "thr", tok(low)], ["dm"], lambda: V.tensor_tensor(T.dm[:], by("so", low), T.thr[:], AluOpType.is_gt))
-        op("v", ["dm", "rst"], ["ds"], lambda: V.tensor_tensor_scan(T.ds[:], T.rst[:], T.dm[:], 0.0, MUL, ADD))
-        op("v", ["ds", "tf%d" % delta], ["tf%d" % t], lambda: V.tensor_tensor(tf(t), T.ds[:, 15:C:16], tf(delta), MUL))
-        op("v", ["tf%d" % t, "tf%d" % o_f], ["tf%d" % nf], lambda: V.tensor_tensor(tf(nf), tf(t), tf(o_f), ADD))
-        op("v", ["tf%d" % nf], [tok(nu)], lambda: V.tensor_copy(tu(nu), tf(nf)))
-        return nu, nf
-
-    def means(n, o_u):
-        bk = "bk%d" % n
-
-        def inverse():
-            op("v", ["iots", tok(o_u)], [bk], lambda: V.tensor_copy(by(bk, o_u), T.iots[:]))
-
-        if n < len(STEP):
-            m = n + 1
-            arrives("a_ol%d" % m, send(STEP[n], T["ol%d" % m][:], tu(o_u), tok(o_u), "a_ol%d" % m, few=1), ["ol%d" % m])
-        shared = (3,)
-        for b in shared:
-            op("s", ["f%d" % b, tok(o_u)], ["gg%d" % b], lambda: S.activation(T["gg%d" % b][:], by("f%d" % b, o_u), COPY))
-        parts = pieces(n)
-        turn = [(b, 0) for b in range(4)]
-        for b in range(4):
-            if b in shared:
-                op("v", ["gg%d" % b, "pa%d" % b], ["u%d" % b], lambda: V.tensor_tensor(T["u%d" % b][:], T["gg%d" % b][:], T.pa[:, 512 * b:512 * b + C], ADD))
+        def emit(name):
+            c = calls[name]
+            q, need = c["q"], {}
+            for a in c["after"]:
+                sem, val = token[a]
+                need[sem] = max(need.get(sem, 0), val)
+            for sem in sorted(need):
+                wait(q, sem, need[sem])
+            if c["kind"] == "op":
+                count[q] += 1
+                sem = "c" + q
+                c["what"]().then_inc(T.sem[sem], 1)
+                totals[sem] = count[q]
+            elif c["kind"] == "load":
+                sem, pairs = c["what"]
+                for out, in_ in pairs:
+                    queues[q].dma_start(out, in_).then_inc(T.sem[sem], 16)
+                    totals[sem] = totals.get(sem, 0) + 16
             else:
-                op("v", ["f%d" % b, "fd%d" % b, tok(o_u)], ["u%d" % b], lambda: V.tensor_tensor(T["u%d" % b][:], by("f%d" % b, o_u), T["fd%d" % b][:], ADD))
-        if len(parts) == 2:
-            turn = [(0, 0), (0, 1), (1, 0), (2, 0), (1, 1), (2, 1)]
-        for b, h in turn:
-            p, e = parts[h]
-            op("s", ["u%d" % b, tok(o_u)], ["zt%d%d" % (b, h)], lambda: S.activation(T.zt[:, 4 * p + b:4 * e:4], T["u%d" % b][:, 0:C].indirect(T.tu[:, K * o_u + p // 16:K * o_u + e // 16]), COPY, scale=0.5))
-        if n < len(STEP):
-            inverse()
+                step, pairs, sem, few = c["what"]
+                dst = T.cores[rank ^ step]
+                e = topo.engines(core, dst)
+                if few is not None:
+                    e = e[few::2]
+                rid, pid, _ = topo.addr(dst)
+                for out, in_ in pairs:
+                    g.remote_dma(out, in_, T.sem[sem], T.sem["sent"], pid, rid, sum(1 << i for i in e))
+                    totals["sent"] = totals.get("sent", 0) + len(e)
+                    totals[sem] = totals.get(sem, 0) + len(e)
+            token[name] = (sem, totals[sem])
+            snap[token[name]] = dict(seen[q]) if c["kind"] != "send" else {}
+
+        left = len(calls)
+        while left > 0:
+            before = left
+            for q in queues:
+                while heads[q] < len(order[q]) and all(a in token for a in calls[order[q][heads[q]]]["after"]):
+                    emit(order[q][heads[q]])
+                    heads[q] += 1
+                    left -= 1
+            assert left < before, [order[q][heads[q]] for q in queues if heads[q] < len(order[q])]
+        for sem in sorted(totals):
+            wait("g", sem, totals[sem])
+
+    used = {"tu": 0, "tf": 0, "ls": 0, "hs": 0}
+    width = {"tu": K, "tf": K, "ls": C, "hs": C}
+    ring = {"tu": 48, "tf": 48, "ls": LISTS, "hs": 14}
+
+    def new(kind):
+        used[kind] += 1
+        return "%s.%d" % (kind, (used[kind] - 1) % ring[kind])
+
+    def pair():
+        used["tf"] += used["tf"] % 2
+        return [new("tf"), new("tf")]
+
+    def ap(key, a=0, b=None, step=1, part=slice(0, 128)):
+        if "." in key:
+            kind, i = key.split(".")
+            w = width[kind]
+            return T[kind][part, w * int(i) + a:w * int(i) + (w if b is None else b):step]
+        return T[key][part, a:(C if b is None else b):step]
+
+    def by(key, table, p=0, e=C):
+        return ap(key).indirect(ap(table, p // 16, e // 16))
+
+    def move(name, reads, writes, out, in_, scale=None):
+        if name not in ON_VECTOR[phase[0]].split():
+            op(name, "s", reads, writes, lambda: S.activation(out, in_, COPY, scale=1.0 if scale is None else scale))
+        elif scale is None:
+            op(name, "v", reads, writes, lambda: V.tensor_copy(out, in_))
+        else:
+            op(name, "v", reads, writes, lambda: V.tensor_scalar(out, in_, scale, None, MUL))
+
+    def gather(name, out, key, table):
+        if name not in SPLIT[phase[0]].split():
+            return move(name, [key, table], [out], ap(out), by(key, table))
+        before = wrote.get(out, []), read.get(out, [])
+        move(name + "<", [key, table], [out], ap(out, 0, MID), by(key, table, 0, MID))
+        first = wrote[out]
+        wrote[out], read[out] = before
+        move(name + ">", [key, table], [out], ap(out, MID, C), by(key, table, MID, C))
+        wrote[out] = first + wrote[out]
+
+    def scan(name, key, part=slice(0, 128)):
+        h = new("hs")
+        op(name, "v", [key, "d0"], [h], lambda: V.tensor_tensor_scan(ap(h, 0, C, 1, part), T.d0[part, 0:C], ap(key, 0, C, 1, part), 0.0, ADD, MAX))
+        return h
+
+    def conv(a, b, key):
+        h, t = scan(a, key), new("tu")
+        op(b, "v", [h, "bia"], [t], lambda: V.tensor_scalar(ap(t), ap(h, 15, C, 16), T.bia[:, 1:2], None, ADD))
+        return t
+
+    load("od", "y", "l_od", [], ["odl"], [(T.odl[:], T.od[:])])
+    op("mdi", "g", [], ["md"], lambda: g.iota(T.md[:], [[1, 16]], 128, -1))
+    op("one", "g", [], ["one"], lambda: g.iota(T.bia[:, 3:4], [[1, 1]], 3, 4, allow_small_or_imprecise_dtypes=True))
+    op("uoi", "g", [], ["uoi"], lambda: g.iota(T.uoi[:], [[16, 8]], 0, 0))
+    op("ones", "v", [], ["ones"], lambda: V.memset(T.ones[:], 1.0))
+    op("idx", "v", ["ones"], ["idx"], lambda: V.tensor_tensor_scan(T.idx[:], T.ones[:], T.ones[:], -1.0, ADD, MUL))
+    op("iots", "v", ["idx"], ["iots"], lambda: V.tensor_scalar(T.iots[:], T.idx[:, 0:C], float(-MID), None, ADD))
+    op("eye", "v", ["idx", "one"], ["eye"], lambda: V.tensor_scalar(T.eye[:], T.idx[:], T.bia[:, 3:4], None, AluOpType.is_equal))
+    op("md", "v", ["md"], ["md"], lambda: V.tensor_scalar(T.md[:], T.md[:], 15, None, AluOpType.bitwise_and))
+    op("e0", "v", ["md"], ["e0"], lambda: V.tensor_scalar(T.ee[:, 0:16], T.md[:], 0.0, -2 * UP, AluOpType.is_equal, MUL))
+    op("e1", "v", ["md"], ["e1"], lambda: V.tensor_scalar(T.ee[:, 16:32], T.md[:], 1.0, UP, AluOpType.is_equal, MUL))
+    op("d0", "v", ["e0", "e1"], ["d0"], lambda: V.tensor_tensor(T.d0[:, 0:16], T.ee[:, 0:16], T.ee[:, 16:32], ADD))
+    for i in range(5):
+        w = 16 << i
+        op("d%d" % (i + 1), "v", ["d0"], ["d0"], lambda w=w: V.tensor_copy(T.d0[:, w:min(2 * w, C)], T.d0[:, 0:min(w, C - w)]))
+    op("bia0", "v", ["md"], ["bia0"], lambda: V.tensor_scalar(T.bia[:, 0:1], T.md[:, 15:16], 0.0, -UP, AluOpType.not_equal, MUL))
+    op("bia1", "v", ["bia0"], ["bia"], lambda: V.tensor_scalar(T.bia[:, 1:2], T.bia[:, 0:1], float(MID), None, ADD))
+    op("mid", "v", [], ["mid"], lambda: V.memset(T.bia[:, 2:3], float(MID)))
+    op("uo", "v", ["uoi"], ["uo"], lambda: V.tensor_copy(T.uo[:], T.uoi[:]))
+    for b in range(4):
+        op("e%dq" % b, "v", ["eye"], ["qe%d" % b], lambda b=b: V.quantize_mx(T.qe[:, 128 * b:128 * b + 128], T.se[:, 128 * b:128 * b + 128], T.eye[:, 3 - b:515 - b]))
+
+    def first_state():
+        for name, key, out, in_ in (("u", "ut", T.ut[:], T.u[:]), ("x", "xt0", T.xt0[:], T.x[:]), ("v", "vt", T.vt[:], T.v[:]),
+                                    ("wc", "wq", T.wq[:, 0:512].bitcast(dt.uint8), T.wc[:, 0:2048]), ("ws", "wp", T.wp[:, 0:512], T.ws[:, 0:512])):
+            load(name, "y", "l_" + name, ["ol1"] if name in BEHIND.split() else [], [key], [(out, in_)])
+        op("qu", "v", ["ut"], ["qu"], lambda: V.quantize_mx(T.qu[:, 0:128], T.su[:, 0:128], T.ut[:, 0:512]))
+        op("qur", "v", ["qu", "uo"], ["qur"], lambda: V.tensor_copy(T.qur[:, 0:128].bitcast(dt.uint32), T.qu[:, 0:128].bitcast(dt.uint32).indirect(T.uo[:, 0:8])))
+        op("sur", "s", ["qu", "uo"], ["sur"], lambda: S.activation(T.sur[:, 0:128], T.su[:, 0:128].indirect(T.uo[:, 0:8]), COPY))
+        op("qx", "v", ["xt0"], ["xq0"], lambda: V.quantize_mx(T.xq0[:, 0:C], T.xs0[:, 0:C], T.xt0[:, 0:4 * C]))
+
+    def hand_on(n, o=None, own=None):
+        if o is not None:
+            send("send_o", STEP[n - 1], [(T["ol%d" % n][:], ap(o))], [o], "a_o%d" % n, "ol%d" % n, few=0 if n == 1 else None)
+        else:
+            send("send_b", STEP[n - 1], [(T["bl%d" % n][:], ap(own[0], 0, 2 * K))], own, "a_b%d" % n, "bl%d" % n, few=1 if n == 1 else None)
+
+    def first_orders():
+        o, own = new("tu"), pair()
+        op("ou", "v", ["odl"], [o], lambda: V.tensor_copy(ap(o), T.odl[:]))
+        hand_on(1, o=o)
+        op("of", "v", ["odl"], [own[0]], lambda: V.tensor_copy(ap(own[0]), T.odl[:]))
+        op("inv", "v", ["iots", o], ["bk0"], lambda: V.tensor_copy(by("bk0", o), T.iots[:]))
+        back = conv("ia", "ib", "bk0")
+        op("ic", "v", [back], [own[1]], lambda: V.tensor_copy(ap(own[1]), ap(back)))
+        hand_on(1, own=own)
+        return o, back, own
+
+    def apart(n, own):
+        delta, less, base = pair(), pair(), pair()
+        op("delta", "v", ["bl%d" % n] + own, delta, lambda: V.tensor_tensor(ap(delta[0], 0, 2 * K), T["bl%d" % n][:], ap(own[0], 0, 2 * K), SUB))
+        op("less", "v", delta + ["bia0"], less, lambda: V.tensor_scalar(ap(less[0], 0, 2 * K), ap(delta[0], 0, 2 * K), T.bia[:, 0:1], None, MUL))
+        op("base", "v", less + own, base, lambda: V.tensor_tensor(ap(base[0], 0, 2 * K), ap(less[0], 0, 2 * K), ap(own[0], 0, 2 * K), ADD))
+        return delta, base
+
+    def cycles(n):
+        k, m = new("ls"), new("ls")
+        gather("k", k, "bk%d" % (n - 1), "ol%d" % n)
+        a = conv("ka", "kb", k)
+
+        def least(name, out):
+            op(name, "v", ["iots", k], [out], lambda: V.tensor_tensor_scan(ap(out), T.iots[:], ap(k), -UP, MAX, MIN))
+
+        least("m", m)
+        low, power = m, k
+        radix = RADIX[n]
+        for j, r in enumerate(radix):
+            acc = k
+            if j > 0:
+                a = conv("a%d" % j, "b%d" % j, power)
+                acc, q = new("ls"), TWIN[n][j]
+                if low == m and q == "v":
+                    least("w%d" % j, acc)
+                elif q == "v":
+                    op("w%d" % j, "v", [low], [acc], lambda acc=acc, low=low: V.tensor_copy(ap(acc), ap(low)))
+                elif q == "s":
+                    op("w%d" % j, "s", [low], [acc], lambda acc=acc, low=low: S.activation(ap(acc), ap(low), COPY))
+                else:
+                    op("w%d" % j, "g", [low], [acc], lambda acc=acc, low=low: g.affine_select(ap(acc), ap(low), [[0, C]], AluOpType.is_equal, 0.0, 0, 0))
+            for e in range(r - 1 if j > 0 else r - 2):
+                out = new("ls")
+                op("l%d%s" % (j, "'" * e), "v", [acc, low, a], [out], lambda out=out, acc=acc, low=low, a=a: V.tensor_tensor(ap(out), by(acc, a), ap(low), MIN))
+                acc = out
+            if j > 0 or r > 2:
+                low = acc
+            if j < len(radix) - 1:
+                for e in range(r - 1):
+                    out = new("ls")
+                    gather("p%d%s" % (j, "'" * e), out, power, a)
+                    power = out
+        return conv("la", "lb", low)
+
+    def halves(n):
+        low, high = slice(0, 64), slice(64, 128)
+        return (low, high) if rank < rank ^ STEP[n - 1] else (high, low)
+
+    def ahead_of_cycles():
+        h = scan("ida", "iots") if BOTH else None
+        for n in BOTH:
+            first[n] = new("tu")
+            op("id%d" % n, "v", [h, "bia"], [first[n]], lambda n=n: V.tensor_scalar(ap(first[n]), ap(h, 15, C, 16), T.bia[:, 1:2], None, ADD))
+            for i in range(2):
+                name, out = "big%d%d" % (n, i), T["tw%d%d" % (n, i)][halves(n)[0], 0:C]
+                if name in ON_VECTOR[1].split():
+                    op(name, "v", [], [name], lambda out=out: V.memset(out, UP))
+                else:
+                    op(name, "g", [], [name], lambda out=out: g.iota(out, [[0, C]], int(UP), 0, allow_small_or_imprecise_dtypes=True))
+
+    def cycles_of_four(n):
+        H, L = halves(n)
+        k, w, a = new("ls"), new("ls"), first[n]
+
+        def table(name, h, out, part, src):
+            op(name, "v", [h, "bia", out], [out + str(part)], lambda: V.tensor_scalar(ap(out, 0, K, 1, part), ap(h, 15, C, 16, src), T.bia[src, 1:2], None, ADD))
+
+        def least(name, out, key):
+            op(name, "v", ["iots", k], [key], lambda: V.tensor_tensor_scan(ap(out, 0, C, 1, L), T.iots[H, 0:C], ap(k, 0, C, 1, H), -UP, MAX, MIN))
+
+        gather("k", k, "bk%d" % (n - 1), "ol%d" % n)
+        table("kb", scan("ka", k, H), a, H, H)
+        least("m", k, "m")
+        move("p0", [k, "m", a + str(H)], [w], ap(w), by(k, a))
+        for j, r in list(enumerate(RADIX[n]))[1:]:
+            h, a, twin, q = scan("a%d" % j, w, H), new("tu"), "tw%d%d" % (n, j % 2), TWIN[n][j]
+            table("b%d" % j, h, a, H, H)
+            table("c%d" % j, h, a, L, H)
+            out, in_ = T[twin][L, 0:C], ap(w, 0, C, 1, L)
+            if j == 1 and q == "v":
+                least("w1", twin, twin)
+            elif j == 1:
+                in_ = ap(k, 0, C, 1, L)
+            if q == "v" and j > 1:
+                op("w%d" % j, "v", [w], [twin], lambda out=out, in_=in_: V.tensor_copy(out, in_))
+            elif q == "s":
+                op("w%d" % j, "s", ["m" if j == 1 else w], [twin], lambda out=out, in_=in_: S.activation(out, in_, COPY))
+            elif q == "g":
+                op("w%d" % j, "g", ["m" if j == 1 else w], [twin], lambda out=out, in_=in_: g.affine_select(out, in_, [[0, C]], AluOpType.is_equal, 0.0, 0, 0))
+            for e in range(r - 1):
+                out = new("ls")
+                op("l%d%s" % (j, "'" * e), "v", [w, twin, "big%d%d" % (n, j % 2), a + str(H), a + str(L)], [out], lambda out=out, w=w, twin=twin, a=a: V.tensor_tensor(ap(out), by(w, a), T[twin][:], MIN))
+                w = out
+        h, lands = scan("la", w, L), "ll%d" % n
+        table("lb", h, a, H, L)
+        send("send_l", STEP[n - 1], [(T[lands][:], ap(a))], [a + str(H), a + str(L)], "a_l%d" % n, lands)
+        op("lc", "v", [h, "bia"], [lands], lambda: V.tensor_scalar(T[lands][H, 0:K], ap(h, 15, C, 16, L), T.bia[L, 1:2], None, ADD))
+        return lands
+
+    def unpack(n, o):
+        xq, xs = "xq%d" % n, "xs%d" % n
+        op("ms", "t", ["qur", "sur", xq], ["pb0"], lambda: g.tensor.matmul_mx(T.pb[:, 0:C], T.qur[:, 0:128], T.sur[:, 0:128], T[xq][:, 0:C], T[xs][:, 0:C], True, True))
+        for b in range(4):
+            op("mf%d" % b, "t", ["qe%d" % b, xq], ["pa%d" % b], lambda b=b: g.tensor.matmul_mx(T.pa[:, 512 * b:512 * b + C], T.qe[:, 128 * b:128 * b + 128], T.se[:, 128 * b:128 * b + 128], T[xq][:, 0:C], T[xs][:, 0:C], True, True))
+            move("f%d" % b, ["pa%d" % b], ["f%d" % b], T["f%d" % b][:], T.pa[:, 512 * b:512 * b + C])
+            if b in SHARED[n + 1]:
+                continue
+            if "fd%d" % b not in BY_DMA[phase[0]].split():
+                move("fd%d" % b, ["pa%d" % b], ["fd%d" % b], T["fd%d" % b][:], T.pa[:, 512 * b:512 * b + C])
+            else:
+                load("fd%d" % b, "y", "l_f%d" % b, ["f%d" % b], ["fd%d" % b], [(T["fd%d" % b][:], T["f%d" % b][:])])
+        op("sc", "s", ["pb0"], ["sc"], lambda: S.activation(T.sc[:], T.pb[:, 0:C], ActivationFunctionType.Sign))
+        op("so", "s", ["sc", o], ["so"], lambda: S.activation(T.so[:], by("sc", o), ActivationFunctionType.Relu))
+
+    def mix(names, dm, delta, base, out):
+        t, table = new("tf"), new("tu")
+        h = scan(names[0], dm)
+        op(names[1], "v", [h, delta], [t], lambda: V.tensor_tensor(ap(t), ap(h, 15, C, 16), ap(delta), MUL))
+        op(names[2], "v", [t, base], [out], lambda: V.tensor_tensor(ap(out), ap(t), ap(base), ADD))
+        op(names[3], "v", [out], [table], lambda: V.tensor_copy(ap(table), ap(out)))
+        return table
+
+    def sums(n, o):
+        for b in range(4):
+            f, u = "f%d" % b, "u%d" % b
+            if b in SHARED[n]:
+                move("g%d" % b, [f, o], ["gg%d" % b], T["gg%d" % b][:], by(f, o))
+                op(u, "v", ["gg%d" % b, "pa%d" % b], [u], lambda b=b, u=u: V.tensor_tensor(T[u][:], T["gg%d" % b][:], T.pa[:, 512 * b:512 * b + C], ADD))
+            else:
+                op(u, "v", [f, "fd%d" % b, o], [u], lambda b=b, f=f, u=u: V.tensor_tensor(T[u][:], by(f, o), T["fd%d" % b][:], ADD))
+
+    def means(n, o, parts):
         zq, zs, zl, zp = "zq%d" % n, "zs%d" % n, "zl%d" % n, "zp%d" % n
         for h, (p, e) in enumerate(parts):
-            key, sem = "%s%d" % (zq, h), "a_z%d%d" % (n, h)
-            if len(parts) == 2:
-                op("v", ["u3", tok(o_u)], ["zt3%d" % h], lambda: V.tensor_scalar(T.zt[:, 4 * p + 3:4 * e:4], T.u3[:, 0:C].indirect(T.tu[:, K * o_u + p // 16:K * o_u + e // 16]), 0.5, None, MUL))
-            op("v", ["zt%d%d" % (b, h) for b in range(4)], [key], lambda: V.quantize_mx(T[zq][:, p:e], T[zs][:, p:e], T.zt[:, 4 * p:4 * e]))
-            k = send(STEP[n - 1], T[zl][:, p:e].bitcast(dt.uint8), T[zq][:, p:e].bitcast(dt.uint8), key, sem)
-            k += send(STEP[n - 1], T[zp][:, p:e], T[zs][:, p:e], key, sem)
-            arrives(sem, k, ["%s%d" % (zl, h)])
-        if n == len(STEP):
-            inverse()
-        return conv(bk)
+            tag = str(h) if len(parts) > 1 else ""
+            for b in range(4):
+                move("z%d%s" % (b, tag), ["u%d" % b, o], ["zt%d%d" % (b, h)], T.zt[:, 4 * p + b:4 * e:4], by("u%d" % b, o, p, e), 0.5)
+            key = "%s%d" % (zq, h)
+            op("qz" + tag, "v", ["zt%d%d" % (b, h) for b in range(4)], [key], lambda p=p, e=e: V.quantize_mx(T[zq][:, p:e], T[zs][:, p:e], T.zt[:, 4 * p:4 * e]))
+            send("send_z" + tag, STEP[n - 1], [(T[zl][:, p:e].bitcast(dt.uint8), T[zq][:, p:e].bitcast(dt.uint8)), (T[zp][:, p:e], T[zs][:, p:e])], [key], "a_z%d%d" % (n, h), "%s%d" % (zl, h))
 
-    def new_state_between(n, back):
-        zl, zp, xq, xs = "zl%d" % n, "zp%d" % n, "xq%d" % n, "xs%d" % n
+    def layer(n, b, h, p, e, bank, name):
+        zl, zp = "zl%d" % n, "zp%d" % n
+        at = T[bank[:2]][:, 512 * int(bank[2]):512 * int(bank[2]) + e - p]
+        op("m" + name, "t", ["wq", "wp", "%s%d" % (zl, h)], [bank], lambda: g.tensor.matmul_mx(at, T.wq[:, 128 * b:128 * b + 128], T.wp[:, 128 * b:128 * b + 128], T[zl][:, p:e], T[zp][:, p:e], True, True))
+        move(name, [bank], ["r%d%d" % (b, h)], T["r%d" % b][:, p:e], at, 0.03125)
 
-        def r_copy(b):
-            op("s", ["pb%d" % b], ["r%d0" % b], lambda: S.activation(T["r%d" % b][:], T.pb[:, 512 * b:512 * b + C], COPY, scale=0.03125))
-
-        def x_add(b):
-            op("v", ["r%d0" % b, "f%d" % b, tok(back)], ["xt_%d0" % b], lambda: V.tensor_tensor(T.xt[:, b:4 * C:4], by("r%d" % b, back), T["f%d" % b][:], ADD))
-            if b == 3:
-                op("v", ["xt_%d0" % k for k in range(4)], [xq], lambda: V.quantize_mx(T[xq][:, 0:C], T[xs][:, 0:C], T.xt[:, 0:4 * C]))
-
-        for b in range(4):
-            op("t", ["wq", "wp", "%s0" % zl], ["pb%d" % b], lambda: g.tensor.matmul_mx(T.pb[:, 512 * b:512 * b + C], T.wq[:, 128 * b:128 * b + 128], T.wp[:, 128 * b:128 * b + 128], T[zl][:, 0:C], T[zp][:, 0:C], True, True))
-            out["fill_s"].append(lambda b=b: r_copy(b))
-            out["fill_v"].append(lambda b=b: x_add(b))
+    def home(b, h, p, e, runs, back, tag):
+        r, out, rs = "r%d" % b, T.xt[:, 4 * p + b:4 * e:4], ["r%d%d" % (b, i) for i in range(runs)]
+        if "h" + tag in APART[phase[0]].split():
+            move("h" + tag, rs + [back], ["hh%d%d" % (b, h)], T["hh%d" % b][:, p:e], by(r, back, p, e))
+            op("x" + tag, "v", ["hh%d%d" % (b, h), "pa%d" % b], ["xt%d%d" % (b, h)], lambda: V.tensor_tensor(out, T["hh%d" % b][:, p:e], T.pa[:, 512 * b + p:512 * b + e], ADD))
+        else:
+            op("x" + tag, "v", rs + ["f%d" % b, back], ["xt%d%d" % (b, h)], lambda: V.tensor_tensor(out, by(r, back, p, e), T["f%d" % b][:, p:e], ADD))
 
     def new_state(n, back):
-        zl, zp, xq, xs = "zl%d" % n, "zp%d" % n, "xq%d" % n, "xs%d" % n
-        parts = pieces(n)
-        for h, (p, e) in enumerate(parts):
-            bank = "pb" if h == 0 else "pa"
+        for b in range(4):
+            layer(n, b, 0, 0, C, "pb%d" % b, "r%d" % b)
+            home(b, 0, 0, C, 1, back, str(b))
+        op("qx", "v", ["xt%d0" % b for b in range(4)], ["xq%d" % n], lambda: V.quantize_mx(T["xq%d" % n][:, 0:C], T["xs%d" % n][:, 0:C], T.xt[:, 0:4 * C]))
+
+    def last_state(n, back, o):
+        op("osp", "s", ["iots", "mid", o], ["osp"], lambda: S.activation(T.osp[:], by("iots", o), ActivationFunctionType.Identity, bias=T.bia[:, 2:3]))
+        load("fo", "y", "l_fo", ["osp"], [], [(T.fo[:, 0:C], T.osp[0:128:16, 0:C])])
+        op("qv", "v", ["vt"], ["qv"], lambda: V.quantize_mx(T.qv[:, 0:128], T.sv[:, 0:128], T.vt[:, 0:512]))
+        banks = [["pb0", "pb1", "pb2", "pb3"], ["pa0", "pa1", "pb0", "pb1"]]
+        for h, (p, e) in enumerate(LAST):
             for b in range(4):
-                op("t", ["wq", "wp", "%s%d" % (zl, h)], ["%s%d" % (bank, b)], lambda: g.tensor.matmul_mx(T[bank][:, 512 * b:512 * b + e - p], T.wq[:, 128 * b:128 * b + 128], T.wp[:, 128 * b:128 * b + 128], T[zl][:, p:e], T[zp][:, p:e], True, True))
-                op("s", ["%s%d" % (bank, b)], ["r%d%d" % (b, h)], lambda: S.activation(T["r%d" % b][:, p:e], T[bank][:, 512 * b:512 * b + e - p], COPY, scale=0.03125))
-        for h, (p, e) in enumerate(parts):
+                layer(n, b, h, p, e, banks[h][b], "r%d%d" % (b, h))
+        for h, (p, e) in enumerate(ENDS):
             for b in range(4):
-                op("v", ["r%d%d" % (b, k) for k in range(2)] + ["f%d" % b, tok(back)], ["xt_%d%d" % (b, h)], lambda: V.tensor_tensor(T.xt[:, 4 * p + b:4 * e:4], T["r%d" % b][:, 0:C].indirect(T.tu[:, K * back + p // 16:K * back + e // 16]), T["f%d" % b][:, p:e], ADD))
-            op("v", ["xt_%d%d" % (b, h) for b in range(4)], [xq if n < len(STEP) else "%s%d" % (xq, h)], lambda: V.quantize_mx(T[xq][:, p:e], T[xs][:, p:e], T.xt[:, 4 * p:4 * e]))
-            if n == len(STEP):
-                results(h, p, e)
+                home(b, h, p, e, len(LAST), back, "%d%d" % (b, h))
+            key, bank = "xq3%d" % h, "pb%d" % (2 + h)
+            at = T.pb[:, 512 * (2 + h):512 * (2 + h) + e - p]
+            op("qx%d" % h, "v", ["xt%d%d" % (b, h) for b in range(4)], [key], lambda p=p, e=e: V.quantize_mx(T.xq3[:, p:e], T.xs3[:, p:e], T.xt[:, 4 * p:4 * e]))
+            op("my%d" % h, "t", ["qv", key], [bank], lambda at=at, p=p, e=e: g.tensor.matmul_mx(at, T.qv[:, 0:128], T.sv[:, 0:128], T.xq3[:, p:e], T.xs3[:, p:e], True, True))
+            load("oc%d" % h, STORES["oc%d" % h], "l_oc%d" % h, [key], [], [(T.oc[:, 4 * p:4 * e], T.xq3[:, p:e].bitcast(dt.uint8))])
+            move("y%d" % h, [bank], ["ysb%d" % h], T.ysb[:, p:e], at)
+            load("yo%d" % h, STORES["yo%d" % h], "l_y%d" % h, ["ysb%d" % h], [], [(T.y[:, p:e], T.ysb[:, p:e])])
+        for k in range(4):
+            load("o%d" % k, STORES["o%d" % k], "l_osc%d" % k, ["xq3%d" % h for h in range(len(ENDS))], [], [(T.osc[4 * k:4 * k + 4, 0:C], T.xs3[32 * k:32 * k + 4, 0:C])])
 
-    def results(h, p, e):
-        key, bank = "xq3%d" % h, "pb%d" % h
-        op("t", ["qv", key], [bank], lambda: g.tensor.matmul_mx(T.pb[:, 512 * h:512 * h + e - p], T.qv[:, 0:128], T.sv[:, 0:128], T.xq3[:, p:e], T.xs3[:, p:e], True, True))
-        load("y", "l_oc%d" % h, [key], [], [(T.oc[:, 4 * p:4 * e], T.xq3[:, p:e].bitcast(dt.uint8))])
-        op("s", [bank], ["ysb%d" % h], lambda: S.activation(T.ysb[:, p:e], T.pb[:, 512 * h:512 * h + e - p], COPY))
-        load("y", "l_y%d" % h, ["ysb%d" % h], [], [(T.y[:, p:e], T.ysb[:, p:e])])
-        load("s", "l_osc%d" % h, [key], [], [(T.osc[4 * k:4 * k + 4, p:e], T.xs3[32 * k:32 * k + 4, p:e]) for k in range(4)])
-
-    ch = chain(1, o_u, o_f, TV1)
-    if not LATE:
-        next(ch)
-    op("v", ["uoi"], ["uo"], lambda: V.tensor_copy(T.uo[:], T.uoi[:]))
-    op("v", ["ut"], ["qu"], lambda: V.quantize_mx(T.qu[:, 0:128], T.su[:, 0:128], T.ut[:, 0:512]))
-    op("v", ["qu", "uo"], ["qur"], lambda: V.tensor_copy(T.qur[:, 0:128].bitcast(dt.uint32), T.qu[:, 0:128].bitcast(dt.uint32).indirect(T.uo[:, 0:8])))
-    for b in range(4):
-        op("v", ["eye"], ["qe%d" % b], lambda: V.quantize_mx(T.qe[:, 128 * b:128 * b + 128], T.se[:, 128 * b:128 * b + 128], T.eye[:, 3 - b:515 - b]))
-    if LATE:
-        if LATE > 1:
-            op("v", ["xt0"], ["xq0"], lambda: V.quantize_mx(T.xq0[:, 0:C], T.xs0[:, 0:C], T.xt0[:, 0:4 * C]))
-        next(ch)
-    next(ch)
-    next(ch)
-    op("s", ["rti"], ["rst"], lambda: S.activation(T.rst[:], T.rti[:], ActivationFunctionType.Sign))
-    op("s", ["qu", "uo"], ["sur"], lambda: S.activation(T.sur[:, 0:128], T.su[:, 0:128].indirect(T.uo[:, 0:8]), COPY))
-    if LATE < 2:
-        op("v", ["xt0"], ["xq0"], lambda: V.quantize_mx(T.xq0[:, 0:C], T.xs0[:, 0:C], T.xt0[:, 0:4 * C]))
-    unpack_products(0)
-    for fs in F1:
-        next(ch)
-        for b in fs:
-            f_copy(b)
-    next(ch)
-    scores(o_u)
-    f_copy(3)
-    next(ch)
-    next(ch)
-
+    o, back, own = first_orders()
+    first_state()
+    first = {}
+    ahead_of_cycles()
     for n in (1, 2, 3):
-        o_u, o_f = choose(o_f)
-        back = means(n, o_u)
-        if n < 3:
-            ch = chain(n + 1, o_u, o_f, TV2)
-            for _ in range(PRE):
-                next(ch)
-            new_state_between(n, back)
-            next(ch)
-            unpack_products(n)
-            for fs in F2[0]:
-                next(ch)
-                for b in fs:
-                    f_copy(b)
-            scores(o_u)
-            for fs in F2[1]:
-                for b in fs:
-                    f_copy(b)
-                next(ch)
-        else:
-            op("s", ["iotf", tok(o_u)], ["osp"], lambda: S.activation(T.osp[:], by("iotf", o_u), COPY))
-            load("y", "l_fo", ["osp"], ["fo"], [(T.fo[:, 0:C], T.osp[0:128:16, 0:C])])
-            op("v", ["vt"], ["qv"], lambda: V.quantize_mx(T.qv[:, 0:128], T.sv[:, 0:128], T.vt[:, 0:512]))
-            new_state(n, back)
+        delta, base = apart(n, own)
+        low = cycles_of_four(n) if n in BOTH else cycles(n)
+        if n > 1:
+            new_state(n - 1, back)
+        unpack(n - 1, o)
+        dm, dd, own = new("ls"), new("ls"), pair()
+        gather("dm", dm, "so", low)
+        o = mix(["ds", "t", "nf", "nu"], dm, delta[0], base[0], own[0])
+        phase[0] = n + 1
+        if n < len(STEP):
+            hand_on(n + 1, o=o)
+        sums(n, o)
+        gather("dd", dd, dm, back)
+        back = mix(["es", "et", "ef", "eu"], dd, delta[1], base[1], own[1])
+        if n < len(STEP):
+            gather("bk", "bk%d" % n, "iots", back)
+            hand_on(n + 1, own=own)
+        means(n, o, [(0, C)] if n < len(STEP) else LAST)
+    last_state(len(STEP), back, o)
 
-    for sem in sorted(totals):
-        if seen["g"].get(sem, 0) < totals[sem]:
-            g.wait_ge(T.sem[sem], totals[sem])
+    order = {q: ["%d:%s" % (n, name) for n in LIKE for name in PLAN[q][LIKE[n]].split()] for q in queues}
+    order = {q: [name for name in order[q] if name in calls] for q in queues}
+    assert sorted(sum(order.values(), [])) == sorted(calls), set(calls) ^ set(sum(order.values(), []))
+    issue(order)

@@ -11,37 +11,55 @@ ENDS = [(0, 320), (320, C)]
 RADIX = {n: [2, 3, 3, 3, 3, 3] for n in (1, 2, 3)}
 APART = {2: "h2 h3", 3: "h2 h3", 4: "h20 h30 h21 h31"}
 SHARED = {1: (), 2: (), 3: (3,)}
-SPLIT = {1: "dm", 2: "dm", 3: "dm", 4: ""}
-BEHIND = ""
-BOTH = ()
-
-
-def line(head, stage, last, tail, behind):
-    moved = " ".join(behind.values()).split()
-    names = [k.replace("#", str(j)) for j in range(1, last + 1) for k in stage.split()]
-    return " ".join([head] + [name + " " + behind.get(name, "") for name in names if name not in moved] + [tail])
-
+ADDED = {1: (), 2: (), 3: ()}
+FAR = ()
+SCAN = (2, 3)
+SPLIT = {1: "dm k p0", 2: "dm", 3: "dm", 4: ""}
 
 PLAN = {
-    "v": {1: line("ones md idx e1 bia0 iots uo e0 ou d0 inv d1 eye d2 qu e1q mid d3 e2q e0q d4 e3q d5 qx bia1 ka kb ia m ib of ic", "a# b# l# l#'", 5, "la lb dm> base ds t nf nu",
-                  {"b1": "qur", "b2": "w2", "a3": "w3", "b3": "delta", "l3": "less", "b4": "w4", "a5": "w5"}),
-          2: line("u2 es u1 et ef eu u3 u0 k ka kb w1 qz m", "a# b# l# l#'", 5, "la lb dm> ds t nf nu",
-                  {"l1'": "delta", "a2": "less", "b2": "base", "l2'": "r0", "b3": "x0", "l3": "x1", "a4": "x2", "b4": "x3 qx", "l4": "a5", "b5": "w5"}),
-          4: "u2 u1 u0 u3 z30 qz0 z01 qz1 es et ef qv eu r10 r20 r00 r11 x10 r31 x11 r21 x00 x30 x20 qx0 x21 x01 x31 qx1 y1"},
-    "s": {1: line("sur k p0 w1", "p# p#'", 4, "f2 sc so dm<", {"p1'": "f0", "p2'": "f3", "p3'": "f1"}),
-          2: line("dd z2 z1 bk z3 z0 p0", "p# p#'", 4, "f2 f1 sc f0 so dm< f3", {"p1'": "w2", "p2": "r3", "p2'": "r1", "p3": "r2", "p3'": "h2 h3"}),
-          4: "dd g3 z20 z10 z00 z21 z11 z31 osp r30 r01 h30 h20 h21 h31 y0 yo1"},
-    "g": {1: "mdi one uoi send_o send_b", 2: "send_o send_b send_z w3 w4", 4: "send_z0 send_z1"},
-    "t": {1: "mf0 mf3 mf1 mf2 ms", 2: "mr3 mr0 mr1 mr2 mf2 mf1 ms mf0 mf3", 4: "mr10 mr20 mr00 mr11 mr30 mr31 mr01 mr21 my0 my1"},
-    "y": {1: "od u x wc v ws fd0 fd3 fd1 fd2", 2: "fd2 fd1 fd0 fd3", 4: "fo oc0 yo0 oc1 o0 o1 o2 o3"},
+    1: {"v": "ones idx md eye e1 iots e2q e0 uo ou d0 inv e3q d4 of e0q bia0 mid d5 bia1 qu qur qx ia e1q ib ic k> ka kb m p0> a1 b1 l1 l1' a2 b2 w2 l2 l2' a3 w3 b3 delta l3 l3' a4 b4 w4 l4 l4' a5 w5 b5 l5 l5' la lb dm> base ds t nf nu",
+        "s": "d1 d2 d3 sur f3 k< p0< w1 p1 p1' f0 p2 p2' p3 p3' f1 p4 p4' f2 sc less so dm<",
+        "g": "one uoi mdi send_o send_b",
+        "t": "mf3 ms mf0 mf1 mf2",
+        "y": "od u x ws wc v fd3 fd0 fd1 fd2"},
+    2: {"v": "u2 es u1 et ef eu u3 u0 k ka kb m1 qz m a1 b1 l1 l1' delta a2 less b2 base l2 l2' r0 a3 b3 x0 l3 x1 l3' a4 x2 b4 x3 qx l4 a5 l4' b5 w5 l5 l5' la lb dm> ds t nf nu",
+        "s": "dd z2 z1 bk z3 z0 p0 p1 p1' w2 p2 r3 p2' r1 p3 r2 p3' h2 h3 p4 p4' f2 f1 sc f0 so dm< f3",
+        "g": "send_o send_b send_z w3 w4",
+        "t": "mr3 mr0 mr1 mr2 mf2 mf1 ms mf0 mf3",
+        "y": "fd2 fd1 fd0 fd3"},
+    4: {"v": "u2 u1 u0 u3 z30 qz0 z01 qz1 es et ef qv eu r10 r20 r00 r11 x10 r31 x11 r21 x00 x30 x20 qx0 x21 x01 x31 qx1 y1",
+        "s": "dd g3 z20 z10 z00 z21 z11 z31 osp r30 r01 h30 h20 h21 h31 y0 o2 o3 yo1",
+        "g": "send_z0 send_z1",
+        "t": "mr10 mr20 mr00 mr11 mr30 mr31 mr01 mr21 my0 my1",
+        "y": "fo oc0 yo0 oc1 o0 o1"},
 }
-LIKE = {1: 1, 2: 2, 3: 2, 4: 4}
-ON_VECTOR = {n: PLAN["v"][LIKE[n]] for n in LIKE}
-BY_DMA = {n: PLAN["y"][LIKE[n]] for n in LIKE}
-STORES = {name: q for q in "sy" for name in PLAN[q][4].split()}
-TWIN = {n: "-" + "".join(q for j in range(1, len(RADIX[n])) for q in "vsg" if "w%d" % j in PLAN[q][LIKE[n]].split()) for n in RADIX}
+PLAN = {
+    1: {"v": "ones md uo bia0 iots e0 e1 bia1 d0 ou of inv d5 qx k< qu ka m kb ia p0> a1 b1 ib l1 ic l1' e1q a2 b2 qur l2 e0q l2' a3 e2q b3 e3q delta l3 mid l3' a4 b4 w4 l4 l4' a5 w5 b5 l5 l5' la lb dm> ds base t",
+        "s": "d1 d2 d3 d4 k> p0< sur p1 p1' w2 p2 p2' w3 p3 p3' f1 less p4 p4' f3 f0 sc so f2 dm<",
+        "g": "mdi uoi send_o eye w1 send_b",
+        "t": "mf2 mf0 mf3 mf1 ms",
+        "y": "od x u fd1 wc ws v fd3 fd0 fd2"},
+    2: {"v": "es -nf et -nu ef eu u1 u0 u3 ka m kb u2 m1 a1 b1 l1 qz l1' a2 b2 delta l2 l2' a3 r2 b3 x1 l3 x0 l3' x3 a4 x2 b4 qx l4 l4' p4' a5 b5 l5 l5' la lb dm< less ds base t",
+        "s": "dd bk k z1 z3 p0 z0 z2 p1 p1' w2 p2 p2' r1 r3 r0 p3 h3 p3' h2 w4 p4 f1 sc f3 f2 so f0 dm>",
+        "g": "send_o send_b send_z w3 w5",
+        "t": "mr1 mr2 mr3 mr0 mf1 ms mf3 mf0 mf2",
+        "y": "fd1 fd3 fd2 fd0"},
+    3: {"v": "es -nf et -nu ef eu u1 u2 u0 ka delta kb m u3 a1 m1 b1 l1 qz l1' a2 w2 b2 l2 l2' r2 a3 x0 b3 x1 l3 x2 l3' x3 a4 b4 qx l4 l4' a5 w5 b5 l5 l5' la lb dm< base ds t nf nu f2",
+        "s": "dd bk k z1 z2 p0 z0 z3 p1 p1' less p2 p2' r0 r1 r3 h2 p3 h3 p3' w4 p4 p4' sc fe0 so f0 f1 dm> fe1",
+        "g": "send_o send_b send_z w3 send_x",
+        "t": "mr0 mr2 mr1 mr3 ms mf2 mf1 mf0 mg3 mg0 mg1 mg2 mf3",
+        "y": "fd0 fd1"},
+    4: {"v": "es et u0 u1 u2 u3 z10 z21 qz0 ef qv eu qz1 r00 r20 r31 x10 x11 x01 x30 x00 x21 x31 x20 qx1 qx0 y0",
+        "s": "dd -f3 osp g2 g3 z01 z00 z20 z30 z11 z31 r30 r10 r11 r01 h30 r21 h31 h21 h20 y1 o2 yo1 o3",
+        "g": "send_n",
+        "t": "mr30 mr00 mr10 mr20 mr11 mr31 mr01 mr21 my1 my0",
+        "y": "fo oc1 oc0 o0 o1 yo0"},
+}
+LIKE = {1: 1, 2: 2, 3: 3, 4: 4}
+FAR = (3,)
+SHARED = {1: (), 2: (), 3: (2, 3)}
 
-LISTS = 36
+LISTS = 100
 SCRATCH = {
     "md": ("sbuf", [128, 16], "int32"), "ee": ("sbuf", [128, 32], "float32"), "d0": ("sbuf", [128, C], "bfloat16"),
     "iots": ("sbuf", [128, C], "bfloat16"), "ones": ("sbuf", [128, 516], "bfloat16"),
@@ -57,13 +75,14 @@ SCRATCH = {
     "sc": ("sbuf", [128, C], "bfloat16"), "so": ("sbuf", [128, C], "bfloat16"),
     "zt": ("sbuf", [128, 4 * C], "bfloat16"), "xt": ("sbuf", [128, 4 * C], "bfloat16"),
     "ysb": ("sbuf", [128, C], "float32"), "osp": ("sbuf", [128, C], "float32"),
-    "ls": ("sbuf", [128, C * LISTS], "bfloat16"), "hs": ("sbuf", [128, C * 14], "float16"),
+    "ls": ("sbuf", [128, C * LISTS], "bfloat16"), "hs": ("sbuf", [128, C * 40], "float16"),
     "tu": ("sbuf", [128, K * 48], "uint16"), "tf": ("sbuf", [128, K * 48], "float32"),
     "pa": ("psum", [128, 2048], "float32"), "pb": ("psum", [128, 2048], "float32"),
 }
 for _b in range(4):
     SCRATCH["f%d" % _b] = ("sbuf", [128, C], "bfloat16")
     SCRATCH["fd%d" % _b] = ("sbuf", [128, C], "bfloat16")
+    SCRATCH["fe%d" % _b] = ("sbuf", [128, C], "bfloat16")
     SCRATCH["u%d" % _b] = ("sbuf", [128, C], "float32")
     SCRATCH["gg%d" % _b] = ("sbuf", [128, C], "bfloat16")
     SCRATCH["r%d" % _b] = ("sbuf", [128, C], "float32")
@@ -74,17 +93,15 @@ for _n in (1, 2, 3):
     SCRATCH["bk%d" % (_n - 1)] = ("sbuf", [128, C], "bfloat16")
     SCRATCH["ol%d" % _n] = ("sbuf", [128, K], "uint16")
     SCRATCH["bl%d" % _n] = ("sbuf", [128, 2 * K], "float32")
-    SCRATCH["ll%d" % _n] = ("sbuf", [128, K], "uint16")
-    SCRATCH["tw%d0" % _n] = ("sbuf", [128, C], "bfloat16")
-    SCRATCH["tw%d1" % _n] = ("sbuf", [128, C], "bfloat16")
+    SCRATCH["on%d" % _n] = ("sbuf", [128, K], "uint16")
     SCRATCH["zq%d" % _n] = ("sbuf", [128, C], "float8_e4m3fn_x4")
     SCRATCH["zs%d" % _n] = ("sbuf", [128, C], "uint8")
     SCRATCH["zl%d" % _n] = ("sbuf", [128, C], "float8_e4m3fn_x4")
     SCRATCH["zp%d" % _n] = ("sbuf", [128, C], "uint8")
 
 SEMAPHORES = ["cv", "cs", "ct", "cg", "sent"] \
-    + ["a_z10", "a_z20", "a_z30", "a_z31", "a_z32"] + ["a_%s%d" % (k, n) for k in "obl" for n in (1, 2, 3)] \
-    + ["l_" + n for n in ("od", "x", "u", "v", "wc", "ws", "y0", "y1", "fo", "oc0", "oc1", "osc0", "osc1", "osc2", "osc3", "f0", "f1", "f2", "f3")]
+    + ["a_z10", "a_z20", "a_z30", "a_z31", "a_z32"] + ["a_%s%d" % (k, n) for k in "obn" for n in (1, 2, 3)] + ["g_u%d" % b for b in range(4)] \
+    + ["l_" + n for n in ("od", "x", "u", "v", "wc", "ws", "y0", "y1", "y2", "fo", "oc0", "oc1", "oc2", "osc0", "osc1", "osc2", "osc3", "f0", "f1", "f2", "f3")]
 
 ADD, MUL, SUB, MIN, MAX = AluOpType.add, AluOpType.mult, AluOpType.subtract, AluOpType.min, AluOpType.max
 COPY = ActivationFunctionType.Copy
@@ -100,7 +117,7 @@ def rank_program(g, core, T, topo):
     calls, wrote, read = {}, {}, {}
     phase = [1]
 
-    def record(name, q, kind, reads, writes, what):
+    def record(name, kind, reads, writes, what):
         name = "%d:%s" % (phase[0], name)
         after = set()
         for k in reads:
@@ -112,16 +129,16 @@ def rank_program(g, core, T, topo):
             read.setdefault(k, []).append(name)
         for k in writes:
             wrote[k], read[k] = [name], []
-        calls[name] = {"q": q, "kind": kind, "after": after, "what": what}
+        calls[name] = {"kind": kind, "after": after, "what": what}
 
-    def op(name, q, reads, writes, call):
-        record(name, q, "op", reads, writes, call)
+    def op(name, reads, writes, **forms):
+        record(name, "op", reads, writes, forms)
 
-    def load(name, q, sem, reads, writes, pairs):
-        record(name, q, "load", reads, writes, (sem, pairs))
+    def load(name, sem, reads, writes, pairs):
+        record(name, "load", reads, writes, (sem, pairs))
 
     def send(name, step, pairs, key, sem, lands, few=None):
-        record(name, "g", "send", key, [lands], (step, pairs, sem, few))
+        record(name, "send", key, [lands], (step, pairs, sem, few))
 
     def issue(order):
         count, totals, token, snap = {q: 0 for q in queues}, {}, {}, {}
@@ -135,9 +152,9 @@ def rank_program(g, core, T, topo):
                 for a, b in snap.get((sem, val), {}).items():
                     seen[q][a] = max(seen[q].get(a, 0), b)
 
-        def emit(name):
+        def emit(q, name):
             c = calls[name]
-            q, need = c["q"], {}
+            need = {}
             for a in c["after"]:
                 sem, val = token[a]
                 need[sem] = max(need.get(sem, 0), val)
@@ -146,12 +163,12 @@ def rank_program(g, core, T, topo):
             if c["kind"] == "op":
                 count[q] += 1
                 sem = "c" + q
-                c["what"]().then_inc(T.sem[sem], 1)
+                c["what"][q]().then_inc(T.sem[sem], 1)
                 totals[sem] = count[q]
             elif c["kind"] == "load":
                 sem, pairs = c["what"]
                 for out, in_ in pairs:
-                    queues[q].dma_start(out, in_).then_inc(T.sem[sem], 16)
+                    (g.dma_start(out, in_, accum_op=ADD) if q == "g" else queues[q].dma_start(out, in_)).then_inc(T.sem[sem], 16)
                     totals[sem] = totals.get(sem, 0) + 16
             else:
                 step, pairs, sem, few = c["what"]
@@ -172,7 +189,7 @@ def rank_program(g, core, T, topo):
             before = left
             for q in queues:
                 while heads[q] < len(order[q]) and all(a in token for a in calls[order[q][heads[q]]]["after"]):
-                    emit(order[q][heads[q]])
+                    emit(q, order[q][heads[q]])
                     heads[q] += 1
                     left -= 1
             assert left < before, [order[q][heads[q]] for q in queues if heads[q] < len(order[q])]
@@ -181,33 +198,28 @@ def rank_program(g, core, T, topo):
 
     used = {"tu": 0, "tf": 0, "ls": 0, "hs": 0}
     width = {"tu": K, "tf": K, "ls": C, "hs": C}
-    ring = {"tu": 48, "tf": 48, "ls": LISTS, "hs": 14}
 
     def new(kind):
         used[kind] += 1
-        return "%s.%d" % (kind, (used[kind] - 1) % ring[kind])
+        return "%s.%d" % (kind, used[kind] - 1)
 
     def pair():
         used["tf"] += used["tf"] % 2
         return [new("tf"), new("tf")]
 
-    def ap(key, a=0, b=None, step=1, part=slice(0, 128)):
+    def ap(key, a=0, b=None, step=1):
         if "." in key:
             kind, i = key.split(".")
             w = width[kind]
-            return T[kind][part, w * int(i) + a:w * int(i) + (w if b is None else b):step]
-        return T[key][part, a:(C if b is None else b):step]
+            return T[kind][:, w * int(i) + a:w * int(i) + (w if b is None else b):step]
+        return T[key][:, a:(C if b is None else b):step]
 
     def by(key, table, p=0, e=C):
         return ap(key).indirect(ap(table, p // 16, e // 16))
 
     def move(name, reads, writes, out, in_, scale=None):
-        if name not in ON_VECTOR[phase[0]].split():
-            op(name, "s", reads, writes, lambda: S.activation(out, in_, COPY, scale=1.0 if scale is None else scale))
-        elif scale is None:
-            op(name, "v", reads, writes, lambda: V.tensor_copy(out, in_))
-        else:
-            op(name, "v", reads, writes, lambda: V.tensor_scalar(out, in_, scale, None, MUL))
+        op(name, reads, writes, s=lambda: S.activation(out, in_, COPY) if scale is None else S.activation(out, in_, COPY, scale=scale),
+           v=lambda: V.tensor_copy(out, in_) if scale is None else V.tensor_scalar(out, in_, scale, None, MUL))
 
     def gather(name, out, key, table):
         if name not in SPLIT[phase[0]].split():
@@ -219,46 +231,48 @@ def rank_program(g, core, T, topo):
         move(name + ">", [key, table], [out], ap(out, MID, C), by(key, table, MID, C))
         wrote[out] = first + wrote[out]
 
-    def scan(name, key, part=slice(0, 128)):
+    def scan(name, key):
         h = new("hs")
-        op(name, "v", [key, "d0"], [h], lambda: V.tensor_tensor_scan(ap(h, 0, C, 1, part), T.d0[part, 0:C], ap(key, 0, C, 1, part), 0.0, ADD, MAX))
+        op(name, [key, "d0"], [h], v=lambda: V.tensor_tensor_scan(ap(h), T.d0[:, 0:C], ap(key), 0.0, ADD, MAX))
         return h
 
     def conv(a, b, key):
         h, t = scan(a, key), new("tu")
-        op(b, "v", [h, "bia"], [t], lambda: V.tensor_scalar(ap(t), ap(h, 15, C, 16), T.bia[:, 1:2], None, ADD))
+        op(b, [h, "bia"], [t], v=lambda: V.tensor_scalar(ap(t), ap(h, 15, C, 16), T.bia[:, 1:2], None, ADD))
         return t
 
-    load("od", "y", "l_od", [], ["odl"], [(T.odl[:], T.od[:])])
-    op("mdi", "g", [], ["md"], lambda: g.iota(T.md[:], [[1, 16]], 128, -1))
-    op("one", "g", [], ["one"], lambda: g.iota(T.bia[:, 3:4], [[1, 1]], 3, 4, allow_small_or_imprecise_dtypes=True))
-    op("uoi", "g", [], ["uoi"], lambda: g.iota(T.uoi[:], [[16, 8]], 0, 0))
-    op("ones", "v", [], ["ones"], lambda: V.memset(T.ones[:], 1.0))
-    op("idx", "v", ["ones"], ["idx"], lambda: V.tensor_tensor_scan(T.idx[:], T.ones[:], T.ones[:], -1.0, ADD, MUL))
-    op("iots", "v", ["idx"], ["iots"], lambda: V.tensor_scalar(T.iots[:], T.idx[:, 0:C], float(-MID), None, ADD))
-    op("eye", "v", ["idx", "one"], ["eye"], lambda: V.tensor_scalar(T.eye[:], T.idx[:], T.bia[:, 3:4], None, AluOpType.is_equal))
-    op("md", "v", ["md"], ["md"], lambda: V.tensor_scalar(T.md[:], T.md[:], 15, None, AluOpType.bitwise_and))
-    op("e0", "v", ["md"], ["e0"], lambda: V.tensor_scalar(T.ee[:, 0:16], T.md[:], 0.0, -2 * UP, AluOpType.is_equal, MUL))
-    op("e1", "v", ["md"], ["e1"], lambda: V.tensor_scalar(T.ee[:, 16:32], T.md[:], 1.0, UP, AluOpType.is_equal, MUL))
-    op("d0", "v", ["e0", "e1"], ["d0"], lambda: V.tensor_tensor(T.d0[:, 0:16], T.ee[:, 0:16], T.ee[:, 16:32], ADD))
+    def gathered(n, b):
+        tags = ["h%d" % b] if n < len(STEP) else ["h%d%d" % (b, h) for h in range(len(ENDS))]
+        return [tag in APART[n + 1].split() for tag in tags]
+
+    load("od", "l_od", [], ["odl"], [(T.odl[:], T.od[:])])
+    op("mdi", [], ["md"], g=lambda: g.iota(T.md[:], [[1, 16]], 128, -1))
+    op("uoi", [], ["uoi"], g=lambda: g.iota(T.uoi[:], [[16, 8]], 0, 0))
+    op("ones", [], ["ones"], v=lambda: V.memset(T.ones[:], 1.0))
+    op("iots", ["ones"], ["iots"], v=lambda: V.tensor_tensor_scan(T.iots[:], T.ones[:, 0:C], T.ones[:, 0:C], -MID - 1.0, ADD, MUL))
+    op("eye", ["ones"], ["eye"], g=lambda: g.affine_select(T.eye[:], T.ones[:], [[-1, 516]], AluOpType.is_equal, 0.0, 3, 4))
+    op("md", ["md"], ["md"], v=lambda: V.tensor_scalar(T.md[:], T.md[:], 15, None, AluOpType.bitwise_and))
+    op("e0", ["md"], ["e0"], v=lambda: V.tensor_scalar(T.ee[:, 0:16], T.md[:], 0.0, -2 * UP, AluOpType.is_equal, MUL))
+    op("e1", ["md"], ["e1"], v=lambda: V.tensor_scalar(T.ee[:, 16:32], T.md[:], 1.0, UP, AluOpType.is_equal, MUL))
+    op("d0", ["e0", "e1"], ["d0"], v=lambda: V.tensor_tensor(T.d0[:, 0:16], T.ee[:, 0:16], T.ee[:, 16:32], ADD))
     for i in range(5):
         w = 16 << i
-        op("d%d" % (i + 1), "v", ["d0"], ["d0"], lambda w=w: V.tensor_copy(T.d0[:, w:min(2 * w, C)], T.d0[:, 0:min(w, C - w)]))
-    op("bia0", "v", ["md"], ["bia0"], lambda: V.tensor_scalar(T.bia[:, 0:1], T.md[:, 15:16], 0.0, -UP, AluOpType.not_equal, MUL))
-    op("bia1", "v", ["bia0"], ["bia"], lambda: V.tensor_scalar(T.bia[:, 1:2], T.bia[:, 0:1], float(MID), None, ADD))
-    op("mid", "v", [], ["mid"], lambda: V.memset(T.bia[:, 2:3], float(MID)))
-    op("uo", "v", ["uoi"], ["uo"], lambda: V.tensor_copy(T.uo[:], T.uoi[:]))
+        move("d%d" % (i + 1), ["d0"], ["d0"], T.d0[:, w:min(2 * w, C)], T.d0[:, 0:min(w, C - w)])
+    op("bia0", ["md"], ["bia0"], v=lambda: V.tensor_scalar(T.bia[:, 0:1], T.md[:, 15:16], 0.0, -UP, AluOpType.not_equal, MUL))
+    op("bia1", ["bia0"], ["bia"], v=lambda: V.tensor_scalar(T.bia[:, 1:2], T.bia[:, 0:1], float(MID), None, ADD))
+    op("mid", [], ["mid"], v=lambda: V.memset(T.bia[:, 2:3], float(MID)))
+    op("uo", ["uoi"], ["uo"], v=lambda: V.tensor_copy(T.uo[:], T.uoi[:]))
     for b in range(4):
-        op("e%dq" % b, "v", ["eye"], ["qe%d" % b], lambda b=b: V.quantize_mx(T.qe[:, 128 * b:128 * b + 128], T.se[:, 128 * b:128 * b + 128], T.eye[:, 3 - b:515 - b]))
+        op("e%dq" % b, ["eye"], ["qe%d" % b], v=lambda b=b: V.quantize_mx(T.qe[:, 128 * b:128 * b + 128], T.se[:, 128 * b:128 * b + 128], T.eye[:, 3 - b:515 - b]))
 
     def first_state():
         for name, key, out, in_ in (("u", "ut", T.ut[:], T.u[:]), ("x", "xt0", T.xt0[:], T.x[:]), ("v", "vt", T.vt[:], T.v[:]),
                                     ("wc", "wq", T.wq[:, 0:512].bitcast(dt.uint8), T.wc[:, 0:2048]), ("ws", "wp", T.wp[:, 0:512], T.ws[:, 0:512])):
-            load(name, "y", "l_" + name, ["ol1"] if name in BEHIND.split() else [], [key], [(out, in_)])
-        op("qu", "v", ["ut"], ["qu"], lambda: V.quantize_mx(T.qu[:, 0:128], T.su[:, 0:128], T.ut[:, 0:512]))
-        op("qur", "v", ["qu", "uo"], ["qur"], lambda: V.tensor_copy(T.qur[:, 0:128].bitcast(dt.uint32), T.qu[:, 0:128].bitcast(dt.uint32).indirect(T.uo[:, 0:8])))
-        op("sur", "s", ["qu", "uo"], ["sur"], lambda: S.activation(T.sur[:, 0:128], T.su[:, 0:128].indirect(T.uo[:, 0:8]), COPY))
-        op("qx", "v", ["xt0"], ["xq0"], lambda: V.quantize_mx(T.xq0[:, 0:C], T.xs0[:, 0:C], T.xt0[:, 0:4 * C]))
+            load(name, "l_" + name, [], [key], [(out, in_)])
+        op("qu", ["ut"], ["qu"], v=lambda: V.quantize_mx(T.qu[:, 0:128], T.su[:, 0:128], T.ut[:, 0:512]))
+        op("qur", ["qu", "uo"], ["qur"], v=lambda: V.tensor_copy(T.qur[:, 0:128].bitcast(dt.uint32), T.qu[:, 0:128].bitcast(dt.uint32).indirect(T.uo[:, 0:8])))
+        move("sur", ["qu", "uo"], ["sur"], T.sur[:, 0:128], T.su[:, 0:128].indirect(T.uo[:, 0:8]))
+        op("qx", ["xt0"], ["xq0"], v=lambda: V.quantize_mx(T.xq0[:, 0:C], T.xs0[:, 0:C], T.xt0[:, 0:4 * C]))
 
     def hand_on(n, o=None, own=None):
         if o is not None:
@@ -268,20 +282,21 @@ def rank_program(g, core, T, topo):
 
     def first_orders():
         o, own = new("tu"), pair()
-        op("ou", "v", ["odl"], [o], lambda: V.tensor_copy(ap(o), T.odl[:]))
+        op("ou", ["odl"], [o], v=lambda: V.tensor_copy(ap(o), T.odl[:]))
         hand_on(1, o=o)
-        op("of", "v", ["odl"], [own[0]], lambda: V.tensor_copy(ap(own[0]), T.odl[:]))
-        op("inv", "v", ["iots", o], ["bk0"], lambda: V.tensor_copy(by("bk0", o), T.iots[:]))
+        op("of", ["odl"], [own[0]], v=lambda: V.tensor_copy(ap(own[0]), T.odl[:]))
+        op("inv", ["iots", o], ["bk0"], v=lambda: V.tensor_copy(by("bk0", o), T.iots[:]))
         back = conv("ia", "ib", "bk0")
-        op("ic", "v", [back], [own[1]], lambda: V.tensor_copy(ap(own[1]), ap(back)))
+        op("ic", [back], [own[1]], v=lambda: V.tensor_copy(ap(own[1]), ap(back)))
         hand_on(1, own=own)
         return o, back, own
 
     def apart(n, own):
         delta, less, base = pair(), pair(), pair()
-        op("delta", "v", ["bl%d" % n] + own, delta, lambda: V.tensor_tensor(ap(delta[0], 0, 2 * K), T["bl%d" % n][:], ap(own[0], 0, 2 * K), SUB))
-        op("less", "v", delta + ["bia0"], less, lambda: V.tensor_scalar(ap(less[0], 0, 2 * K), ap(delta[0], 0, 2 * K), T.bia[:, 0:1], None, MUL))
-        op("base", "v", less + own, base, lambda: V.tensor_tensor(ap(base[0], 0, 2 * K), ap(less[0], 0, 2 * K), ap(own[0], 0, 2 * K), ADD))
+        op("delta", ["bl%d" % n] + own, delta, v=lambda: V.tensor_tensor(ap(delta[0], 0, 2 * K), T["bl%d" % n][:], ap(own[0], 0, 2 * K), SUB))
+        op("less", delta + ["bia0"], less, v=lambda: V.tensor_scalar(ap(less[0], 0, 2 * K), ap(delta[0], 0, 2 * K), T.bia[:, 0:1], None, MUL),
+           s=lambda: S.activation(ap(less[0], 0, 2 * K), ap(delta[0], 0, 2 * K), COPY, scale=T.bia[:, 0:1]))
+        op("base", less + own, base, v=lambda: V.tensor_tensor(ap(base[0], 0, 2 * K), ap(less[0], 0, 2 * K), ap(own[0], 0, 2 * K), ADD))
         return delta, base
 
     def cycles(n):
@@ -290,29 +305,25 @@ def rank_program(g, core, T, topo):
         a = conv("ka", "kb", k)
 
         def least(name, out):
-            op(name, "v", ["iots", k], [out], lambda: V.tensor_tensor_scan(ap(out), T.iots[:], ap(k), -UP, MAX, MIN))
+            op(name, ["iots", k], [out], v=lambda: V.tensor_tensor_scan(ap(out), T.iots[:], ap(k), -UP, MAX, MIN))
 
         least("m", m)
         low, power = m, k
         radix = RADIX[n]
         for j, r in enumerate(radix):
-            acc = k
             if j > 0:
                 a = conv("a%d" % j, "b%d" % j, power)
-                acc, q = new("ls"), TWIN[n][j]
-                if low == m and q == "v":
-                    least("w%d" % j, acc)
-                elif q == "v":
-                    op("w%d" % j, "v", [low], [acc], lambda acc=acc, low=low: V.tensor_copy(ap(acc), ap(low)))
-                elif q == "s":
-                    op("w%d" % j, "s", [low], [acc], lambda acc=acc, low=low: S.activation(ap(acc), ap(low), COPY))
+                acc = new("ls")
+                if j == 1 and n in SCAN:
+                    least("m1", acc)
                 else:
-                    op("w%d" % j, "g", [low], [acc], lambda acc=acc, low=low: g.affine_select(ap(acc), ap(low), [[0, C]], AluOpType.is_equal, 0.0, 0, 0))
-            for e in range(r - 1 if j > 0 else r - 2):
-                out = new("ls")
-                op("l%d%s" % (j, "'" * e), "v", [acc, low, a], [out], lambda out=out, acc=acc, low=low, a=a: V.tensor_tensor(ap(out), by(acc, a), ap(low), MIN))
-                acc = out
-            if j > 0 or r > 2:
+                    op("w%d" % j, [low], [acc], v=lambda acc=acc, low=low: V.tensor_copy(ap(acc), ap(low)),
+                       s=lambda acc=acc, low=low: S.activation(ap(acc), ap(low), COPY),
+                       g=lambda acc=acc, low=low: g.affine_select(ap(acc), ap(low), [[0, C]], AluOpType.is_equal, 0.0, 0, 0))
+                for e in range(r - 1):
+                    out = new("ls")
+                    op("l%d%s" % (j, "'" * e), [acc, low, a], [out], v=lambda out=out, acc=acc, low=low, a=a: V.tensor_tensor(ap(out), by(acc, a), ap(low), MIN))
+                    acc = out
                 low = acc
             if j < len(radix) - 1:
                 for e in range(r - 1):
@@ -321,92 +332,52 @@ def rank_program(g, core, T, topo):
                     power = out
         return conv("la", "lb", low)
 
-    def halves(n):
-        low, high = slice(0, 64), slice(64, 128)
-        return (low, high) if rank < rank ^ STEP[n - 1] else (high, low)
-
-    def ahead_of_cycles():
-        h = scan("ida", "iots") if BOTH else None
-        for n in BOTH:
-            first[n] = new("tu")
-            op("id%d" % n, "v", [h, "bia"], [first[n]], lambda n=n: V.tensor_scalar(ap(first[n]), ap(h, 15, C, 16), T.bia[:, 1:2], None, ADD))
-            for i in range(2):
-                name, out = "big%d%d" % (n, i), T["tw%d%d" % (n, i)][halves(n)[0], 0:C]
-                if name in ON_VECTOR[1].split():
-                    op(name, "v", [], [name], lambda out=out: V.memset(out, UP))
-                else:
-                    op(name, "g", [], [name], lambda out=out: g.iota(out, [[0, C]], int(UP), 0, allow_small_or_imprecise_dtypes=True))
-
-    def cycles_of_four(n):
-        H, L = halves(n)
-        k, w, a = new("ls"), new("ls"), first[n]
-
-        def table(name, h, out, part, src):
-            op(name, "v", [h, "bia", out], [out + str(part)], lambda: V.tensor_scalar(ap(out, 0, K, 1, part), ap(h, 15, C, 16, src), T.bia[src, 1:2], None, ADD))
-
-        def least(name, out, key):
-            op(name, "v", ["iots", k], [key], lambda: V.tensor_tensor_scan(ap(out, 0, C, 1, L), T.iots[H, 0:C], ap(k, 0, C, 1, H), -UP, MAX, MIN))
-
-        gather("k", k, "bk%d" % (n - 1), "ol%d" % n)
-        table("kb", scan("ka", k, H), a, H, H)
-        least("m", k, "m")
-        move("p0", [k, "m", a + str(H)], [w], ap(w), by(k, a))
-        for j, r in list(enumerate(RADIX[n]))[1:]:
-            h, a, twin, q = scan("a%d" % j, w, H), new("tu"), "tw%d%d" % (n, j % 2), TWIN[n][j]
-            table("b%d" % j, h, a, H, H)
-            table("c%d" % j, h, a, L, H)
-            out, in_ = T[twin][L, 0:C], ap(w, 0, C, 1, L)
-            if j == 1 and q == "v":
-                least("w1", twin, twin)
-            elif j == 1:
-                in_ = ap(k, 0, C, 1, L)
-            if q == "v" and j > 1:
-                op("w%d" % j, "v", [w], [twin], lambda out=out, in_=in_: V.tensor_copy(out, in_))
-            elif q == "s":
-                op("w%d" % j, "s", ["m" if j == 1 else w], [twin], lambda out=out, in_=in_: S.activation(out, in_, COPY))
-            elif q == "g":
-                op("w%d" % j, "g", ["m" if j == 1 else w], [twin], lambda out=out, in_=in_: g.affine_select(out, in_, [[0, C]], AluOpType.is_equal, 0.0, 0, 0))
-            for e in range(r - 1):
-                out = new("ls")
-                op("l%d%s" % (j, "'" * e), "v", [w, twin, "big%d%d" % (n, j % 2), a + str(H), a + str(L)], [out], lambda out=out, w=w, twin=twin, a=a: V.tensor_tensor(ap(out), by(w, a), T[twin][:], MIN))
-                w = out
-        h, lands = scan("la", w, L), "ll%d" % n
-        table("lb", h, a, H, L)
-        send("send_l", STEP[n - 1], [(T[lands][:], ap(a))], [a + str(H), a + str(L)], "a_l%d" % n, lands)
-        op("lc", "v", [h, "bia"], [lands], lambda: V.tensor_scalar(T[lands][H, 0:K], ap(h, 15, C, 16, L), T.bia[L, 1:2], None, ADD))
-        return lands
-
     def unpack(n, o):
         xq, xs = "xq%d" % n, "xs%d" % n
-        op("ms", "t", ["qur", "sur", xq], ["pb0"], lambda: g.tensor.matmul_mx(T.pb[:, 0:C], T.qur[:, 0:128], T.sur[:, 0:128], T[xq][:, 0:C], T[xs][:, 0:C], True, True))
+        op("ms", ["qur", "sur", xq], ["pb0"], t=lambda: g.tensor.matmul_mx(T.pb[:, 0:C], T.qur[:, 0:128], T.sur[:, 0:128], T[xq][:, 0:C], T[xs][:, 0:C], True, True))
+        op("sc", ["pb0"], ["sc"], s=lambda: S.activation(T.sc[:], T.pb[:, 0:C], ActivationFunctionType.Sign),
+           v=lambda: V.tensor_scalar(T.sc[:], T.pb[:, 0:C], 0.0, None, AluOpType.is_gt))
+        op("so", ["sc", o], ["so"], s=lambda: S.activation(T.so[:], by("sc", o), ActivationFunctionType.Relu),
+           v=lambda: V.tensor_scalar(T.so[:], by("sc", o), 0.0, None, MAX))
+
+        def planes(name, p, q, s):
+            for b in range(4):
+                op("%s%d" % (name, b), ["qe%d" % b, q], ["%s%d" % (p, b)], t=lambda b=b: g.tensor.matmul_mx(T[p][:, 512 * b:512 * b + C], T.qe[:, 128 * b:128 * b + 128], T.se[:, 128 * b:128 * b + 128], T[q][:, 0:C], T[s][:, 0:C], True, True))
+
+        planes("mf", "pa", xq, xs)
+        p = "pa"
+        if n + 1 in FAR:
+            p, zl, zp = "pb", "zl%d" % (n + 1), "zp%d" % (n + 1)
+            send("send_x", STEP[n], [(T[zl][:].bitcast(dt.uint8), T[xq][:].bitcast(dt.uint8)), (T[zp][:], T[xs][:])], [xq], "a_z%d0" % (n + 1), zl)
+            planes("mg", p, zl, zp)
+            for b in range(4):
+                if not all(gathered(n + 1, b)):
+                    move("fe%d" % b, ["pa%d" % b], ["fe%d" % b], T["fe%d" % b][:], T.pa[:, 512 * b:512 * b + C])
         for b in range(4):
-            op("mf%d" % b, "t", ["qe%d" % b, xq], ["pa%d" % b], lambda b=b: g.tensor.matmul_mx(T.pa[:, 512 * b:512 * b + C], T.qe[:, 128 * b:128 * b + 128], T.se[:, 128 * b:128 * b + 128], T[xq][:, 0:C], T[xs][:, 0:C], True, True))
-            move("f%d" % b, ["pa%d" % b], ["f%d" % b], T["f%d" % b][:], T.pa[:, 512 * b:512 * b + C])
-            if b in SHARED[n + 1]:
-                continue
-            if "fd%d" % b not in BY_DMA[phase[0]].split():
-                move("fd%d" % b, ["pa%d" % b], ["fd%d" % b], T["fd%d" % b][:], T.pa[:, 512 * b:512 * b + C])
-            else:
-                load("fd%d" % b, "y", "l_f%d" % b, ["f%d" % b], ["fd%d" % b], [(T["fd%d" % b][:], T["f%d" % b][:])])
-        op("sc", "s", ["pb0"], ["sc"], lambda: S.activation(T.sc[:], T.pb[:, 0:C], ActivationFunctionType.Sign))
-        op("so", "s", ["sc", o], ["so"], lambda: S.activation(T.so[:], by("sc", o), ActivationFunctionType.Relu))
+            move("f%d" % b, ["%s%d" % (p, b)], ["f%d" % b], T["f%d" % b][:], T[p][:, 512 * b:512 * b + C])
+            if b not in SHARED[n + 1] + ADDED[n + 1]:
+                load("fd%d" % b, "l_f%d" % b, ["f%d" % b], ["fd%d" % b], [(T["fd%d" % b][:], T["f%d" % b][:])])
 
     def mix(names, dm, delta, base, out):
         t, table = new("tf"), new("tu")
         h = scan(names[0], dm)
-        op(names[1], "v", [h, delta], [t], lambda: V.tensor_tensor(ap(t), ap(h, 15, C, 16), ap(delta), MUL))
-        op(names[2], "v", [t, base], [out], lambda: V.tensor_tensor(ap(out), ap(t), ap(base), ADD))
-        op(names[3], "v", [out], [table], lambda: V.tensor_copy(ap(table), ap(out)))
+        op(names[1], [h, delta], [t], v=lambda: V.tensor_tensor(ap(t), ap(h, 15, C, 16), ap(delta), MUL))
+        op(names[2], [t, base], [out], v=lambda: V.tensor_tensor(ap(out), ap(t), ap(base), ADD))
+        op(names[3], [out], [table], v=lambda: V.tensor_copy(ap(table), ap(out)))
         return table
 
     def sums(n, o):
+        p = "pb" if n in FAR else "pa"
         for b in range(4):
             f, u = "f%d" % b, "u%d" % b
             if b in SHARED[n]:
                 move("g%d" % b, [f, o], ["gg%d" % b], T["gg%d" % b][:], by(f, o))
-                op(u, "v", ["gg%d" % b, "pa%d" % b], [u], lambda b=b, u=u: V.tensor_tensor(T[u][:], T["gg%d" % b][:], T.pa[:, 512 * b:512 * b + C], ADD))
+                op(u, ["gg%d" % b, "%s%d" % (p, b)], [u], v=lambda b=b, u=u: V.tensor_tensor(T[u][:], T["gg%d" % b][:], T[p][:, 512 * b:512 * b + C], ADD))
+            elif b in ADDED[n]:
+                move("g%d" % b, [f, o], [u], T[u][:], by(f, o))
+                load(u, "g_" + u, [f, u], [u], [(T[u][:], T[f][:])])
             else:
-                op(u, "v", [f, "fd%d" % b, o], [u], lambda b=b, f=f, u=u: V.tensor_tensor(T[u][:], by(f, o), T["fd%d" % b][:], ADD))
+                op(u, [f, "fd%d" % b, o], [u], v=lambda b=b, f=f, u=u: V.tensor_tensor(T[u][:], by(f, o), T["fd%d" % b][:], ADD))
 
     def means(n, o, parts):
         zq, zs, zl, zp = "zq%d" % n, "zs%d" % n, "zl%d" % n, "zp%d" % n
@@ -415,57 +386,57 @@ def rank_program(g, core, T, topo):
             for b in range(4):
                 move("z%d%s" % (b, tag), ["u%d" % b, o], ["zt%d%d" % (b, h)], T.zt[:, 4 * p + b:4 * e:4], by("u%d" % b, o, p, e), 0.5)
             key = "%s%d" % (zq, h)
-            op("qz" + tag, "v", ["zt%d%d" % (b, h) for b in range(4)], [key], lambda p=p, e=e: V.quantize_mx(T[zq][:, p:e], T[zs][:, p:e], T.zt[:, 4 * p:4 * e]))
-            send("send_z" + tag, STEP[n - 1], [(T[zl][:, p:e].bitcast(dt.uint8), T[zq][:, p:e].bitcast(dt.uint8)), (T[zp][:, p:e], T[zs][:, p:e])], [key], "a_z%d%d" % (n, h), "%s%d" % (zl, h))
+            op("qz" + tag, ["zt%d%d" % (b, h) for b in range(4)], [key], v=lambda p=p, e=e: V.quantize_mx(T[zq][:, p:e], T[zs][:, p:e], T.zt[:, 4 * p:4 * e]))
+            if n not in FAR:
+                send("send_z" + tag, STEP[n - 1], [(T[zl][:, p:e].bitcast(dt.uint8), T[zq][:, p:e].bitcast(dt.uint8)), (T[zp][:, p:e], T[zs][:, p:e])], [key], "a_z%d%d" % (n, h), "%s%d" % (zl, h))
 
     def layer(n, b, h, p, e, bank, name):
-        zl, zp = "zl%d" % n, "zp%d" % n
+        zl, zp = ("zq%d" % n, "zs%d" % n) if n in FAR else ("zl%d" % n, "zp%d" % n)
         at = T[bank[:2]][:, 512 * int(bank[2]):512 * int(bank[2]) + e - p]
-        op("m" + name, "t", ["wq", "wp", "%s%d" % (zl, h)], [bank], lambda: g.tensor.matmul_mx(at, T.wq[:, 128 * b:128 * b + 128], T.wp[:, 128 * b:128 * b + 128], T[zl][:, p:e], T[zp][:, p:e], True, True))
+        op("m" + name, ["wq", "wp", "%s%d" % (zl, h)], [bank], t=lambda: g.tensor.matmul_mx(at, T.wq[:, 128 * b:128 * b + 128], T.wp[:, 128 * b:128 * b + 128], T[zl][:, p:e], T[zp][:, p:e], True, True))
         move(name, [bank], ["r%d%d" % (b, h)], T["r%d" % b][:, p:e], at, 0.03125)
 
-    def home(b, h, p, e, runs, back, tag):
+    def home(n, b, h, p, e, runs, back, tag):
         r, out, rs = "r%d" % b, T.xt[:, 4 * p + b:4 * e:4], ["r%d%d" % (b, i) for i in range(runs)]
-        if "h" + tag in APART[phase[0]].split():
+        if gathered(n, b)[h]:
             move("h" + tag, rs + [back], ["hh%d%d" % (b, h)], T["hh%d" % b][:, p:e], by(r, back, p, e))
-            op("x" + tag, "v", ["hh%d%d" % (b, h), "pa%d" % b], ["xt%d%d" % (b, h)], lambda: V.tensor_tensor(out, T["hh%d" % b][:, p:e], T.pa[:, 512 * b + p:512 * b + e], ADD))
+            op("x" + tag, ["hh%d%d" % (b, h), "pa%d" % b], ["xt%d%d" % (b, h)], v=lambda: V.tensor_tensor(out, T["hh%d" % b][:, p:e], T.pa[:, 512 * b + p:512 * b + e], ADD))
         else:
-            op("x" + tag, "v", rs + ["f%d" % b, back], ["xt%d%d" % (b, h)], lambda: V.tensor_tensor(out, by(r, back, p, e), T["f%d" % b][:, p:e], ADD))
+            f = "%s%d" % ("fe" if n in FAR else "f", b)
+            op("x" + tag, rs + [f, back], ["xt%d%d" % (b, h)], v=lambda: V.tensor_tensor(out, by(r, back, p, e), T[f][:, p:e], ADD))
 
     def new_state(n, back):
         for b in range(4):
             layer(n, b, 0, 0, C, "pb%d" % b, "r%d" % b)
-            home(b, 0, 0, C, 1, back, str(b))
-        op("qx", "v", ["xt%d0" % b for b in range(4)], ["xq%d" % n], lambda: V.quantize_mx(T["xq%d" % n][:, 0:C], T["xs%d" % n][:, 0:C], T.xt[:, 0:4 * C]))
+            home(n, b, 0, 0, C, 1, back, str(b))
+        op("qx", ["xt%d0" % b for b in range(4)], ["xq%d" % n], v=lambda: V.quantize_mx(T["xq%d" % n][:, 0:C], T["xs%d" % n][:, 0:C], T.xt[:, 0:4 * C]))
 
     def last_state(n, back, o):
-        op("osp", "s", ["iots", "mid", o], ["osp"], lambda: S.activation(T.osp[:], by("iots", o), ActivationFunctionType.Identity, bias=T.bia[:, 2:3]))
-        load("fo", "y", "l_fo", ["osp"], [], [(T.fo[:, 0:C], T.osp[0:128:16, 0:C])])
-        op("qv", "v", ["vt"], ["qv"], lambda: V.quantize_mx(T.qv[:, 0:128], T.sv[:, 0:128], T.vt[:, 0:512]))
-        banks = [["pb0", "pb1", "pb2", "pb3"], ["pa0", "pa1", "pb0", "pb1"]]
+        op("osp", ["iots", "mid", o], ["osp"], s=lambda: S.activation(T.osp[:], by("iots", o), ActivationFunctionType.Identity, bias=T.bia[:, 2:3]),
+           v=lambda: V.tensor_scalar(T.osp[:], by("iots", o), float(MID), None, ADD))
+        load("fo", "l_fo", ["osp"], [], [(T.fo[:, 0:C], T.osp[0:128:16, 0:C])])
+        op("qv", ["vt"], ["qv"], v=lambda: V.quantize_mx(T.qv[:, 0:128], T.sv[:, 0:128], T.vt[:, 0:512]))
         for h, (p, e) in enumerate(LAST):
             for b in range(4):
-                layer(n, b, h, p, e, banks[h][b], "r%d%d" % (b, h))
+                layer(n, b, h, p, e, "%s%d" % ("pb" if h % 2 == 0 or any(gathered(n, b)) else "pa", b), "r%d%d" % (b, h))
         for h, (p, e) in enumerate(ENDS):
             for b in range(4):
-                home(b, h, p, e, len(LAST), back, "%d%d" % (b, h))
-            key, bank = "xq3%d" % h, "pb%d" % (2 + h)
-            at = T.pb[:, 512 * (2 + h):512 * (2 + h) + e - p]
-            op("qx%d" % h, "v", ["xt%d%d" % (b, h) for b in range(4)], [key], lambda p=p, e=e: V.quantize_mx(T.xq3[:, p:e], T.xs3[:, p:e], T.xt[:, 4 * p:4 * e]))
-            op("my%d" % h, "t", ["qv", key], [bank], lambda at=at, p=p, e=e: g.tensor.matmul_mx(at, T.qv[:, 0:128], T.sv[:, 0:128], T.xq3[:, p:e], T.xs3[:, p:e], True, True))
-            load("oc%d" % h, STORES["oc%d" % h], "l_oc%d" % h, [key], [], [(T.oc[:, 4 * p:4 * e], T.xq3[:, p:e].bitcast(dt.uint8))])
+                home(n, b, h, p, e, len(LAST), back, "%d%d" % (b, h))
+            key, bank = "xq3%d" % h, "pb%d" % (h % 2)
+            at = T.pb[:, 512 * (h % 2):512 * (h % 2) + e - p]
+            op("qx%d" % h, ["xt%d%d" % (b, h) for b in range(4)], [key], v=lambda p=p, e=e: V.quantize_mx(T.xq3[:, p:e], T.xs3[:, p:e], T.xt[:, 4 * p:4 * e]))
+            op("my%d" % h, ["qv", key], [bank], t=lambda at=at, p=p, e=e: g.tensor.matmul_mx(at, T.qv[:, 0:128], T.sv[:, 0:128], T.xq3[:, p:e], T.xs3[:, p:e], True, True))
+            load("oc%d" % h, "l_oc%d" % h, [key], [], [(T.oc[:, 4 * p:4 * e], T.xq3[:, p:e].bitcast(dt.uint8))])
             move("y%d" % h, [bank], ["ysb%d" % h], T.ysb[:, p:e], at)
-            load("yo%d" % h, STORES["yo%d" % h], "l_y%d" % h, ["ysb%d" % h], [], [(T.y[:, p:e], T.ysb[:, p:e])])
+            load("yo%d" % h, "l_y%d" % h, ["ysb%d" % h], [], [(T.y[:, p:e], T.ysb[:, p:e])])
         for k in range(4):
-            load("o%d" % k, STORES["o%d" % k], "l_osc%d" % k, ["xq3%d" % h for h in range(len(ENDS))], [], [(T.osc[4 * k:4 * k + 4, 0:C], T.xs3[32 * k:32 * k + 4, 0:C])])
+            load("o%d" % k, "l_osc%d" % k, ["xq3%d" % h for h in range(len(ENDS))], [], [(T.osc[4 * k:4 * k + 4, 0:C], T.xs3[32 * k:32 * k + 4, 0:C])])
 
     o, back, own = first_orders()
     first_state()
-    first = {}
-    ahead_of_cycles()
     for n in (1, 2, 3):
         delta, base = apart(n, own)
-        low = cycles_of_four(n) if n in BOTH else cycles(n)
+        low = cycles(n)
         if n > 1:
             new_state(n - 1, back)
         unpack(n - 1, o)
@@ -475,16 +446,21 @@ def rank_program(g, core, T, topo):
         phase[0] = n + 1
         if n < len(STEP):
             hand_on(n + 1, o=o)
-        sums(n, o)
+        far = o
+        if n in FAR:
+            far = "on%d" % n
+            send("send_n", STEP[n - 1], [(T[far][:], ap(o))], [o], "a_n%d" % n, far)
+        sums(n, far)
         gather("dd", dd, dm, back)
         back = mix(["es", "et", "ef", "eu"], dd, delta[1], base[1], own[1])
         if n < len(STEP):
             gather("bk", "bk%d" % n, "iots", back)
             hand_on(n + 1, own=own)
-        means(n, o, [(0, C)] if n < len(STEP) else LAST)
+        parts = [(0, C)] if n < len(STEP) else LAST
+        means(n, far, parts)
     last_state(len(STEP), back, o)
 
-    order = {q: ["%d:%s" % (n, name) for n in LIKE for name in PLAN[q][LIKE[n]].split()] for q in queues}
+    order = {q: ["%d:%s" % (n + (name[0] == "+") - (name[0] == "-"), name.lstrip("+-")) for n in LIKE for name in PLAN[LIKE[n]][q].split()] for q in queues}
     order = {q: [name for name in order[q] if name in calls] for q in queues}
     assert sorted(sum(order.values(), [])) == sorted(calls), set(calls) ^ set(sum(order.values(), []))
     issue(order)

@@ -8,62 +8,42 @@ UP = 512.0
 LAST = [(0, 224), (224, C)]
 ENDS = [(0, 320), (320, C)]
 
-RADIX = {n: [2, 3, 3, 3, 3, 3] for n in (1, 2, 3)}
+FORM = {}
+HALF = ()
+RADIX = {n: [3, 3, 3, 3, 3] if n in HALF else [2, 3, 3, 3, 3, 3] for n in (1, 2, 3)}
 APART = {2: "h2 h3", 3: "h2 h3", 4: "h20 h30 h21 h31"}
-SHARED = {1: (), 2: (), 3: (3,)}
-ADDED = {1: (), 2: (), 3: ()}
-FAR = ()
-SCAN = (2, 3)
-SPLIT = {1: "dm k p0", 2: "dm", 3: "dm", 4: ""}
-
-PLAN = {
-    1: {"v": "ones idx md eye e1 iots e2q e0 uo ou d0 inv e3q d4 of e0q bia0 mid d5 bia1 qu qur qx ia e1q ib ic k> ka kb m p0> a1 b1 l1 l1' a2 b2 w2 l2 l2' a3 w3 b3 delta l3 l3' a4 b4 w4 l4 l4' a5 w5 b5 l5 l5' la lb dm> base ds t nf nu",
-        "s": "d1 d2 d3 sur f3 k< p0< w1 p1 p1' f0 p2 p2' p3 p3' f1 p4 p4' f2 sc less so dm<",
-        "g": "one uoi mdi send_o send_b",
-        "t": "mf3 ms mf0 mf1 mf2",
-        "y": "od u x ws wc v fd3 fd0 fd1 fd2"},
-    2: {"v": "u2 es u1 et ef eu u3 u0 k ka kb m1 qz m a1 b1 l1 l1' delta a2 less b2 base l2 l2' r0 a3 b3 x0 l3 x1 l3' a4 x2 b4 x3 qx l4 a5 l4' b5 w5 l5 l5' la lb dm> ds t nf nu",
-        "s": "dd z2 z1 bk z3 z0 p0 p1 p1' w2 p2 r3 p2' r1 p3 r2 p3' h2 h3 p4 p4' f2 f1 sc f0 so dm< f3",
-        "g": "send_o send_b send_z w3 w4",
-        "t": "mr3 mr0 mr1 mr2 mf2 mf1 ms mf0 mf3",
-        "y": "fd2 fd1 fd0 fd3"},
-    4: {"v": "u2 u1 u0 u3 z30 qz0 z01 qz1 es et ef qv eu r10 r20 r00 r11 x10 r31 x11 r21 x00 x30 x20 qx0 x21 x01 x31 qx1 y1",
-        "s": "dd g3 z20 z10 z00 z21 z11 z31 osp r30 r01 h30 h20 h21 h31 y0 o2 o3 yo1",
-        "g": "send_z0 send_z1",
-        "t": "mr10 mr20 mr00 mr11 mr30 mr31 mr01 mr21 my0 my1",
-        "y": "fo oc0 yo0 oc1 o0 o1"},
-}
-PLAN = {
-    1: {"v": "ones md uo bia0 iots e0 e1 bia1 d0 ou of inv d5 qx k< qu ka m kb ia p0> a1 b1 ib l1 ic l1' e1q a2 b2 qur l2 e0q l2' a3 e2q b3 e3q delta l3 mid l3' a4 b4 w4 l4 l4' a5 w5 b5 l5 l5' la lb dm> ds base t",
-        "s": "d1 d2 d3 d4 k> p0< sur p1 p1' w2 p2 p2' w3 p3 p3' f1 less p4 p4' f3 f0 sc so f2 dm<",
-        "g": "mdi uoi send_o eye w1 send_b",
-        "t": "mf2 mf0 mf3 mf1 ms",
-        "y": "od x u fd1 wc ws v fd3 fd0 fd2"},
-    2: {"v": "es -nf et -nu ef eu u1 u0 u3 ka m kb u2 m1 a1 b1 l1 qz l1' a2 b2 delta l2 l2' a3 r2 b3 x1 l3 x0 l3' x3 a4 x2 b4 qx l4 l4' p4' a5 b5 l5 l5' la lb dm< less ds base t",
-        "s": "dd bk k z1 z3 p0 z0 z2 p1 p1' w2 p2 p2' r1 r3 r0 p3 h3 p3' h2 w4 p4 f1 sc f3 f2 so f0 dm>",
-        "g": "send_o send_b send_z w3 w5",
-        "t": "mr1 mr2 mr3 mr0 mf1 ms mf3 mf0 mf2",
-        "y": "fd1 fd3 fd2 fd0"},
-    3: {"v": "es -nf et -nu ef eu u1 u2 u0 ka delta kb m u3 a1 m1 b1 l1 qz l1' a2 w2 b2 l2 l2' r2 a3 x0 b3 x1 l3 x2 l3' x3 a4 b4 qx l4 l4' a5 w5 b5 l5 l5' la lb dm< base ds t nf nu f2",
-        "s": "dd bk k z1 z2 p0 z0 z3 p1 p1' less p2 p2' r0 r1 r3 h2 p3 h3 p3' w4 p4 p4' sc fe0 so f0 f1 dm> fe1",
-        "g": "send_o send_b send_z w3 send_x",
-        "t": "mr0 mr2 mr1 mr3 ms mf2 mf1 mf0 mg3 mg0 mg1 mg2 mf3",
-        "y": "fd0 fd1"},
-    4: {"v": "es et u0 u1 u2 u3 z10 z21 qz0 ef qv eu qz1 r00 r20 r31 x10 x11 x01 x30 x00 x21 x31 x20 qx1 qx0 y0",
-        "s": "dd -f3 osp g2 g3 z01 z00 z20 z30 z11 z31 r30 r10 r11 r01 h30 r21 h31 h21 h20 y1 o2 yo1 o3",
-        "g": "send_n",
-        "t": "mr30 mr00 mr10 mr20 mr11 mr31 mr01 mr21 my1 my0",
-        "y": "fo oc1 oc0 o0 o1 yo0"},
-}
-LIKE = {1: 1, 2: 2, 3: 3, 4: 4}
-FAR = (3,)
 SHARED = {1: (), 2: (), 3: (2, 3)}
+FAR = (3,)
+SCAN = (2, 3)
+SPLIT = {1: "dm k p0", 2: "dm x0 x1 x2 x3", 3: "dm x0 x1 x2 x3", 4: ""}
 
-LISTS = 100
+PLAN = {
+    1: {"v": "ones md iots bia0 e1 dz0 e0 uo bia1 ou d0 hbl of dz1 inv qx k< ia ka qu kb m p0> qur a1 ib b1 e2q l1 e0q l1' a2 ic b2 e3q l2 l2' a3 w3 b3 base delta l3 e1q l3' a4 w4 b4 l4 l4' a5 w5 b5 l5 l5' la lb dm> ds mid nf",
+        "s": "d1 d2 d3 d4 d5 k> p0< w1 p1 p1' w2 p2 p2' sur p3 p3' f1 p4 p4' sc f2 f3 so f0 dm<",
+        "g": "mdi uoi send_o eye send_b",
+        "t": "ms mf0 mf3 mf1 mf2",
+        "y": "od x u fd1 wc ws fd2 fd0 fd3"},
+    2: {"v": "es -nu ef eu u1 u0 u3 ka m kb u2 z3 a1 m1 b1 qz l1 base l1' a2 w2 b2 r0 l2 x0> l2' a3 x0< b3 x1> x1< l3 x3< l3' a4 x3> b4 x2< x2> l4 qx l4' a5 w5 b5 l5 delta l5' la lb dm< ds nf",
+        "s": "dd bk k z0 z1 p0 z2 p1 p1' p2 r3 p2' r1 h3 p3 r2 p3' h2 w4 p4 p4' sc f1 f0 so f2 dm>",
+        "g": "send_o send_b send_z w3",
+        "t": "mr0 mr3 mr2 mr1 ms mf1 mf2 mf0 mf3",
+        "y": "fd0 fd1 fd2 -v fd3"},
+    3: {"v": "es -nu ef eu u2 u0 u1 ka m kb u3 z1 a1 m1 b1 qz l1 l1' a2 w2 b2 delta l2 r0 l2' x0> a3 x0< b3 x2< x2> l3 x1< l3' a4 x1> b4 x3> x3< l4 qx l4' a5 w5 b5 l5 l5' la lb +qv dm> base ds nf nu f2",
+        "s": "dd -f3 bk k z0 z2 p0 z3 p1 p1' p2 r2 p2' h2 r1 p3 r3 p3' h3 w4 p4 p4' sc fe0 so f1 f0 dm< fe1 f3",
+        "g": "send_o send_b send_z w3 send_x",
+        "t": "mr2 mr0 mr3 mr1 ms mf0 mg1 mf2 mg0 mg3 mg2 mf1 mf3",
+        "y": "fd1 fd0"},
+    4: {"v": "dd u0 u3 u1 u2 z10 es qz0 z21 ef qz1 r30 r10 r11 eu r21 x11 x00 x01 x10 x30 x31 x21 x20 qx1 qx0 y1 y0",
+        "s": "osp g3 g2 z00 z30 z31 z20 z01 z11 r20 r00 r01 r31 h20 h30 h31 h21 oc1 oc0 o0 yo0",
+        "g": "send_n",
+        "t": "mr20 mr30 mr00 mr10 mr11 mr01 mr21 mr31 my1 my0",
+        "y": "fo o2 o3 yo1 o1"},
+}
+
 SCRATCH = {
     "md": ("sbuf", [128, 16], "int32"), "ee": ("sbuf", [128, 32], "float32"), "d0": ("sbuf", [128, C], "bfloat16"),
     "iots": ("sbuf", [128, C], "bfloat16"), "ones": ("sbuf", [128, 516], "bfloat16"),
-    "idx": ("sbuf", [128, 516], "float16"), "eye": ("sbuf", [128, 516], "bfloat16"), "bia": ("sbuf", [128, 4], "float32"),
+    "eye": ("sbuf", [128, 516], "bfloat16"), "bia": ("sbuf", [128, 4], "float32"),
     "uoi": ("sbuf", [128, 8], "int32"), "uo": ("sbuf", [128, 8], "uint16"),
     "odl": ("sbuf", [128, K], "int32"), "ut": ("sbuf", [128, 512], "bfloat16"),
     "vt": ("sbuf", [128, 512], "bfloat16"), "xt0": ("sbuf", [128, 4 * C], "bfloat16"),
@@ -75,8 +55,9 @@ SCRATCH = {
     "sc": ("sbuf", [128, C], "bfloat16"), "so": ("sbuf", [128, C], "bfloat16"),
     "zt": ("sbuf", [128, 4 * C], "bfloat16"), "xt": ("sbuf", [128, 4 * C], "bfloat16"),
     "ysb": ("sbuf", [128, C], "float32"), "osp": ("sbuf", [128, C], "float32"),
-    "ls": ("sbuf", [128, C * LISTS], "bfloat16"), "hs": ("sbuf", [128, C * 40], "float16"),
-    "tu": ("sbuf", [128, K * 48], "uint16"), "tf": ("sbuf", [128, K * 48], "float32"),
+    "ls": ("sbuf", [128, C * 90], "bfloat16"), "hs": ("sbuf", [128, C * 30], "float16"), "tu": ("sbuf", [128, K * 48], "uint16"),
+    "wd": ("sbuf", [128, 2 * C * 8], "bfloat16"),
+    "ot0": ("sbuf", [128, 2 * K], "float16"), "dz": ("sbuf", [128, 6 * K], "float16"), "hb": ("sbuf", [128, 6 * C + 45], "float16"),
     "pa": ("psum", [128, 2048], "float32"), "pb": ("psum", [128, 2048], "float32"),
 }
 for _b in range(4):
@@ -92,15 +73,17 @@ for _b in range(4):
 for _n in (1, 2, 3):
     SCRATCH["bk%d" % (_n - 1)] = ("sbuf", [128, C], "bfloat16")
     SCRATCH["ol%d" % _n] = ("sbuf", [128, K], "uint16")
-    SCRATCH["bl%d" % _n] = ("sbuf", [128, 2 * K], "float32")
+    SCRATCH["bl%d" % _n] = ("sbuf", [128, 2 * K if _n == 1 else 6 * K], "float16")
+    SCRATCH["ot%d" % _n] = ("sbuf", [128, 6 * K], "float16")
     SCRATCH["on%d" % _n] = ("sbuf", [128, K], "uint16")
+    for _k in ("lt", "ll", "lm"):
+        SCRATCH["%s%d" % (_k, _n)] = ("sbuf", [128, K], "bfloat16")
     SCRATCH["zq%d" % _n] = ("sbuf", [128, C], "float8_e4m3fn_x4")
     SCRATCH["zs%d" % _n] = ("sbuf", [128, C], "uint8")
     SCRATCH["zl%d" % _n] = ("sbuf", [128, C], "float8_e4m3fn_x4")
     SCRATCH["zp%d" % _n] = ("sbuf", [128, C], "uint8")
 
-SEMAPHORES = ["cv", "cs", "ct", "cg", "sent"] \
-    + ["a_z10", "a_z20", "a_z30", "a_z31", "a_z32"] + ["a_%s%d" % (k, n) for k in "obn" for n in (1, 2, 3)] + ["g_u%d" % b for b in range(4)] \
+SEMAPHORES = ["cv", "cs", "ct", "cg", "sent"] + ["a_z10", "a_z11", "a_z20", "a_z21", "a_z30"] + ["a_%s%d" % (k, n) for k in "obnl" for n in (1, 2, 3)] \
     + ["l_" + n for n in ("od", "x", "u", "v", "wc", "ws", "y0", "y1", "y2", "fo", "oc0", "oc1", "oc2", "osc0", "osc1", "osc2", "osc3", "f0", "f1", "f2", "f3")]
 
 ADD, MUL, SUB, MIN, MAX = AluOpType.add, AluOpType.mult, AluOpType.subtract, AluOpType.min, AluOpType.max
@@ -125,6 +108,8 @@ def rank_program(g, core, T, topo):
         for k in writes:
             after.update(wrote.get(k, []))
             after.update(read.get(k, []))
+            for tag in "<>":
+                after.update(read.pop(k + tag, []) + wrote.pop(k + tag, []))
         for k in reads:
             read.setdefault(k, []).append(name)
         for k in writes:
@@ -168,7 +153,7 @@ def rank_program(g, core, T, topo):
             elif c["kind"] == "load":
                 sem, pairs = c["what"]
                 for out, in_ in pairs:
-                    (g.dma_start(out, in_, accum_op=ADD) if q == "g" else queues[q].dma_start(out, in_)).then_inc(T.sem[sem], 16)
+                    queues[q].dma_start(out, in_).then_inc(T.sem[sem], 16)
                     totals[sem] = totals.get(sem, 0) + 16
             else:
                 step, pairs, sem, few = c["what"]
@@ -196,49 +181,53 @@ def rank_program(g, core, T, topo):
         for sem in sorted(totals):
             wait("g", sem, totals[sem])
 
-    used = {"tu": 0, "tf": 0, "ls": 0, "hs": 0}
-    width = {"tu": K, "tf": K, "ls": C, "hs": C}
+    used = {"tu": 0, "ls": 0, "hs": 0, "wd": 5}
+    width = {"tu": K, "ls": C, "hs": C, "wd": 2 * C}
 
     def new(kind):
         used[kind] += 1
         return "%s.%d" % (kind, used[kind] - 1)
 
-    def pair():
-        used["tf"] += used["tf"] % 2
-        return [new("tf"), new("tf")]
-
     def ap(key, a=0, b=None, step=1):
         if "." in key:
             kind, i = key.split(".")
             w = width[kind]
+            if kind == "wd":
+                return T.wd[:, w * int(i) + 2 * a:w * int(i) + (w if b is None else 2 * b):2 * step or 1]
             return T[kind][:, w * int(i) + a:w * int(i) + (w if b is None else b):step]
         return T[key][:, a:(C if b is None else b):step]
 
     def by(key, table, p=0, e=C):
-        return ap(key).indirect(ap(table, p // 16, e // 16))
+        return ap(key, step=0 if key[:2] == "wd" else 1).indirect(ap(table, p // 16, e // 16))
 
     def move(name, reads, writes, out, in_, scale=None):
         op(name, reads, writes, s=lambda: S.activation(out, in_, COPY) if scale is None else S.activation(out, in_, COPY, scale=scale),
            v=lambda: V.tensor_copy(out, in_) if scale is None else V.tensor_scalar(out, in_, scale, None, MUL))
 
+    HALVES = (("<", 0, MID), (">", MID, C))
+
+    def part(key, tag):
+        return key + tag if key + tag in wrote else key
+
     def gather(name, out, key, table):
         if name not in SPLIT[phase[0]].split():
             return move(name, [key, table], [out], ap(out), by(key, table))
-        before = wrote.get(out, []), read.get(out, [])
-        move(name + "<", [key, table], [out], ap(out, 0, MID), by(key, table, 0, MID))
-        first = wrote[out]
-        wrote[out], read[out] = before
-        move(name + ">", [key, table], [out], ap(out, MID, C), by(key, table, MID, C))
-        wrote[out] = first + wrote[out]
+        for tag, p, e in HALVES:
+            read[out + tag] = read.get(out + tag, []) + read.get(out, []) + wrote.get(out, [])
+            move(name + tag, [key, part(table, tag)], [out + tag], ap(out, p, e), by(key, table, p, e))
+        wrote[out], read[out] = wrote[out + "<"] + wrote[out + ">"], []
 
-    def scan(name, key):
-        h = new("hs")
-        op(name, [key, "d0"], [h], v=lambda: V.tensor_tensor_scan(ap(h), T.d0[:, 0:C], ap(key), 0.0, ADD, MAX))
-        return h
-
-    def conv(a, b, key):
-        h, t = scan(a, key), new("tu")
-        op(b, [h, "bia"], [t], v=lambda: V.tensor_scalar(ap(t), ap(h, 15, C, 16), T.bia[:, 1:2], None, ADD))
+    def conv(a, b, key, double=True):
+        h, t = new("hs"), new("tu")
+        if double and key[:2] == "wd":
+            op(a, [key, "d0"], [h], v=lambda: V.tensor_tensor_scan(ap(h), T.d0[:, 0:C], ap(key), 0.0, ADD, MAX))
+            op(b, [h, "bia"], [t], v=lambda: V.tensor_scalar(ap(t), ap(h, 15, C, 16), T.bia[:, 1:2], 2.0, ADD, MUL))
+            return t
+        for tag, p, e in HALVES if a in SPLIT[phase[0]].split() else (("", 0, C),):
+            op(a + tag, [part(key, tag), "d0"], [h + tag], v=lambda p=p, e=e: V.tensor_tensor_scan(ap(h, p, e), T.d0[:, p:e], ap(key, p, e), 0.0, ADD, MAX))
+            op(b + tag, [h + tag, "bia"], [t + tag], v=lambda p=p, e=e: V.tensor_scalar(ap(t, p // 16, e // 16), ap(h, p + 15, e, 16), T.bia[:, 1:2], None, ADD))
+        if tag:
+            wrote[t] = wrote[t + "<"] + wrote[t + ">"]
         return t
 
     def gathered(n, b):
@@ -261,6 +250,12 @@ def rank_program(g, core, T, topo):
     op("bia0", ["md"], ["bia0"], v=lambda: V.tensor_scalar(T.bia[:, 0:1], T.md[:, 15:16], 0.0, -UP, AluOpType.not_equal, MUL))
     op("bia1", ["bia0"], ["bia"], v=lambda: V.tensor_scalar(T.bia[:, 1:2], T.bia[:, 0:1], float(MID), None, ADD))
     op("mid", [], ["mid"], v=lambda: V.memset(T.bia[:, 2:3], float(MID)))
+    op("hbl", ["ones", "bia0"], ["hbl"], v=lambda: V.tensor_scalar(T.hb[:, 61::48], T.ones[:, 0:2 * K], T.bia[:, 0:1], None, MUL))
+    op("dz0", ["ones"], ["dz0"], v=lambda: V.tensor_scalar(T.dz[:, 0::3], T.ones[:, 0:2 * K], 0.0, None, MUL))
+    op("dz1", ["ones", "dz0"], ["dz01"], v=lambda: V.tensor_copy(T.dz[:, 1::3], T.ones[:, 0:2 * K]))
+    if FORM:
+        for i in range(5):
+            op("wd%d" % i, [], ["wd.%d" % i], v=lambda i=i: V.memset(T.wd[:, 2 * C * i + 1:2 * C * (i + 1):2], -UP))
     op("uo", ["uoi"], ["uo"], v=lambda: V.tensor_copy(T.uo[:], T.uoi[:]))
     for b in range(4):
         op("e%dq" % b, ["eye"], ["qe%d" % b], v=lambda b=b: V.quantize_mx(T.qe[:, 128 * b:128 * b + 128], T.se[:, 128 * b:128 * b + 128], T.eye[:, 3 - b:515 - b]))
@@ -278,28 +273,55 @@ def rank_program(g, core, T, topo):
         if o is not None:
             send("send_o", STEP[n - 1], [(T["ol%d" % n][:], ap(o))], [o], "a_o%d" % n, "ol%d" % n, few=0 if n == 1 else None)
         else:
-            send("send_b", STEP[n - 1], [(T["bl%d" % n][:], ap(own[0], 0, 2 * K))], own, "a_b%d" % n, "bl%d" % n, few=1 if n == 1 else None)
+            send("send_b", STEP[n - 1], [(T["bl%d" % n][:], T["ot%d" % (n - 1)][:])], own, "a_b%d" % n, "bl%d" % n, few=1 if n == 1 else None)
 
     def first_orders():
-        o, own = new("tu"), pair()
+        o, own = new("tu"), ["ot00", "ot01"]
         op("ou", ["odl"], [o], v=lambda: V.tensor_copy(ap(o), T.odl[:]))
         hand_on(1, o=o)
-        op("of", ["odl"], [own[0]], v=lambda: V.tensor_copy(ap(own[0]), T.odl[:]))
+        op("of", ["odl"], [own[0]], v=lambda: V.tensor_copy(T.ot0[:, 0:K], T.odl[:]))
         op("inv", ["iots", o], ["bk0"], v=lambda: V.tensor_copy(by("bk0", o), T.iots[:]))
         back = conv("ia", "ib", "bk0")
-        op("ic", [back], [own[1]], v=lambda: V.tensor_copy(ap(own[1]), ap(back)))
+        op("ic", [back], [own[1]], v=lambda: V.tensor_copy(T.ot0[:, K:2 * K], ap(back)))
         hand_on(1, own=own)
         return o, back, own
 
     def apart(n, own):
-        delta, less, base = pair(), pair(), pair()
-        op("delta", ["bl%d" % n] + own, delta, v=lambda: V.tensor_tensor(ap(delta[0], 0, 2 * K), T["bl%d" % n][:], ap(own[0], 0, 2 * K), SUB))
-        op("less", delta + ["bia0"], less, v=lambda: V.tensor_scalar(ap(less[0], 0, 2 * K), ap(delta[0], 0, 2 * K), T.bia[:, 0:1], None, MUL),
-           s=lambda: S.activation(ap(less[0], 0, 2 * K), ap(delta[0], 0, 2 * K), COPY, scale=T.bia[:, 0:1]))
-        op("base", less + own, base, v=lambda: V.tensor_tensor(ap(base[0], 0, 2 * K), ap(less[0], 0, 2 * K), ap(own[0], 0, 2 * K), ADD))
-        return delta, base
+        mine, far, step = "ot%d" % (n - 1), "bl%d" % n, 1 if n == 1 else 3
+        op("delta", [far] + own, ["dz"], v=lambda: V.tensor_tensor(T.dz[:, 2::3], T[far][:, step - 1::step], T[mine][:, step - 1::step], SUB))
+        op("base", own, ["hbo"], v=lambda: V.tensor_copy(T.hb[:, 77::48], T[mine][:, step - 1::step]))
+
+    def wide(n):
+        m, g1, g2, power, other = ["wd.%d" % i for i in range(5)]
+
+        def lower(name, a, b):
+            out = new("wd")
+            op(name, [a, b], [out], v=lambda: V.tensor_tensor_scan(ap(out, step=0), ap(a, step=0), ap(b, step=0), -UP, MAX, MIN))
+            return out
+
+        gather("k", power, "bk%d" % (n - 1), "ol%d" % n)
+        a = conv("ka", "kb", power)
+        op("m", ["iots", power], [m], v=lambda k=power: V.tensor_tensor_scan(ap(m), T.iots[:], ap(k), -UP, MAX, MIN))
+        gather("p0", other, power, a)
+        low, power, other = m, other, power
+        for j, form in enumerate(FORM[n], 1):
+            a = conv("a%d" % j, "b%d" % j, power)
+            gather("n%d" % j, g1, low, a)
+            if form == "p":
+                low = lower("s%d" % j, g1, low)
+                gather("n%d'" % j, g2, g1, a)
+                low = lower("s%d'" % j, g2, low)
+            else:
+                op("l%d'" % j, [g1, low, a], [g2], v=lambda low=low, a=a: V.tensor_tensor(ap(g2), by(g1, a), ap(low), MIN))
+                low = lower("s%d'" % j, g2, g1)
+            if j < len(FORM[n]):
+                gather("p%d" % j, other, power, a)
+                gather("p%d'" % j, power, other, a)
+        return conv("la", "lb", low, False)
 
     def cycles(n):
+        if n in FORM:
+            return wide(n)
         k, m = new("ls"), new("ls")
         gather("k", k, "bk%d" % (n - 1), "ol%d" % n)
         a = conv("ka", "kb", k)
@@ -310,11 +332,15 @@ def rank_program(g, core, T, topo):
         least("m", m)
         low, power = m, k
         radix = RADIX[n]
+        if radix[0] == 3:
+            twin, low = new("ls"), new("ls")
+            least("m0", twin)
+            op("l0", [twin, m, a], [low], v=lambda low=low, a=a: V.tensor_tensor(ap(low), by(twin, a), ap(m), MIN))
         for j, r in enumerate(radix):
             if j > 0:
                 a = conv("a%d" % j, "b%d" % j, power)
                 acc = new("ls")
-                if j == 1 and n in SCAN:
+                if j == 1 and n in SCAN and radix[0] == 2:
                     least("m1", acc)
                 else:
                     op("w%d" % j, [low], [acc], v=lambda acc=acc, low=low: V.tensor_copy(ap(acc), ap(low)),
@@ -330,7 +356,15 @@ def rank_program(g, core, T, topo):
                     out = new("ls")
                     gather("p%d%s" % (j, "'" * e), out, power, a)
                     power = out
-        return conv("la", "lb", low)
+        if n not in HALF:
+            return conv("la", "lb", low)
+        h, table, mine, far, both = new("hs"), new("tu"), "lt%d" % n, "ll%d" % n, "lm%d" % n
+        op("la", [low, "d0"], [h], v=lambda: V.tensor_tensor_scan(ap(h), T.d0[:, 0:C], ap(low), 0.0, ADD, MAX))
+        op("lb", [h, "bia0"], [mine], v=lambda: V.tensor_scalar(T[mine][:], ap(h, 15, C, 16), T.bia[:, 0:1], None, ADD))
+        send("send_l", STEP[n - 1], [(T[far][:], T[mine][:])], [mine], "a_l%d" % n, far)
+        op("lc", [mine, far], [both], v=lambda: V.tensor_tensor(T[both][:], T[mine][:], T[far][:], MIN))
+        op("ld", [both], [table], v=lambda: V.tensor_scalar(ap(table), T[both][:], float(MID), None, ADD))
+        return table
 
     def unpack(n, o):
         xq, xs = "xq%d" % n, "xs%d" % n
@@ -355,15 +389,15 @@ def rank_program(g, core, T, topo):
                     move("fe%d" % b, ["pa%d" % b], ["fe%d" % b], T["fe%d" % b][:], T.pa[:, 512 * b:512 * b + C])
         for b in range(4):
             move("f%d" % b, ["%s%d" % (p, b)], ["f%d" % b], T["f%d" % b][:], T[p][:, 512 * b:512 * b + C])
-            if b not in SHARED[n + 1] + ADDED[n + 1]:
+            if b not in SHARED[n + 1]:
                 load("fd%d" % b, "l_f%d" % b, ["f%d" % b], ["fd%d" % b], [(T["fd%d" % b][:], T["f%d" % b][:])])
 
-    def mix(names, dm, delta, base, out):
-        t, table = new("tf"), new("tu")
-        h = scan(names[0], dm)
-        op(names[1], [h, delta], [t], v=lambda: V.tensor_tensor(ap(t), ap(h, 15, C, 16), ap(delta), MUL))
-        op(names[2], [t, base], [out], v=lambda: V.tensor_tensor(ap(out), ap(t), ap(base), ADD))
-        op(names[3], [out], [table], v=lambda: V.tensor_copy(ap(table), ap(out)))
+    def mix(names, dm, n, i):
+        table, ot, h, out = new("tu"), T["ot%d" % n], "hb%d" % i, "ot%d%d" % (n, i)
+        op(names[0], [dm, "d0"], [h], v=lambda: V.tensor_tensor_scan(T.hb[:, 3 * C * i:3 * C * (i + 1):3], T.d0[:, 0:C], ap(dm), 0.0, ADD, MAX))
+        op(names[1], [h, "hbl", "hbo", "dz", "dz01"], [out], v=lambda: V.tensor_tensor_scan(
+            ot[:, 3 * K * i:3 * K * (i + 1)], T.dz[:, 3 * K * i:3 * K * (i + 1)], T.hb[:, 3 * C * i + 45:3 * C * (i + 1) + 45:16], 0.0, MUL, ADD))
+        op(names[2], [out], [table], v=lambda: V.tensor_copy(ap(table), ot[:, 3 * K * i + 2:3 * K * (i + 1):3]))
         return table
 
     def sums(n, o):
@@ -373,9 +407,6 @@ def rank_program(g, core, T, topo):
             if b in SHARED[n]:
                 move("g%d" % b, [f, o], ["gg%d" % b], T["gg%d" % b][:], by(f, o))
                 op(u, ["gg%d" % b, "%s%d" % (p, b)], [u], v=lambda b=b, u=u: V.tensor_tensor(T[u][:], T["gg%d" % b][:], T[p][:, 512 * b:512 * b + C], ADD))
-            elif b in ADDED[n]:
-                move("g%d" % b, [f, o], [u], T[u][:], by(f, o))
-                load(u, "g_" + u, [f, u], [u], [(T[u][:], T[f][:])])
             else:
                 op(u, [f, "fd%d" % b, o], [u], v=lambda b=b, f=f, u=u: V.tensor_tensor(T[u][:], by(f, o), T["fd%d" % b][:], ADD))
 
@@ -408,7 +439,20 @@ def rank_program(g, core, T, topo):
     def new_state(n, back):
         for b in range(4):
             layer(n, b, 0, 0, C, "pb%d" % b, "r%d" % b)
-            home(n, b, 0, 0, C, 1, back, str(b))
+            if "x%d" % b not in SPLIT[n + 1].split():
+                home(n, b, 0, 0, C, 1, back, str(b))
+                continue
+            r, hh, f, apart = "r%d" % b, "hh%d" % b, "f%d" % b, gathered(n, b)[0]
+            if apart:
+                move("h%d" % b, [r + "0", back], [hh + "0"], T[hh][:], by(r, back))
+            for tag, p, e in HALVES:
+                out, key = T.xt[:, 4 * p + b:4 * e:4], "xt%d0" % b
+                read[key + tag] = read.get(key + tag, []) + read.get(key, []) + wrote.get(key, [])
+                if apart:
+                    op("x%d%s" % (b, tag), [hh + "0", "pa%d" % b], [key + tag], v=lambda out=out, hh=hh, b=b, p=p, e=e: V.tensor_tensor(out, T[hh][:, p:e], T.pa[:, 512 * b + p:512 * b + e], ADD))
+                else:
+                    op("x%d%s" % (b, tag), [r + "0", f, back], [key + tag], v=lambda out=out, r=r, f=f, p=p, e=e: V.tensor_tensor(out, by(r, back, p, e), T[f][:, p:e], ADD))
+            wrote[key], read[key] = wrote[key + "<"] + wrote[key + ">"], []
         op("qx", ["xt%d0" % b for b in range(4)], ["xq%d" % n], v=lambda: V.quantize_mx(T["xq%d" % n][:, 0:C], T["xs%d" % n][:, 0:C], T.xt[:, 0:4 * C]))
 
     def last_state(n, back, o):
@@ -435,14 +479,14 @@ def rank_program(g, core, T, topo):
     o, back, own = first_orders()
     first_state()
     for n in (1, 2, 3):
-        delta, base = apart(n, own)
+        apart(n, own)
         low = cycles(n)
         if n > 1:
             new_state(n - 1, back)
         unpack(n - 1, o)
-        dm, dd, own = new("ls"), new("ls"), pair()
+        dm, dd, own = new("ls"), new("ls"), ["ot%d0" % n, "ot%d1" % n]
         gather("dm", dm, "so", low)
-        o = mix(["ds", "t", "nf", "nu"], dm, delta[0], base[0], own[0])
+        o = mix(["ds", "nf", "nu"], dm, n, 0)
         phase[0] = n + 1
         if n < len(STEP):
             hand_on(n + 1, o=o)
@@ -452,7 +496,7 @@ def rank_program(g, core, T, topo):
             send("send_n", STEP[n - 1], [(T[far][:], ap(o))], [o], "a_n%d" % n, far)
         sums(n, far)
         gather("dd", dd, dm, back)
-        back = mix(["es", "et", "ef", "eu"], dd, delta[1], base[1], own[1])
+        back = mix(["es", "ef", "eu"], dd, n, 1)
         if n < len(STEP):
             gather("bk", "bk%d" % n, "iots", back)
             hand_on(n + 1, own=own)
@@ -460,7 +504,6 @@ def rank_program(g, core, T, topo):
         means(n, far, parts)
     last_state(len(STEP), back, o)
 
-    order = {q: ["%d:%s" % (n + (name[0] == "+") - (name[0] == "-"), name.lstrip("+-")) for n in LIKE for name in PLAN[LIKE[n]][q].split()] for q in queues}
-    order = {q: [name for name in order[q] if name in calls] for q in queues}
+    order = {q: ["%d:%s" % (n - name.count("-") + name.count("+"), name.lstrip("+-")) for n in PLAN for name in PLAN[n][q].split()] for q in queues}
     assert sorted(sum(order.values(), [])) == sorted(calls), set(calls) ^ set(sum(order.values(), []))
     issue(order)

from concourse.mybir import dt, AluOpType, ActivationFunctionType

C = 448
K = C // 16
STEP = [1, 2, 3]
MID = C // 2
UP = 512.0
LAST = [(0, 224), (224, C)]
ENDS = [(0, 320), (320, C)]

FORM = {}
HALF = ()
RADIX = {n: [3, 3, 3, 3, 3] if n in HALF else [2, 3, 3, 3, 3, 3] for n in (1, 2, 3)}
APART = {2: "h2 h3", 3: "h2 h3", 4: "h20 h30 h21 h31"}
SHARED = {1: (), 2: (), 3: (2, 3)}
FAR = (3,)
SCAN = (2, 3)
SPLIT = {1: "dm k p0", 2: "dm x0 x1 x2 x3", 3: "dm x0 x1 x2 x3", 4: ""}

PLAN = {
    1: {"v": "ones md iots bia0 e1 dz0 e0 uo bia1 ou d0 hbl of dz1 inv qx k< ia ka qu kb m p0> qur a1 ib b1 e2q l1 e0q l1' a2 ic b2 e3q l2 l2' a3 w3 b3 base delta l3 e1q l3' a4 w4 b4 l4 l4' a5 w5 b5 l5 l5' la lb dm> ds mid nf",
        "s": "d1 d2 d3 d4 d5 k> p0< w1 p1 p1' w2 p2 p2' sur p3 p3' f1 p4 p4' sc f2 f3 so f0 dm<",
        "g": "mdi uoi send_o eye send_b",
        "t": "ms mf0 mf3 mf1 mf2",
        "y": "od x u fd1 wc ws fd2 fd0 fd3"},
    2: {"v": "es -nu ef eu u1 u0 u3 ka m kb u2 z3 a1 m1 b1 qz l1 base l1' a2 w2 b2 r0 l2 x0> l2' a3 x0< b3 x1> x1< l3 x3< l3' a4 x3> b4 x2< x2> l4 qx l4' a5 w5 b5 l5 delta l5' la lb dm< ds nf",
        "s": "dd bk k z0 z1 p0 z2 p1 p1' p2 r3 p2' r1 h3 p3 r2 p3' h2 w4 p4 p4' sc f1 f0 so f2 dm>",
        "g": "send_o send_b send_z w3",
        "t": "mr0 mr3 mr2 mr1 ms mf1 mf2 mf0 mf3",
        "y": "fd0 fd1 fd2 -v fd3"},
    3: {"v": "es -nu ef eu u2 u0 u1 ka m kb u3 z1 a1 m1 b1 qz l1 l1' a2 w2 b2 delta l2 r0 l2' x0> a3 x0< b3 x2< x2> l3 x1< l3' a4 x1> b4 x3> x3< l4 qx l4' a5 w5 b5 l5 l5' la lb +qv dm> base ds nf nu f2",
        "s": "dd -f3 bk k z0 z2 p0 z3 p1 p1' p2 r2 p2' h2 r1 p3 r3 p3' h3 w4 p4 p4' sc fe0 so f1 f0 dm< fe1 f3",
        "g": "send_o send_b send_z w3 send_x",
        "t": "mr2 mr0 mr3 mr1 ms mf0 mg1 mf2 mg0 mg3 mg2 mf1 mf3",
        "y": "fd1 fd0"},
    4: {"v": "dd u0 u3 u1 u2 z10 es qz0 z21 ef qz1 r30 r10 r11 eu r21 x11 x00 x01 x10 x30 x31 x21 x20 qx1 qx0 y1 y0",
        "s": "osp g3 g2 z00 z30 z31 z20 z01 z11 r20 r00 r01 r31 h20 h30 h31 h21 oc1 oc0 o0 yo0",
        "g": "send_n",
        "t": "mr20 mr30 mr00 mr10 mr11 mr01 mr21 mr31 my1 my0",
        "y": "fo o2 o3 yo1 o1"},
}

SCRATCH = {
    "md": ("sbuf", [128, 16], "int32"), "ee": ("sbuf", [128, 32], "float32"), "d0": ("sbuf", [128, C], "bfloat16"),
    "iots": ("sbuf", [128, C], "bfloat16"), "ones": ("sbuf", [128, 516], "bfloat16"),
    "eye": ("sbuf", [128, 516], "bfloat16"), "bia": ("sbuf", [128, 4], "float32"),
    "uoi": ("sbuf", [128, 8], "int32"), "uo": ("sbuf", [128, 8], "uint16"),
    "odl": ("sbuf", [128, K], "int32"), "ut": ("sbuf", [128, 512], "bfloat16"),
    "vt": ("sbuf", [128, 512], "bfloat16"), "xt0": ("sbuf", [128, 4 * C], "bfloat16"),
    "qu": ("sbuf", [128, 128], "float8_e4m3fn_x4"), "su": ("sbuf", [128, 128], "uint8"),
    "qur": ("sbuf", [128, 128], "float8_e4m3fn_x4"), "sur": ("sbuf", [128, 128], "uint8"),
    "qv": ("sbuf", [128, 128], "float8_e4m3fn_x4"), "sv": ("sbuf", [128, 128], "uint8"),
    "qe": ("sbuf", [128, 512], "float8_e4m3fn_x4"), "se": ("sbuf", [128, 512], "uint8"),
    "wq": ("sbuf", [128, 512], "float8_e4m3fn_x4"), "wp": ("sbuf", [128, 512], "uint8"),
    "sc": ("sbuf", [128, C], "bfloat16"), "so": ("sbuf", [128, C], "bfloat16"),
    "zt": ("sbuf", [128, 4 * C], "bfloat16"), "xt": ("sbuf", [128, 4 * C], "bfloat16"),
    "ysb": ("sbuf", [128, C], "float32"), "osp": ("sbuf", [128, C], "float32"),
    "ls": ("sbuf", [128, C * 90], "bfloat16"), "hs": ("sbuf", [128, C * 30], "float16"), "tu": ("sbuf", [128, K * 48], "uint16"),
    "wd": ("sbuf", [128, 2 * C * 8], "bfloat16"),
    "ot0": ("sbuf", [128, 2 * K], "float16"), "dz": ("sbuf", [128, 6 * K], "float16"), "hb": ("sbuf", [128, 6 * C + 45], "float16"),
    "pa": ("psum", [128, 2048], "float32"), "pb": ("psum", [128, 2048], "float32"),
}
for _b in range(4):
    SCRATCH["f%d" % _b] = ("sbuf", [128, C], "bfloat16")
    SCRATCH["fd%d" % _b] = ("sbuf", [128, C], "bfloat16")
    SCRATCH["fe%d" % _b] = ("sbuf", [128, C], "bfloat16")
    SCRATCH["u%d" % _b] = ("sbuf", [128, C], "float32")
    SCRATCH["gg%d" % _b] = ("sbuf", [128, C], "bfloat16")
    SCRATCH["r%d" % _b] = ("sbuf", [128, C], "float32")
    SCRATCH["hh%d" % _b] = ("sbuf", [128, C], "float32")
    SCRATCH["xq%d" % _b] = ("sbuf", [128, C], "float8_e4m3fn_x4")
    SCRATCH["xs%d" % _b] = ("sbuf", [128, C], "uint8")
for _n in (1, 2, 3):
    SCRATCH["bk%d" % (_n - 1)] = ("sbuf", [128, C], "bfloat16")
    SCRATCH["ol%d" % _n] = ("sbuf", [128, K], "uint16")
    SCRATCH["bl%d" % _n] = ("sbuf", [128, 2 * K if _n == 1 else 6 * K], "float16")
    SCRATCH["ot%d" % _n] = ("sbuf", [128, 6 * K], "float16")
    SCRATCH["on%d" % _n] = ("sbuf", [128, K], "uint16")
    for _k in ("lt", "ll", "lm"):
        SCRATCH["%s%d" % (_k, _n)] = ("sbuf", [128, K], "bfloat16")
    SCRATCH["zq%d" % _n] = ("sbuf", [128, C], "float8_e4m3fn_x4")
    SCRATCH["zs%d" % _n] = ("sbuf", [128, C], "uint8")
    SCRATCH["zl%d" % _n] = ("sbuf", [128, C], "float8_e4m3fn_x4")
    SCRATCH["zp%d" % _n] = ("sbuf", [128, C], "uint8")

SEMAPHORES = ["cv", "cs", "ct", "cg", "sent"] + ["a_z10", "a_z11", "a_z20", "a_z21", "a_z30"] + ["a_%s%d" % (k, n) for k in "obnl" for n in (1, 2, 3)] \
    + ["l_" + n for n in ("od", "x", "u", "v", "wc", "ws", "y0", "y1", "y2", "fo", "oc0", "oc1", "oc2", "osc0", "osc1", "osc2", "osc3", "f0", "f1", "f2", "f3")]

ADD, MUL, SUB, MIN, MAX = AluOpType.add, AluOpType.mult, AluOpType.subtract, AluOpType.min, AluOpType.max
COPY = ActivationFunctionType.Copy


def rank_program(g, core, T, topo):
    rank = T.rank_of(core)
    if rank is None:
        return
    V, S = g.vector, g.scalar
    queues = {"v": V, "s": S, "t": g.tensor, "g": g, "y": g.sync}

    calls, wrote, read = {}, {}, {}
    phase = [1]

    def record(name, kind, reads, writes, what):
        name = "%d:%s" % (phase[0], name)
        after = set()
        for k in reads:
            after.update(wrote.get(k, []))
        for k in writes:
            after.update(wrote.get(k, []))
            after.update(read.get(k, []))
            for tag in "<>":
                after.update(read.pop(k + tag, []) + wrote.pop(k + tag, []))
        for k in reads:
            read.setdefault(k, []).append(name)
        for k in writes:
            wrote[k], read[k] = [name], []
        calls[name] = {"kind": kind, "after": after, "what": what}

    def op(name, reads, writes, **forms):
        record(name, "op", reads, writes, forms)

    def load(name, sem, reads, writes, pairs):
        record(name, "load", reads, writes, (sem, pairs))

    def send(name, step, pairs, key, sem, lands, few=None):
        record(name, "send", key, [lands], (step, pairs, sem, few))

    def issue(order):
        count, totals, token, snap = {q: 0 for q in queues}, {}, {}, {}
        seen = {q: {} for q in queues}
        heads = {q: 0 for q in queues}

        def wait(q, sem, val):
            if seen[q].get(sem, 0) < val:
                queues[q].wait_ge(T.sem[sem], val)
                seen[q][sem] = val
                for a, b in snap.get((sem, val), {}).items():
                    seen[q][a] = max(seen[q].get(a, 0), b)

        def emit(q, name):
            c = calls[name]
            need = {}
            for a in c["after"]:
                sem, val = token[a]
                need[sem] = max(need.get(sem, 0), val)
            for sem in sorted(need):
                wait(q, sem, need[sem])
            if c["kind"] == "op":
                count[q] += 1
                sem = "c" + q
                c["what"][q]().then_inc(T.sem[sem], 1)
                totals[sem] = count[q]
            elif c["kind"] == "load":
                sem, pairs = c["what"]
                for out, in_ in pairs:
                    queues[q].dma_start(out, in_).then_inc(T.sem[sem], 16)
                    totals[sem] = totals.get(sem, 0) + 16
            else:
                step, pairs, sem, few = c["what"]
                dst = T.cores[rank ^ step]
                e = topo.engines(core, dst)
                if few is not None:
                    e = e[few::2]
                rid, pid, _ = topo.addr(dst)
                for out, in_ in pairs:
                    g.remote_dma(out, in_, T.sem[sem], T.sem["sent"], pid, rid, sum(1 << i for i in e))
                    totals["sent"] = totals.get("sent", 0) + len(e)
                    totals[sem] = totals.get(sem, 0) + len(e)
            token[name] = (sem, totals[sem])
            snap[token[name]] = dict(seen[q]) if c["kind"] != "send" else {}

        left = len(calls)
        while left > 0:
            before = left
            for q in queues:
                while heads[q] < len(order[q]) and all(a in token for a in calls[order[q][heads[q]]]["after"]):
                    emit(q, order[q][heads[q]])
                    heads[q] += 1
                    left -= 1
            assert left < before, [order[q][heads[q]] for q in queues if heads[q] < len(order[q])]
        for sem in sorted(totals):
            wait("g", sem, totals[sem])

    used = {"tu": 0, "ls": 0, "hs": 0, "wd": 5}
    width = {"tu": K, "ls": C, "hs": C, "wd": 2 * C}

    def new(kind):
        used[kind] += 1
        return "%s.%d" % (kind, used[kind] - 1)

    def ap(key, a=0, b=None, step=1):
        if "." in key:
            kind, i = key.split(".")
            w = width[kind]
            if kind == "wd":
                return T.wd[:, w * int(i) + 2 * a:w * int(i) + (w if b is None else 2 * b):2 * step or 1]
            return T[kind][:, w * int(i) + a:w * int(i) + (w if b is None else b):step]
        return T[key][:, a:(C if b is None else b):step]

    def by(key, table, p=0, e=C):
        return ap(key, step=0 if key[:2] == "wd" else 1).indirect(ap(table, p // 16, e // 16))

    def move(name, reads, writes, out, in_, scale=None):
        op(name, reads, writes, s=lambda: S.activation(out, in_, COPY) if scale is None else S.activation(out, in_, COPY, scale=scale),
           v=lambda: V.tensor_copy(out, in_) if scale is None else V.tensor_scalar(out, in_, scale, None, MUL))

    HALVES = (("<", 0, MID), (">", MID, C))

    def part(key, tag):
        return key + tag if key + tag in wrote else key

    def gather(name, out, key, table):
        if name not in SPLIT[phase[0]].split():
            return move(name, [key, table], [out], ap(out), by(key, table))
        for tag, p, e in HALVES:
            read[out + tag] = read.get(out + tag, []) + read.get(out, []) + wrote.get(out, [])
            move(name + tag, [key, part(table, tag)], [out + tag], ap(out, p, e), by(key, table, p, e))
        wrote[out], read[out] = wrote[out + "<"] + wrote[out + ">"], []

    def conv(a, b, key, double=True):
        h, t = new("hs"), new("tu")
        if double and key[:2] == "wd":
            op(a, [key, "d0"], [h], v=lambda: V.tensor_tensor_scan(ap(h), T.d0[:, 0:C], ap(key), 0.0, ADD, MAX))
            op(b, [h, "bia"], [t], v=lambda: V.tensor_scalar(ap(t), ap(h, 15, C, 16), T.bia[:, 1:2], 2.0, ADD, MUL))
            return t
        for tag, p, e in HALVES if a in SPLIT[phase[0]].split() else (("", 0, C),):
            op(a + tag, [part(key, tag), "d0"], [h + tag], v=lambda p=p, e=e: V.tensor_tensor_scan(ap(h, p, e), T.d0[:, p:e], ap(key, p, e), 0.0, ADD, MAX))
            op(b + tag, [h + tag, "bia"], [t + tag], v=lambda p=p, e=e: V.tensor_scalar(ap(t, p // 16, e // 16), ap(h, p + 15, e, 16), T.bia[:, 1:2], None, ADD))
        if tag:
            wrote[t] = wrote[t + "<"] + wrote[t + ">"]
        return t

    def gathered(n, b):
        tags = ["h%d" % b] if n < len(STEP) else ["h%d%d" % (b, h) for h in range(len(ENDS))]
        return [tag in APART[n + 1].split() for tag in tags]

    load("od", "l_od", [], ["odl"], [(T.odl[:], T.od[:])])
    op("mdi", [], ["md"], g=lambda: g.iota(T.md[:], [[1, 16]], 128, -1))
    op("uoi", [], ["uoi"], g=lambda: g.iota(T.uoi[:], [[16, 8]], 0, 0))
    op("ones", [], ["ones"], v=lambda: V.memset(T.ones[:], 1.0))
    op("iots", ["ones"], ["iots"], v=lambda: V.tensor_tensor_scan(T.iots[:], T.ones[:, 0:C], T.ones[:, 0:C], -MID - 1.0, ADD, MUL))
    op("eye", ["ones"], ["eye"], g=lambda: g.affine_select(T.eye[:], T.ones[:], [[-1, 516]], AluOpType.is_equal, 0.0, 3, 4))
    op("md", ["md"], ["md"], v=lambda: V.tensor_scalar(T.md[:], T.md[:], 15, None, AluOpType.bitwise_and))
    op("e0", ["md"], ["e0"], v=lambda: V.tensor_scalar(T.ee[:, 0:16], T.md[:], 0.0, -2 * UP, AluOpType.is_equal, MUL))
    op("e1", ["md"], ["e1"], v=lambda: V.tensor_scalar(T.ee[:, 16:32], T.md[:], 1.0, UP, AluOpType.is_equal, MUL))
    op("d0", ["e0", "e1"], ["d0"], v=lambda: V.tensor_tensor(T.d0[:, 0:16], T.ee[:, 0:16], T.ee[:, 16:32], ADD))
    for i in range(5):
        w = 16 << i
        move("d%d" % (i + 1), ["d0"], ["d0"], T.d0[:, w:min(2 * w, C)], T.d0[:, 0:min(w, C - w)])
    op("bia0", ["md"], ["bia0"], v=lambda: V.tensor_scalar(T.bia[:, 0:1], T.md[:, 15:16], 0.0, -UP, AluOpType.not_equal, MUL))
    op("bia1", ["bia0"], ["bia"], v=lambda: V.tensor_scalar(T.bia[:, 1:2], T.bia[:, 0:1], float(MID), None, ADD))
    op("mid", [], ["mid"], v=lambda: V.memset(T.bia[:, 2:3], float(MID)))
    op("hbl", ["ones", "bia0"], ["hbl"], v=lambda: V.tensor_scalar(T.hb[:, 61::48], T.ones[:, 0:2 * K], T.bia[:, 0:1], None, MUL))
    op("dz0", ["ones"], ["dz0"], v=lambda: V.tensor_scalar(T.dz[:, 0::3], T.ones[:, 0:2 * K], 0.0, None, MUL))
    op("dz1", ["ones", "dz0"], ["dz01"], v=lambda: V.tensor_copy(T.dz[:, 1::3], T.ones[:, 0:2 * K]))
    if FORM:
        for i in range(5):
            op("wd%d" % i, [], ["wd.%d" % i], v=lambda i=i: V.memset(T.wd[:, 2 * C * i + 1:2 * C * (i + 1):2], -UP))
    op("uo", ["uoi"], ["uo"], v=lambda: V.tensor_copy(T.uo[:], T.uoi[:]))
    for b in range(4):
        op("e%dq" % b, ["eye"], ["qe%d" % b], v=lambda b=b: V.quantize_mx(T.qe[:, 128 * b:128 * b + 128], T.se[:, 128 * b:128 * b + 128], T.eye[:, 3 - b:515 - b]))

    def first_state():
        for name, key, out, in_ in (("u", "ut", T.ut[:], T.u[:]), ("x", "xt0", T.xt0[:], T.x[:]), ("v", "vt", T.vt[:], T.v[:]),
                                    ("wc", "wq", T.wq[:, 0:512].bitcast(dt.uint8), T.wc[:, 0:2048]), ("ws", "wp", T.wp[:, 0:512], T.ws[:, 0:512])):
            load(name, "l_" + name, [], [key], [(out, in_)])
        op("qu", ["ut"], ["qu"], v=lambda: V.quantize_mx(T.qu[:, 0:128], T.su[:, 0:128], T.ut[:, 0:512]))
        op("qur", ["qu", "uo"], ["qur"], v=lambda: V.tensor_copy(T.qur[:, 0:128].bitcast(dt.uint32), T.qu[:, 0:128].bitcast(dt.uint32).indirect(T.uo[:, 0:8])))
        move("sur", ["qu", "uo"], ["sur"], T.sur[:, 0:128], T.su[:, 0:128].indirect(T.uo[:, 0:8]))
        op("qx", ["xt0"], ["xq0"], v=lambda: V.quantize_mx(T.xq0[:, 0:C], T.xs0[:, 0:C], T.xt0[:, 0:4 * C]))

    def hand_on(n, o=None, own=None):
        if o is not None:
            send("send_o", STEP[n - 1], [(T["ol%d" % n][:], ap(o))], [o], "a_o%d" % n, "ol%d" % n, few=0 if n == 1 else None)
        else:
            send("send_b", STEP[n - 1], [(T["bl%d" % n][:], T["ot%d" % (n - 1)][:])], own, "a_b%d" % n, "bl%d" % n, few=1 if n == 1 else None)

    def first_orders():
        o, own = new("tu"), ["ot00", "ot01"]
        op("ou", ["odl"], [o], v=lambda: V.tensor_copy(ap(o), T.odl[:]))
        hand_on(1, o=o)
        op("of", ["odl"], [own[0]], v=lambda: V.tensor_copy(T.ot0[:, 0:K], T.odl[:]))
        op("inv", ["iots", o], ["bk0"], v=lambda: V.tensor_copy(by("bk0", o), T.iots[:]))
        back = conv("ia", "ib", "bk0")
        op("ic", [back], [own[1]], v=lambda: V.tensor_copy(T.ot0[:, K:2 * K], ap(back)))
        hand_on(1, own=own)
        return o, back, own

    def apart(n, own):
        mine, far, step = "ot%d" % (n - 1), "bl%d" % n, 1 if n == 1 else 3
        op("delta", [far] + own, ["dz"], v=lambda: V.tensor_tensor(T.dz[:, 2::3], T[far][:, step - 1::step], T[mine][:, step - 1::step], SUB))
        op("base", own, ["hbo"], v=lambda: V.tensor_copy(T.hb[:, 77::48], T[mine][:, step - 1::step]))

    def wide(n):
        m, g1, g2, power, other = ["wd.%d" % i for i in range(5)]

        def lower(name, a, b):
            out = new("wd")
            op(name, [a, b], [out], v=lambda: V.tensor_tensor_scan(ap(out, step=0), ap(a, step=0), ap(b, step=0), -UP, MAX, MIN))
            return out

        gather("k", power, "bk%d" % (n - 1), "ol%d" % n)
        a = conv("ka", "kb", power)
        op("m", ["iots", power], [m], v=lambda k=power: V.tensor_tensor_scan(ap(m), T.iots[:], ap(k), -UP, MAX, MIN))
        gather("p0", other, power, a)
        low, power, other = m, other, power
        for j, form in enumerate(FORM[n], 1):
            a = conv("a%d" % j, "b%d" % j, power)
            gather("n%d" % j, g1, low, a)
            if form == "p":
                low = lower("s%d" % j, g1, low)
                gather("n%d'" % j, g2, g1, a)
                low = lower("s%d'" % j, g2, low)
            else:
                op("l%d'" % j, [g1, low, a], [g2], v=lambda low=low, a=a: V.tensor_tensor(ap(g2), by(g1, a), ap(low), MIN))
                low = lower("s%d'" % j, g2, g1)
            if j < len(FORM[n]):
                gather("p%d" % j, other, power, a)
                gather("p%d'" % j, power, other, a)
        return conv("la", "lb", low, False)

    def cycles(n):
        if n in FORM:
            return wide(n)
        k, m = new("ls"), new("ls")
        gather("k", k, "bk%d" % (n - 1), "ol%d" % n)
        a = conv("ka", "kb", k)

        def least(name, out):
            op(name, ["iots", k], [out], v=lambda: V.tensor_tensor_scan(ap(out), T.iots[:], ap(k), -UP, MAX, MIN))

        least("m", m)
        low, power = m, k
        radix = RADIX[n]
        if radix[0] == 3:
            twin, low = new("ls"), new("ls")
            least("m0", twin)
            op("l0", [twin, m, a], [low], v=lambda low=low, a=a: V.tensor_tensor(ap(low), by(twin, a), ap(m), MIN))
        for j, r in enumerate(radix):
            if j > 0:
                a = conv("a%d" % j, "b%d" % j, power)
                acc = new("ls")
                if j == 1 and n in SCAN and radix[0] == 2:
                    least("m1", acc)
                else:
                    op("w%d" % j, [low], [acc], v=lambda acc=acc, low=low: V.tensor_copy(ap(acc), ap(low)),
                       s=lambda acc=acc, low=low: S.activation(ap(acc), ap(low), COPY),
                       g=lambda acc=acc, low=low: g.affine_select(ap(acc), ap(low), [[0, C]], AluOpType.is_equal, 0.0, 0, 0))
                for e in range(r - 1):
                    out = new("ls")
                    op("l%d%s" % (j, "'" * e), [acc, low, a], [out], v=lambda out=out, acc=acc, low=low, a=a: V.tensor_tensor(ap(out), by(acc, a), ap(low), MIN))
                    acc = out
                low = acc
            if j < len(radix) - 1:
                for e in range(r - 1):
                    out = new("ls")
                    gather("p%d%s" % (j, "'" * e), out, power, a)
                    power = out
        if n not in HALF:
            return conv("la", "lb", low)
        h, table, mine, far, both = new("hs"), new("tu"), "lt%d" % n, "ll%d" % n, "lm%d" % n
        op("la", [low, "d0"], [h], v=lambda: V.tensor_tensor_scan(ap(h), T.d0[:, 0:C], ap(low), 0.0, ADD, MAX))
        op("lb", [h, "bia0"], [mine], v=lambda: V.tensor_scalar(T[mine][:], ap(h, 15, C, 16), T.bia[:, 0:1], None, ADD))
        send("send_l", STEP[n - 1], [(T[far][:], T[mine][:])], [mine], "a_l%d" % n, far)
        op("lc", [mine, far], [both], v=lambda: V.tensor_tensor(T[both][:], T[mine][:], T[far][:], MIN))
        op("ld", [both], [table], v=lambda: V.tensor_scalar(ap(table), T[both][:], float(MID), None, ADD))
        return table

    def unpack(n, o):
        xq, xs = "xq%d" % n, "xs%d" % n
        op("ms", ["qur", "sur", xq], ["pb0"], t=lambda: g.tensor.matmul_mx(T.pb[:, 0:C], T.qur[:, 0:128], T.sur[:, 0:128], T[xq][:, 0:C], T[xs][:, 0:C], True, True))
        op("sc", ["pb0"], ["sc"], s=lambda: S.activation(T.sc[:], T.pb[:, 0:C], ActivationFunctionType.Sign),
           v=lambda: V.tensor_scalar(T.sc[:], T.pb[:, 0:C], 0.0, None, AluOpType.is_gt))
        op("so", ["sc", o], ["so"], s=lambda: S.activation(T.so[:], by("sc", o), ActivationFunctionType.Relu),
           v=lambda: V.tensor_scalar(T.so[:], by("sc", o), 0.0, None, MAX))

        def planes(name, p, q, s):
            for b in range(4):
                op("%s%d" % (name, b), ["qe%d" % b, q], ["%s%d" % (p, b)], t=lambda b=b: g.tensor.matmul_mx(T[p][:, 512 * b:512 * b + C], T.qe[:, 128 * b:128 * b + 128], T.se[:, 128 * b:128 * b + 128], T[q][:, 0:C], T[s][:, 0:C], True, True))

        planes("mf", "pa", xq, xs)
        p = "pa"
        if n + 1 in FAR:
            p, zl, zp = "pb", "zl%d" % (n + 1), "zp%d" % (n + 1)
            send("send_x", STEP[n], [(T[zl][:].bitcast(dt.uint8), T[xq][:].bitcast(dt.uint8)), (T[zp][:], T[xs][:])], [xq], "a_z%d0" % (n + 1), zl)
            planes("mg", p, zl, zp)
            for b in range(4):
                if not all(gathered(n + 1, b)):
                    move("fe%d" % b, ["pa%d" % b], ["fe%d" % b], T["fe%d" % b][:], T.pa[:, 512 * b:512 * b + C])
        for b in range(4):
            move("f%d" % b, ["%s%d" % (p, b)], ["f%d" % b], T["f%d" % b][:], T[p][:, 512 * b:512 * b + C])
            if b not in SHARED[n + 1]:
                load("fd%d" % b, "l_f%d" % b, ["f%d" % b], ["fd%d" % b], [(T["fd%d" % b][:], T["f%d" % b][:])])

    def mix(names, dm, n, i):
        table, ot, h, out = new("tu"), T["ot%d" % n], "hb%d" % i, "ot%d%d" % (n, i)
        op(names[0], [dm, "d0"], [h], v=lambda: V.tensor_tensor_scan(T.hb[:, 3 * C * i:3 * C * (i + 1):3], T.d0[:, 0:C], ap(dm), 0.0, ADD, MAX))
        op(names[1], [h, "hbl", "hbo", "dz", "dz01"], [out], v=lambda: V.tensor_tensor_scan(
            ot[:, 3 * K * i:3 * K * (i + 1)], T.dz[:, 3 * K * i:3 * K * (i + 1)], T.hb[:, 3 * C * i + 45:3 * C * (i + 1) + 45:16], 0.0, MUL, ADD))
        op(names[2], [out], [table], v=lambda: V.tensor_copy(ap(table), ot[:, 3 * K * i + 2:3 * K * (i + 1):3]))
        return table

    def sums(n, o):
        p = "pb" if n in FAR else "pa"
        for b in range(4):
            f, u = "f%d" % b, "u%d" % b
            if b in SHARED[n]:
                move("g%d" % b, [f, o], ["gg%d" % b], T["gg%d" % b][:], by(f, o))
                op(u, ["gg%d" % b, "%s%d" % (p, b)], [u], v=lambda b=b, u=u: V.tensor_tensor(T[u][:], T["gg%d" % b][:], T[p][:, 512 * b:512 * b + C], ADD))
            else:
                op(u, [f, "fd%d" % b, o], [u], v=lambda b=b, f=f, u=u: V.tensor_tensor(T[u][:], by(f, o), T["fd%d" % b][:], ADD))

    def means(n, o, parts):
        zq, zs, zl, zp = "zq%d" % n, "zs%d" % n, "zl%d" % n, "zp%d" % n
        for h, (p, e) in enumerate(parts):
            tag = str(h) if len(parts) > 1 else ""
            for b in range(4):
                move("z%d%s" % (b, tag), ["u%d" % b, o], ["zt%d%d" % (b, h)], T.zt[:, 4 * p + b:4 * e:4], by("u%d" % b, o, p, e), 0.5)
            key = "%s%d" % (zq, h)
            op("qz" + tag, ["zt%d%d" % (b, h) for b in range(4)], [key], v=lambda p=p, e=e: V.quantize_mx(T[zq][:, p:e], T[zs][:, p:e], T.zt[:, 4 * p:4 * e]))
            if n not in FAR:
                send("send_z" + tag, STEP[n - 1], [(T[zl][:, p:e].bitcast(dt.uint8), T[zq][:, p:e].bitcast(dt.uint8)), (T[zp][:, p:e], T[zs][:, p:e])], [key], "a_z%d%d" % (n, h), "%s%d" % (zl, h))

    def layer(n, b, h, p, e, bank, name):
        zl, zp = ("zq%d" % n, "zs%d" % n) if n in FAR else ("zl%d" % n, "zp%d" % n)
        at = T[bank[:2]][:, 512 * int(bank[2]):512 * int(bank[2]) + e - p]
        op("m" + name, ["wq", "wp", "%s%d" % (zl, h)], [bank], t=lambda: g.tensor.matmul_mx(at, T.wq[:, 128 * b:128 * b + 128], T.wp[:, 128 * b:128 * b + 128], T[zl][:, p:e], T[zp][:, p:e], True, True))
        move(name, [bank], ["r%d%d" % (b, h)], T["r%d" % b][:, p:e], at, 0.03125)

    def home(n, b, h, p, e, runs, back, tag):
        r, out, rs = "r%d" % b, T.xt[:, 4 * p + b:4 * e:4], ["r%d%d" % (b, i) for i in range(runs)]
        if gathered(n, b)[h]:
            move("h" + tag, rs + [back], ["hh%d%d" % (b, h)], T["hh%d" % b][:, p:e], by(r, back, p, e))
            op("x" + tag, ["hh%d%d" % (b, h), "pa%d" % b], ["xt%d%d" % (b, h)], v=lambda: V.tensor_tensor(out, T["hh%d" % b][:, p:e], T.pa[:, 512 * b + p:512 * b + e], ADD))
        else:
            f = "%s%d" % ("fe" if n in FAR else "f", b)
            op("x" + tag, rs + [f, back], ["xt%d%d" % (b, h)], v=lambda: V.tensor_tensor(out, by(r, back, p, e), T[f][:, p:e], ADD))

    def new_state(n, back):
        for b in range(4):
            layer(n, b, 0, 0, C, "pb%d" % b, "r%d" % b)
            if "x%d" % b not in SPLIT[n + 1].split():
                home(n, b, 0, 0, C, 1, back, str(b))
                continue
            r, hh, f, apart = "r%d" % b, "hh%d" % b, "f%d" % b, gathered(n, b)[0]
            if apart:
                move("h%d" % b, [r + "0", back], [hh + "0"], T[hh][:], by(r, back))
            for tag, p, e in HALVES:
                out, key = T.xt[:, 4 * p + b:4 * e:4], "xt%d0" % b
                read[key + tag] = read.get(key + tag, []) + read.get(key, []) + wrote.get(key, [])
                if apart:
                    op("x%d%s" % (b, tag), [hh + "0", "pa%d" % b], [key + tag], v=lambda out=out, hh=hh, b=b, p=p, e=e: V.tensor_tensor(out, T[hh][:, p:e], T.pa[:, 512 * b + p:512 * b + e], ADD))
                else:
                    op("x%d%s" % (b, tag), [r + "0", f, back], [key + tag], v=lambda out=out, r=r, f=f, p=p, e=e: V.tensor_tensor(out, by(r, back, p, e), T[f][:, p:e], ADD))
            wrote[key], read[key] = wrote[key + "<"] + wrote[key + ">"], []
        op("qx", ["xt%d0" % b for b in range(4)], ["xq%d" % n], v=lambda: V.quantize_mx(T["xq%d" % n][:, 0:C], T["xs%d" % n][:, 0:C], T.xt[:, 0:4 * C]))

    def last_state(n, back, o):
        op("osp", ["iots", "mid", o], ["osp"], s=lambda: S.activation(T.osp[:], by("iots", o), ActivationFunctionType.Identity, bias=T.bia[:, 2:3]),
           v=lambda: V.tensor_scalar(T.osp[:], by("iots", o), float(MID), None, ADD))
        load("fo", "l_fo", ["osp"], [], [(T.fo[:, 0:C], T.osp[0:128:16, 0:C])])
        op("qv", ["vt"], ["qv"], v=lambda: V.quantize_mx(T.qv[:, 0:128], T.sv[:, 0:128], T.vt[:, 0:512]))
        for h, (p, e) in enumerate(LAST):
            for b in range(4):
                layer(n, b, h, p, e, "%s%d" % ("pb" if h % 2 == 0 or any(gathered(n, b)) else "pa", b), "r%d%d" % (b, h))
        for h, (p, e) in enumerate(ENDS):
            for b in range(4):
                home(n, b, h, p, e, len(LAST), back, "%d%d" % (b, h))
            key, bank = "xq3%d" % h, "pb%d" % (h % 2)
            at = T.pb[:, 512 * (h % 2):512 * (h % 2) + e - p]
            op("qx%d" % h, ["xt%d%d" % (b, h) for b in range(4)], [key], v=lambda p=p, e=e: V.quantize_mx(T.xq3[:, p:e], T.xs3[:, p:e], T.xt[:, 4 * p:4 * e]))
            op("my%d" % h, ["qv", key], [bank], t=lambda at=at, p=p, e=e: g.tensor.matmul_mx(at, T.qv[:, 0:128], T.sv[:, 0:128], T.xq3[:, p:e], T.xs3[:, p:e], True, True))
            load("oc%d" % h, "l_oc%d" % h, [key], [], [(T.oc[:, 4 * p:4 * e], T.xq3[:, p:e].bitcast(dt.uint8))])
            move("y%d" % h, [bank], ["ysb%d" % h], T.ysb[:, p:e], at)
            load("yo%d" % h, "l_y%d" % h, ["ysb%d" % h], [], [(T.y[:, p:e], T.ysb[:, p:e])])
        for k in range(4):
            load("o%d" % k, "l_osc%d" % k, ["xq3%d" % h for h in range(len(ENDS))], [], [(T.osc[4 * k:4 * k + 4, 0:C], T.xs3[32 * k:32 * k + 4, 0:C])])

    o, back, own = first_orders()
    first_state()
    for n in (1, 2, 3):
        apart(n, own)
        low = cycles(n)
        if n > 1:
            new_state(n - 1, back)
        unpack(n - 1, o)
        dm, dd, own = new("ls"), new("ls"), ["ot%d0" % n, "ot%d1" % n]
        gather("dm", dm, "so", low)
        o = mix(["ds", "nf", "nu"], dm, n, 0)
        phase[0] = n + 1
        if n < len(STEP):
            hand_on(n + 1, o=o)
        far = o
        if n in FAR:
            far = "on%d" % n
            send("send_n", STEP[n - 1], [(T[far][:], ap(o))], [o], "a_n%d" % n, far)
        sums(n, far)
        gather("dd", dd, dm, back)
        back = mix(["es", "ef", "eu"], dd, n, 1)
        if n < len(STEP):
            gather("bk", "bk%d" % n, "iots", back)
            hand_on(n + 1, own=own)
        parts = [(0, C)] if n < len(STEP) else LAST
        means(n, far, parts)
    last_state(len(STEP), back, o)

    order = {q: ["%d:%s" % (n - name.count("-") + name.count("+"), name.lstrip("+-")) for n in PLAN for name in PLAN[n][q].split()] for q in queues}
    assert sorted(sum(order.values(), [])) == sorted(calls), set(calls) ^ set(sum(order.values(), []))
    issue(order)
